import numpy as np, ml_dtypes
CORES = [35,38,43,46]
N = 4
BF = ml_dtypes.bfloat16
def gentries(a):
    return np.ascontiguousarray(a.reshape(8, 16, -1).transpose(0, 2, 1)).reshape(8, -1)
def gtable(e):
    e = np.asarray(e); return np.ascontiguousarray(e.reshape(8, -1, 16).transpose(0, 2, 1)).reshape(128, -1).astype(np.int32)
V, L, C, RO, MIN, SH = 1024, 8, 4, 3, 4, 3
T = N * V; LN = L // N; H = T // C
def lists(rng):
    return np.argsort(rng.random((8, L, T)), axis=-1).reshape(8, L, C, H)
def turn(pm):
    hl = np.zeros((8, L, T), np.int64)
    np.put_along_axis(hl, pm.reshape(8, L, T), np.broadcast_to(np.tile(np.arange(H), C), (8, L, T)), 2)
    return hl
def parts(rng):
    s = rng.permutation(np.array([24, 48, 64, 96, 128, 160, 200, 256])); lo = rng.integers(0, (257 - s)[:, None], (8, 16))
    x = lo[:, :, None] + rng.integers(0, s[:, None, None], (8, 16, T))
    hits = lo[:, :, None, None] + rng.integers(0, s[:, None, None, None], (8, 16, L, H))
    th = (6 * s[:, None] * rng.random((8, T)) ** 2).astype(np.int64)
    return x, hits, lists(rng), th
def pack(x, hits, pm, th):
    hl = turn(pm).reshape(8, L, N, V).transpose(2, 0, 1, 3).reshape(N, 8, L * V)
    cl = pm.reshape(8, N, LN, C, H).transpose(1, 0, 3, 2, 4).reshape(N, 8, C * LN * H)
    return {"fx": np.ascontiguousarray(x.reshape(8, 16, N, V).transpose(2, 0, 1, 3)).reshape(N, 128, V).astype(np.float32).astype(BF),
            "hv": np.ascontiguousarray(hits.reshape(8, 16, N, LN * H).transpose(2, 0, 1, 3)).reshape(N, 128, LN * H).astype(np.float32).astype(BF),
            "hl": np.stack([gtable(a) for a in hl]), "cl": np.stack([gtable(a) for a in cl]),
            "th": np.ascontiguousarray(th.reshape(8, N, V).transpose(1, 0, 2)).astype(np.int32)}
def contest(x, hits, live, pm):
    out = []
    for l in range(L):
        best = np.full((8, H), 2 ** 24, np.int64)
        for c in range(C):
            t = pm[:, l, c]
            d = np.add.reduce(np.abs(hits[:, :, l] - np.take_along_axis(x, t[:, None, :], 2)), axis=1)
            best = np.minimum(best, np.where(np.take_along_axis(live[:, l], t, 1), d * 4096 + t, 2 ** 24))
        out.append(best & 4095)
    return np.stack(out, axis=1)
def apart(x, b, hl):
    who = np.stack([np.take_along_axis(b[:, l], hl[:, l], 1) for l in range(L)], axis=1)
    e = np.stack([np.add.reduce(np.abs(x - np.take_along_axis(x, who[:, l][:, None, :], 2)), axis=1) for l in range(L)], axis=1)
    return who, e
def classes(rng):
    p = C * np.argsort(rng.random((L, C, H)), axis=2) + np.arange(C)[None, :, None]
    return np.take_along_axis(p, np.argsort(rng.random((L, C, H)), axis=1), axis=1)
def far(rng):
    c = np.arange(T) % C; x = rng.integers(1, 129, (16, T)); x[:, c == 0] = 0
    top = 255 - (rng.random((16, T)) < rng.choice(np.array([0.0, 0.1, 0.3]), T)).astype(np.int64)
    hits = np.full((16, L, H), 255); hits[:, rng.integers(0, L)] = 0
    th = np.where(c == 1, np.add.reduce(top, axis=0) + rng.integers(0, 2, T), 4081)
    return np.where(c == 1, top, x), hits, classes(rng), th
def fall(rng):
    x = 50 * (np.arange(T) % C) + rng.integers(0, 16, (16, T))
    hits = 50 * (np.arange(L) % C)[None, :, None] + rng.integers(0, 16, (16, L, H))
    return x, hits, classes(rng)
def late(rng):
    c = np.arange(T) % C
    x = rng.integers(0, 4, (16, T)) + np.where(c == 0, 0, np.where(c == 1, 208, np.where(c == 2, 200, 100)))
    hits = rng.integers(0, 4, (16, L, H))
    if RO > 2: hits[:, rng.integers(0, L)] += 200
    th = np.where(c == 0, 4081, np.where(c == 1, rng.integers(177, 369, T), 0))
    return x, hits, classes(rng), th
def setup_inputs(rng):
    return pack(*parts(rng))
def setup_inputs_ties(rng):
    x, hits, pm, th = parts(rng); lo = rng.integers(0, 253, (8, 16))
    x = lo[:, :, None] + rng.integers(0, 3, (8, 16, T)); hits = lo[:, :, None, None] + rng.integers(0, 3, (8, 16, L, H))
    for g in (2, 5): x[g] = x[g][:, rng.integers(0, 8, T)]
    e = apart(x, contest(x, hits, np.ones((8, L, T), bool), pm), turn(pm))[1]
    at = np.take_along_axis(e, rng.integers(0, L, (8, 1, T)), 1)[:, 0] + rng.integers(0, 2, (8, T))
    th = np.where(rng.random((8, T)) < 0.5, at, rng.integers(0, 18, (8, T)))
    return pack(x, hits, pm, th)
def setup_inputs_counts(rng):
    x, hits, pm, th = parts(rng)
    w = np.take_along_axis(pm, rng.integers(0, C, (8, L, 1, H)), 2)[:, :, 0]
    hits = np.stack([x[g][:, w[g]] for g in range(8)])
    o = rng.permutation(8); share = np.zeros((8, 1)); share[o[:5], 0] = np.array([1.0, 0.0, 0.2, 0.5, 0.8])
    th = np.where(rng.random((8, T)) < share, 4081, 0)
    for g in o[5:7]: x[g], hits[g], pm[g] = fall(rng)
    th[o[5]] = 4081; th[o[6]] = np.where(np.arange(T) // V == rng.integers(0, N), 4081, 0)
    x[o[7]], hits[o[7]], pm[o[7]], th[o[7]] = late(rng)
    return pack(x, hits, pm, th)
def setup_inputs_ends(rng):
    x, hits, pm, th = parts(rng)
    x = 255 * rng.integers(0, 2, (8, 16, T)); hits = 255 * rng.integers(0, 2, (8, 16, L, H)); th = rng.choice(np.array([0, 1, 1800, 2040, 2041, 2295, 4080, 4081]), (8, T))
    p = np.ascontiguousarray(pm.reshape(8, L, T)); a, z = np.arange(C), T - 1 - np.arange(C)
    for g in range(8):
        for l, h, want in ((0, 0, z), (L - 1, H - 1, a)):
            for c in range(C):
                k = int(np.nonzero(p[g, l] == want[c])[0][0]); m = c * H + h; was = int(p[g, l, m])
                p[g, l, m] = int(want[c]); p[g, l, k] = was if k != m else int(want[c])
    x[:, :, z] = 0; hits[:, :, 0, 0] = 255; x[:, :, a] = 255; hits[:, :, L - 1, H - 1] = 0
    for t in (z, a): th[:, t] = (np.arange(8) & 1)[:, None]
    p = p.reshape(8, L, C, H); o = rng.permutation(8)
    for g in o[:2]: x[g], hits[g], p[g], th[g] = far(rng)
    x[o[1]] = 255 - x[o[1]]; hits[o[1]] = 255 - hits[o[1]]
    g = int(o[2]); hits[g] = 0; x[g] = 255 - (rng.random((16, T)) < 0.08).astype(np.int64)
    x[g, rng.integers(0, 16, T // 8), rng.permutation(T)[:T // 8]] = 0
    th[g] = rng.choice(np.array([0, 1, 2, 3, 255, 256]), T)
    return pack(x, hits, p, th)
def setup_inputs_alike(rng):
    x, hits, pm, th = parts(rng); pm = np.ascontiguousarray(pm)
    pm[0] = np.arange(T).reshape(C, H); pm[1] = (np.arange(T).reshape(H, C)[:, ::-1]).T; pm[3] = pm[3, 0]; pm[4] = np.arange(T)[::-1].reshape(C, H)
    for g in (0, 4, 6): x[g] = np.tile(x[g][:, :V], (1, N))
    for g in (0, 5): th[g] = rng.integers(0, 2, T)
    x[5] = x[5][:, rng.integers(0, 4, T)]; hits[7] = hits[7][:, :, :1]
    return pack(x, hits, pm, th)
def setup_inputs_spread(rng):
    x, hits, pm, th = parts(rng)
    x = (np.exp2(8 * rng.random((8, 1, T))) * rng.random((8, 16, T))).astype(np.int64)
    hits = (np.exp2(8 * rng.random((8, 1, L, H))) * rng.random((8, 16, L, H))).astype(np.int64)
    th = np.minimum(np.exp2(12 * rng.random((8, T))).astype(np.int64) - 1, 4081)
    return pack(x, hits, pm, th)
def claims(hl, cl):
    a = np.stack([gentries(q) for q in hl]).astype(np.int64).reshape(N, 8, L, V).transpose(1, 2, 0, 3).reshape(8, L, T)
    b = np.stack([gentries(q) for q in cl]).astype(np.int64).reshape(N, 8, C, LN, H).transpose(1, 0, 3, 2, 4).reshape(8, L, C, H)
    return a, b
def check_inputs(d):
    bad = []
    for k in ("fx", "hv"):
        v = d[k].astype(np.float32)
        if not np.all((v >= 0) & (v <= 255) & (v == np.floor(v))): bad.append("whole numbers of " + k)
    for k, hi in (("hl", H - 1), ("cl", T - 1), ("th", 4081)):
        if np.min(d[k]) < 0 or np.max(d[k]) > hi: bad.append("range of " + k)
    if not bad:
        a, b = claims(d["hl"], d["cl"]); b = b.reshape(8, L, T)
        if not np.all(np.sort(b, axis=-1) == np.arange(T)) or not np.all(np.take_along_axis(a, b, 2) == np.tile(np.arange(H), C)): bad.append("claimants of the hits")
    return bad
def reference(fx, hv, hl, cl, th):
    x = fx.astype(np.float32).astype(np.int64).reshape(N, 8, 16, V).transpose(1, 2, 0, 3).reshape(8, 16, T)
    hits = hv.astype(np.float32).astype(np.int64).reshape(N, 8, 16, LN * H).transpose(1, 2, 0, 3).reshape(8, 16, L, H)
    mine, pm = claims(hl, cl); t = th.astype(np.int64).transpose(1, 0, 2).reshape(8, 1, T)
    live = np.ones((8, L, T), bool)
    for rnd in range(RO):
        b = contest(x, hits, live, pm); who, e = apart(x, b, mine)
        live = live & ((who == np.arange(T)) | (e >= t))
        n = np.add.reduce(live.astype(np.int64), axis=1)
        live = live & (n >= MIN)[:, None, :]; n = np.where(n >= MIN, n, 0)
        tot = (L - n)[:, None, :] * x
        for l in range(L): tot = tot + live[:, l][:, None, :] * np.take_along_axis(hits[:, :, l], mine[:, l][:, None, :], 2)
        x = tot >> SH
    return {"yx": np.ascontiguousarray(x.reshape(8, 16, N, V).transpose(2, 0, 1, 3)).reshape(N, 128, V).astype(np.float32).astype(BF),
            "yl": np.ascontiguousarray(live.reshape(8, L, N, V).transpose(2, 0, 1, 3)).reshape(N, 8, L * V).astype(np.float32).astype(BF)}

@@ -1,0 +1,621 @@
+from concourse.bass import DstId, RemoteDMATransfer
+from concourse.mybir import AluOpType as ALU, ActivationFunctionType as ACT
+
+RO = 3
+BF, F32, I32, U16 = "bfloat16", "float32", "int32", "uint16"
+SCRATCH = {}
+for _where, _dt, _list in (
+    ("dram", I32, (("ocl", 512, 128), ("dcl", 4, 128, 128))),
+    ("dram", BF, (("ofx", 1024, 128), ("ohv", 512, 512), ("dhv", 4, 128, 512), ("dth", 8, 128, 64))),
+    ("sbuf", I32, (("hs", 512), ("hq", 512), ("hr", 512), ("ths", 64), ("clc", 4, 128), ("s1", 512), ("s2", 256), ("cls", 512), ("clw", 1024),
+                   ("z1", 512), ("z2", 512), ("Km", 128), ("Ko", 128), ("x1", 1024), ("yi", 1024), ("pi", 16))),
+    ("sbuf", U16, (("hbo", 512), ("posT", 512), ("clu", 512), ("clx", 512), ("ob", 128))),
+    ("sbuf", F32, (("thc", 512), ("tio", 4096), ("z3", 512), ("K", 512), ("M1", 256), ("Sm", 1024), ("pf", 24), ("row", 192), ("io3", 128),
+                   ("posc", 256), ("pos0", 256))),
+    ("sbuf", BF, (("hu", 4, 256), ("hb", 1024), ("thh", 64), ("thl", 64), ("thw", 4096), ("one", 1024), ("xw", 8192), ("hh", 2048), ("h1p", 2048),
+                  ("D", 8192), ("A", 8192), ("A2", 8192), ("Db", 2048), ("vw", 8192), ("vT", 8192), ("best", 512), ("dd", 512), ("live", 16, 32),
+                  ("L", 512), ("d8", 512), ("W8", 512), ("xc", 1024), ("xm", 1024), ("OT", 8, 192), ("OL", 8, 192), ("KEYW", 144), ("ONEW", 144),
+                  ("INVW", 288), ("THW", 288), ("SUMW", 144), ("SELW", 144), ("RW", 768), ("ID", 1024), ("BC", 2048), ("NW", 128), ("XB", 1024),
+                  ("WX", 1024), ("Z", 128))),
+    ("psum", F32, tuple(("pb%d" % _b, 512) for _b in range(8))),
+):
+    for _x in _list:
+        SCRATCH[_x[0]] = (_where, ([] if _where == "dram" else [128]) + list(_x[1:]), _dt)
+SEMAPHORES = ["cV", "cS", "cP", "cG", "sent", "acl", "ahl", "ath", "afx", "ahv", "ao0", "ao1"] + ["d%d" % _k for _k in range(40)]
+
+EST = {"CY": 1.04, "GA": 1.56, "PE": 0.52, "FIX": 60.0, "LAT": 90.0, "TT": 2.0, "DQ": 70.0, "MASK": (0, 1, 0, 1, 0, 1, 0, 1),
+       "LEAD": 10000.0, "Q": 50.0, "CONST": 1e6, "WDMA": 0, "WLAT": 7000.0, "NH": 2, "VB": 0.0}
+PLAN = "1e0k1q1A1m1U1o0200080c040g0a0e061i1g1s1y1G1w1K2Q1Q0w0q0s0o0m1k0u0U140y0A0C0Q0W0S2O12104g4s4o0i1S1C221E20261Y0E1W242y2c2e0I2i280G4k4cgM161u2F182g2I2n2N4j4w4A4v4r4n4E0K4z4f4H3i3g2a2A2D4DgIh21ah5gAgY4KgP4N0M0Y2W2U3q1I3m2s3o3k3s1O3ugQ3630320O3w4W3y4OgU4Q2kgD4S3A503Z4Y1c4Ugj5854gWh02o3C52342YgE5agqfW5cgn563E5eh83G5g3K5i1M5k5m2w5ogT3V2rgLgG3O3chg3X5t3I423M445G415r465I5whshk5A645C485u4ahi5E66gl60623Qhw5O5Q6c5K6ghmhofY5y5Mg45Sgs68hy6i6ehq6shA6o3S2u6ahuhbhC6E6k5Ug8396q6GhE6m5W5Y6M6Q6w2ShG2LhIhK6ugphM6y6OhR2GhO3e3bg0hSgc6ShWguhc6Ahf6CiE6I6K727O746X6Vgwis7WiG7NgzhYi4icieiAg2i66Yg670ioiC4I7V7Q7Si076787a7c80gai27ehU7giu7Y7i827k7m7o7qi884867s88iaiqig8aii7A8eiwik8ch68g8iimiy7w7D7IiU7LiQ7E7HiW8kiM8w8o8q8ziS7zj28sj4iIiK8AjagejeiOjcj6iY8v8Dgg8E8Mjgj8j0kckbjkki7u8Ikl8Gjjjrjtkgkekokm8Ujmkq8O8K8Q8Sksjojukujykw8WkCjAky8Y90kAkEjCkGkIjE9294jwjKjGjIjM96jO98jQ9akUkMkQkY8m9e9i9mkX9ol09gkT9dk2jYk6k1k99q9s9ukO9SjUjW9Ga49Ck59kl2la9wa09I9y9Oa69Ea2l49U9Aa89Kaa9Ml6le9QaEaGlc9WacaoagaAl8liak9YawlkasaiaqlgaylmaCamaeauaKlobAaJbDbLaRaTaOaMbEbGlqbIlslulwlElylBlDbMbOlGbQlIlKbSaUbUbWaYlMmclOb0kKb2moaWjSb4mgb6bYbac2memim4lSb8c0bcc4bem6mqlUlQmsm0c6bgc8cccgbkmulWbsbvm2lYbomkmwmmmycockcfbrcnm8mAbwmQcrbzcibmmamCmSmUmMmImEn2mYmWcscwmKmOcumGn4n0n6nYcIcAn9cEo1nhnfcyo9nco2nanicKnmo6nooanqoenscCcMognycGcOoinAokcQnknuo4oqcSnwocomcUcWd4cYosd1oonCnEdadCoud6owoynUnMnQoInSnOoMd3dGoEnIoLdqoAdcnWdEoHoDdIoOnKd8dSdUdOdQdidup2caoQoUdkdedWdKdwdgdsdmdydYdooSp6esdAe8e4e0p4oWoYdMbie2eaeup0eoegekp8ece6emeepaeqeiewezfdeFeHpceCeAfapefjfefgeKeIpgpipspkfkpmpopAprnGpwpyfofmfqeMq0qcq4fsq2qeq6fupuqgeOqipOpSpQpUpCfCq8eQpGqafEpEpIpWqEpKpYqAqkqweYqmfwqGpMqIqMqyqOqsqCqKqQqoeSqqf2fyquqSqUf4fGf0eUqXryrBr5r3r0qYrGfIrJeWf6fArCr6rKrafKrircr8rOrerQrgfMrSf8rkrqrErUrmrMs4ros0rWs2rsrus6rYs8rwsafOfSscsgfQsefUsi"
+ARRIVE = {"acl": 6000.0, "ahl": 12000.0, "ath": 6000.0, "afx": 8000.0, "ahv": 10000.0}
+EXT = ("fx", "hv", "hl", "cl", "th", "yx", "yl")
+DEAD = float(1 << 24)
+
+
+def r(name, *idx):
+    if name in EXT:
+        return (name, idx, 0, 0, 0, 0)
+    shape = SCRATCH[name][1]
+    full = list(idx) + [slice(None)] * (len(shape) - len(idx))
+    lo, hi = [], []
+    for s, n in zip(full, shape):
+        if isinstance(s, slice):
+            rg = range(*s.indices(n))
+            lo.append(rg[0]); hi.append(rg[-1])
+        else:
+            lo.append(s); hi.append(s)
+    a = b = 0
+    for k in range(1, len(shape)):
+        a = a * shape[k] + lo[k]; b = b * shape[k] + hi[k]
+    return (name, idx, lo[0], hi[0], a, b)
+
+
+def c(name, a, n, step=1):
+    return r(name, slice(None), slice(a, a + n, step) if step != 1 else slice(a, a + n))
+
+
+def p(vb, a=0, n=512):
+    return ("@", vb, a, a + n)
+
+
+def build(me):
+    ops = []
+    nvb = [0]
+    lead = [0.0]
+    CY, GA, PEC, FIX = EST["CY"], EST["GA"], EST["PE"], EST["FIX"]
+
+    def bank():
+        nvb[0] += 1
+        return nvb[0]
+
+    def add(alts, R, W, kind="c", lat=0.0, sem=None, at=0.0, prio=0.0):
+        ops.append(dict(alts=alts, R=R, W=W, kind=kind, lat=lat, sem=sem, at=at, prio=prio + lead[0]))
+
+    def width(x):
+        if x[0] == "@":
+            return x[3] - x[2]
+        shape = SCRATCH[x[0]][1]
+        full = list(x[1]) + [slice(None)] * (len(shape) - len(x[1]))
+        n = 1
+        for s, m in zip(full[1:], shape[1:]):
+            if isinstance(s, slice):
+                n *= len(range(*s.indices(m)))
+        return n
+
+    def narrow(x):
+        return x[0] != "@" and SCRATCH[x[0]][2] in (BF, U16)
+
+    def vcost(n, per):
+        return FIX + max(64.0, n * per) * CY
+
+    def vc(out, in_):
+        return vcost(width(in_), 0.5 if narrow(out) and narrow(in_) else 1.0)
+
+    def val(ap, s):
+        return ap(s) if isinstance(s, tuple) else s
+
+    def ts(out, in0, s1, s2, op0, op1=None):
+        def f(q, ap):
+            if op1 is None:
+                return q.tensor_scalar(ap(out), ap(in0), val(ap, s1), None, op0)
+            return q.tensor_scalar(ap(out), ap(in0), val(ap, s1), val(ap, s2), op0, op1)
+        add({"V": (vc(out, in0), f)}, [in0] + [s for s in (s1, s2) if isinstance(s, tuple)], [out])
+
+    def tt(out, in0, in1, op):
+        per = 1.0 if "@" in (in0[0], in1[0]) else EST["TT"]
+        add({"V": (vcost(width(in0), per), lambda q, ap: q.tensor_tensor(ap(out), ap(in0), ap(in1), op))}, [in0, in1], [out])
+
+    def cp(out, in_):
+        add({"V": (vc(out, in_), lambda q, ap: q.tensor_copy(ap(out), ap(in_)))}, [in_], [out])
+
+    def fill(out, v):
+        add({"V": (vc(out, out), lambda q, ap: q.memset(ap(out), v))}, [], [out])
+
+    def act(out, in_, fn, bias=0.0, scale=1.0):
+        add({"S": (vcost(width(in_), 1.0), lambda q, ap: q.activation(ap(out), ap(in_), fn, bias=bias, scale=scale))}, [in_], [out])
+
+    def plus(out, in_, bias):
+        add({"V": (vc(out, in_), lambda q, ap: q.tensor_scalar(ap(out), ap(in_), bias, None, ALU.add)),
+             "S": (vcost(width(in_), 1.0), lambda q, ap: q.activation(ap(out), ap(in_), ACT.Identity, bias=bias))}, [in_], [out])
+
+    def times(out, in_, s):
+        add({"V": (vc(out, in_), lambda q, ap: q.tensor_scalar(ap(out), ap(in_), val(ap, s), None, ALU.mult)),
+             "S": (vcost(width(in_), 1.0), lambda q, ap: q.activation(ap(out), ap(in_), ACT.Identity, scale=val(ap, s)))},
+            [in_] + ([s] if isinstance(s, tuple) else []), [out])
+
+    def gather(out, win, off):
+        d = FIX + width(out) * GA * CY
+        add({"V": (d, lambda q, ap: q.tensor_copy(ap(out), ap(win).indirect(ap(off)))),
+             "S": (d, lambda q, ap: q.activation(ap(out), ap(win).indirect(ap(off)), ACT.Copy))}, [win, off], [out])
+
+    def gather_op(out, win, off, in1, op):
+        d = FIX + width(out) * GA * CY
+        add({"V": (d, lambda q, ap: q.tensor_tensor(ap(out), ap(win).indirect(ap(off)), ap(in1), op))}, [win, off, in1], [out])
+
+    def mm(lst):
+        def f(q, ap):
+            last = None
+            for (o, l, x, a, b) in lst:
+                last = q.matmul(ap(o), ap(l), ap(x), a, b)
+            return last
+        R = []
+        for (o, l, x, a, b) in lst:
+            R += [t for t in (l, x) if t not in R]
+        add({"P": (30.0 + sum(max(64, width(x)) for (o, l, x, a, b) in lst) * PEC, f)}, R, [lst[0][0]])
+
+    def iota(out, pat, base, mult):
+        if SCRATCH[out[0]][2] == I32:
+            f = lambda q, ap: q.iota(ap(out), pat, base, mult)
+        else:
+            f = lambda q, ap: q.iota(ap(out), pat, base, mult, allow_small_or_imprecise_dtypes=True)
+        add({"G": (160.0 + 2 * width(out) * CY, f)}, [], [out])
+
+    def select(out, pat, base):
+        n = width(out)
+        add({"G": (200.0 + 2 * n * CY, lambda q, ap: q.affine_select(ap(out), ap(c("one", 0, n)), pat, ALU.is_equal, 0.0, base, -1))}, [c("one", 0, n)], [out])
+        ops[-1]["behind"] = "ahv"
+
+    def dma(pairs, lat=2200.0, engs="YS", prio=0.0):
+        f = lambda q, ap: [q.dma_start(ap(o), ap(i)) for (o, i) in pairs]
+        add({e: (EST["DQ"] * len(pairs), f) for e in engs}, [i for (o, i) in pairs], [o for (o, i) in pairs], kind="d", lat=lat, prio=prio)
+
+    def send(sem, pieces):
+        add({"G": (500.0, pieces)}, [s for d in pieces for (s, t) in pieces[d]], [], kind="r", sem=sem, prio=1e6)
+
+    def arrive(sem, W, at):
+        add({}, [], W, kind="a", sem=sem, at=at)
+
+    others = [d for d in range(4) if d != me]
+    runs = [(a, b) for (a, b) in ((0, me), (me + 1, 4)) if b > a]
+    S = slice
+    ALL = slice(None)
+
+    dma([(r("ocl", S(128 * a, 128 * b)), r("cl", S(32 * a, 32 * b))) for (a, b) in runs], engs="Y", prio=9e6)
+    dma([(r("ths"), r("th"))], engs="S", prio=9e6)
+    for half in range(2):
+        dma([(r("hs", S(32 * q, 32 * q + 32), S(128 * d, 128 * d + 128)), r("hl", S(32 * d, 32 * d + 32), S(128 * q, 128 * q + 128)))
+             for q in (2 * half, 2 * half + 1) for d in range(4)], engs="YS"[half], prio=8e6)
+    dma([(r("dcl", me), r("cl", S(32 * me, 32 * me + 32)))], engs="Y", prio=7e6)
+    dma([(r("ofx", S(256 * a, 256 * b)), r("fx", S(32 * a, 32 * b))) for (a, b) in runs], lat=3000.0, engs="S", prio=6e6)
+    dma([(r("ohv", S(128 * a, 128 * b)), r("hv", S(32 * a, 32 * b))) for (a, b) in runs], lat=4000.0, engs="Y", prio=5e6)
+    dma([(c("xc", 512 * f + 128 * me, 128), r("fx", S(32 * me + 16 * f, 32 * me + 16 * f + 16))) for f in range(2)], engs="S", prio=4e6)
+    dma([(r("dhv", me), r("hv", S(32 * me, 32 * me + 32)))], engs="Y", prio=4e6)
+    lead[0] = 1e6
+    fill(r("clw"), 0)
+    fill(r("one"), 1.0)
+    for k in range(4):
+        act(c("thw", 1024 * k, 1024), r("one"), ACT.Copy)
+    send("acl", {d: [(r("ocl", S(128 * d, 128 * d + 128)), r("dcl", me))] for d in others})
+    cp(r("thh"), r("ths"))
+    tt(r("thl"), r("ths"), r("thh"), ALU.subtract)
+    send("ath", {d: [(r("thh"), r("dth", me)), (r("thl"), r("dth", 4 + me))] for d in others})
+    dma([(r("dth", me), r("thh")), (r("dth", 4 + me), r("thl"))], engs="Y")
+    ts(r("hq"), r("hs"), 15, None, ALU.bitwise_and)
+    ts(r("hr"), r("hs"), 4, None, ALU.arith_shift_right)
+    cp(r("hu", ALL, ALL, S(0, 128)), r("hq"))
+    cp(r("hu", ALL, ALL, S(128, 256)), r("hr"))
+    send("ahl", {d: [(r("hu", ALL, d), c("hb", 256 * me, 256))] for d in others})
+    cp(c("hb", 256 * me, 256), r("hu", ALL, me))
+    send("afx", {d: [(r("ofx", S(256 * d + 128 * f, 256 * d + 128 * f + 128)), c("xc", 512 * f + 128 * me, 128)) for f in range(2)] for d in others})
+    send("ahv", {d: [(r("ohv", S(128 * d, 128 * d + 128)), r("dhv", me))] for d in others})
+    lead[0] = 0.0
+    arrive("acl", [r("dcl", d) for d in others], ARRIVE["acl"])
+    arrive("ath", [r("dth", k + d) for d in others for k in (0, 4)], ARRIVE["ath"])
+    arrive("ahl", [c("hb", 256 * d, 256) for d in others], ARRIVE["ahl"])
+    arrive("afx", [c("xc", 512 * f + 128 * d, 128) for d in others for f in range(2)], ARRIVE["afx"])
+    arrive("ahv", [r("dhv", d) for d in others], ARRIVE["ahv"])
+    dma([(r("clc", S(64 * m, 64 * m + 64), ALL, S(64 * f, 64 * f + 64)), r("dcl", ALL, S(64 * f, 64 * f + 64), S(64 * m, 64 * m + 64)))
+         for f in range(2) for m in range(2)], engs="S", prio=3e6)
+    dma([(r("clw", S(64 * m + 4 * f + cc, 64 * m + 64, 16)), r("dcl", ALL, S(64 * f + cc, 64 * f + 64, 4), S(64 * m, 64 * m + 64)))
+         for f in range(2) for m in range(2) for cc in range(4)], engs="Y", prio=3e6)
+    dma([(r("thw", S(16 * gg + 2 * f, 16 * gg + 2 * f + 2)), r("dth", ALL, S(32 * me + 16 * f, 32 * me + 16 * f + 16)))
+         for f in range(2) for gg in range(8)], engs="S", prio=2e6)
+    for f in range(2):
+        dma([(r("hh", S(64 * m, 64 * m + 64), S(1024 * f + 512 * hf, 1024 * f + 512 * hf + 512)), r("dhv", ALL, S(64 * f + 2 * m + hf, 64 * f + 64, 4)))
+             for m in range(2) for hf in range(2)], engs="Y", prio=1e6 - f)
+
+    lead[0] = EST["CONST"]
+    iota(c("pi", 0, 1), [[0, 1]], 0, 1)
+    iota(r("row"), [[1, 192]], 0, 0)
+    iota(r("pos0"), [[1024, 4], [16, 64]], 0, 0)
+    iota(r("io3"), [[0, 8], [1, 16]], 0, 0)
+    pi = lambda k: c("pi", k, 1)
+    pf = lambda k: c("pf", k, 1)
+    SHR, AND, MUL, ADD, EQ = ALU.arith_shift_right, ALU.bitwise_and, ALU.mult, ALU.add, ALU.is_equal
+    ts(pi(1), pi(0), 4, None, SHR)
+    ts(pi(2), pi(0), 15, None, AND)
+    ts(pi(3), pi(0), 4, 1, SHR, AND)
+    ts(pi(4), pi(0), 5, None, SHR)
+    ts(pi(5), pi(0), 4, 3, SHR, AND)
+    ts(pi(6), pi(0), 6, None, SHR)
+    ts(pi(7), pi(0), 2, 3, SHR, AND)
+    ts(pi(8), pi(0), 1, 7, SHR, AND)
+    cp(pf(0), pi(0))
+    ts(pf(1), pi(1), 16.0, 15.0, MUL, ADD)
+    cp(pf(2), pi(2))
+    ts(pf(3), pi(2), 8.0, 7.0, MUL, ADD)
+    ts(pf(4), pi(6), 16.0, 15.0, MUL, ADD)
+    ts(pf(5), pi(5), 32.0, pf(4), MUL, ADD)
+    ts(pf(6), pi(2), 0.0, None, EQ)
+    ts(pf(7), pi(2), 64.0, None, ADD)
+    ts(pf(8), pi(4), 16.0, pf(7), MUL, ADD)
+    for f in range(2):
+        ts(pf(9 + 2 * f), pi(3), float(f), 64.0, EQ, MUL)
+        ts(pf(10 + 2 * f), pi(3), float(f), None, EQ)
+        ts(pf(13 + f), pi(7), float(f), 1024.0, EQ, MUL)
+        ts(pf(15 + f), pi(8), float(f), None, EQ)
+    for k in range(4):
+        ts(c("RW", 192 * k, 192), r("row"), pf(8), pf(9 + k), EQ, MUL)
+    ts(r("ONEW"), c("row", 0, 144), pf(1), None, EQ)
+    times(r("KEYW"), r("ONEW"), 4096.0)
+    for f in range(2):
+        times(c("INVW", 144 * f, 144), r("ONEW"), pf(13 + f))
+        times(c("THW", 144 * f, 144), r("ONEW"), pf(15 + f))
+    ts(r("SUMW"), c("row", 0, 144), pf(3), None, EQ)
+    ts(r("SELW"), c("row", 0, 144), pf(5), pf(6), EQ, MUL)
+    ts(c("ID", 0, 128), c("row", 0, 128), pf(0), None, EQ)
+    for k, wgt in enumerate((-1.0, -DEAD, 8192.0, -32768.0, 1.0 / 512.0, 8.0, DEAD)):
+        times(c("ID", 128 * k + 128, 128), c("ID", 0, 128), wgt)
+    IDN, NEG, PEN, BST, DED, SML, ID8, ALLD = [c("ID", 128 * k, 128) for k in range(8)]
+    if not EST["WDMA"]:
+        select(r("WX"), [[1, 8], [0, 8], [8, 16]], 0)
+    ts(r("posc"), r("pos0"), pf(2), None, ADD)
+    ts(r("NW"), r("io3"), pf(2), None, EQ)
+    lead[0] = 0.0
+    for k in range(4):
+        iota(c("tio", 1024 * k, 1024), [[1, 1024]], 1024 * k, 0)
+        ops[-1]["behind"] = "ahv"
+    for k in range(2):
+        select(c("BC", 1024 * k, 1024), [[1, 8], [16, 8], [0, 16]], 8 * k)
+    select(c("XB", 0, 256), [[1, 2], [0, 16], [2, 8]], 0)
+    times(c("XB", 768, 256), c("XB", 0, 256), 0.125)
+    times(c("XB", 256, 256), c("XB", 0, 256), 512.0)
+    times(c("XB", 512, 256), c("XB", 0, 256), -512.0)
+    fill(r("Z"), 0.0)
+    sl = lambda name, top, k: c(name, top - k, 128)
+
+    lead[0] = 1e6
+    tt(c("s1", 0, 256), r("clc", ALL, S(0, 2)), r("clc", ALL, S(2, 4)), ALU.min)
+    tt(c("s1", 256, 256), r("clc", ALL, S(0, 2)), r("clc", ALL, S(2, 4)), ALU.max)
+    tt(c("s2", 0, 128), c("s1", 0, 128), c("s1", 128, 128), ALU.max)
+    tt(c("s2", 128, 128), c("s1", 256, 128), c("s1", 384, 128), ALU.min)
+    tt(c("cls", 0, 128), c("s1", 0, 128), c("s1", 128, 128), ALU.min)
+    tt(c("cls", 384, 128), c("s1", 256, 128), c("s1", 384, 128), ALU.max)
+    tt(c("cls", 128, 128), c("s2", 0, 128), c("s2", 128, 128), ALU.min)
+    tt(c("cls", 256, 128), c("s2", 0, 128), c("s2", 128, 128), ALU.max)
+    cp(r("clu"), r("cls"))
+    if EST["WDMA"]:
+        ts(r("z1"), r("cls"), 7, 7, SHR, AND)
+        ts(r("z2"), r("cls"), 10, None, SHR)
+        b = bank()
+        ts(p(b), r("z1"), 384.0, None, MUL)
+        tt(p(b), p(b), r("cls"), ADD)
+        ts(r("z3"), r("z2"), -896.0, None, MUL)
+        tt(r("z1"), p(b), r("z3"), ADD)
+        cp(r("clx"), r("z1"))
+
+    def window(f, src, rs=range(4)):
+        if EST["WDMA"]:
+            dma([(r("xw", S(16 * l, 16 * l + 16), S(4096 * f, 4096 * f + 4096)), c(src, 512 * f, 512)) for l in range(8)], lat=EST["WLAT"], engs="Y")
+            return
+        for rr in rs:
+            for up in range(2):
+                b = bank()
+                mm([(p(b, 128 * u, 128), c("WX", 128 * (4 * up + u), 128), c(src, 512 * f + 128 * rr, 128), True, True) for u in range(4)])
+                plus(c("xw", 4096 * f + 1024 * rr + 512 * up, 512), p(b), 0.0)
+
+    def stream(f):
+        F = 4096 * f
+        X = 512 * f
+        H = 256 * f
+        NH = EST["NH"]
+        RH = 4 // NH
+        lv = lambda cc: r("live", ALL, S(8 * f + 2 * cc, 8 * f + 2 * cc + 2))
+
+        def base(b, rr, closes):
+            return [(p(b, 64 * rr, 64), c("RW", 192 * (2 * f + t) + 64 - 64 * m, 128), c("hb", 256 * rr + 128 * t + 64 * m, 64),
+                     (t, m) == (0, 0), closes and (t, m) == (1, 1)) for t in range(2) for m in range(2)]
+        b = bank()
+        mm([x for rr in range(4) for x in base(b, rr, True)])
+        cp(c("hbo", H, 256), p(b, 0, 256))
+        b = bank()
+        for rr in range(4):
+            gather_op(c("vT", F + 1024 * rr, 1024), r("clw"), c("hbo", H + 64 * rr, 64), c("tio", 1024 * rr, 1024), ALU.is_lt)
+            mm(base(b, rr, False) + [(p(b, 64 * rr, 64), sl("INVW", 144 * f + 15, s), c("vT", F + 1024 * rr + s, 1024 - s, 16), False, s == 15) for s in range(16)])
+        cp(c("posT", H, 256), p(b, 0, 256))
+        for cc in range(4):
+            gather(c("A2", F + 1024 * cc, 1024), r("thw"), c("clu", 128 * cc + 64 * f, 64))
+        b = bank()
+        for cc in range(4):
+            mm([(p(b, 64 * cc, 64), sl("THW", 144 * f + 15, s), c("A2", F + 1024 * cc + s, 1024 - s, 16), s == 0, s == 15) for s in range(16)])
+        plus(c("thc", H, 256), p(b, 0, 256), 0.0)
+        window(f, "xc")
+        ts(c("x1", X, 512), c("xc", X, 512), 1.0, None, ADD)
+        for hf in range(2):
+            b = bank()
+            mm([(p(b, 64 * s, 64), IDN, c("hh", 1024 * f + 8 * hf + s, 1024 - 8 * hf - s, 16), True, True) for s in range(8)])
+            plus(c("h1p", 1024 * f + 512 * hf, 512), p(b), 1.0)
+
+        for rnd in range(RO):
+            last = rnd == RO - 1
+            for cc in range(4):
+                a = F + 1024 * cc
+                gather_op(c("D", a, 1024), c("xw", F, 4096), c("clx" if EST["WDMA"] else "clu", 128 * cc + 64 * f, 64), c("hh", 1024 * f, 1024), ALU.subtract)
+                act(c("A", a, 1024), c("D", a, 1024), ACT.Abs)
+            b = bank()
+            for cc in range(4):
+                pc = p(b, 64 * cc, 64)
+                lst = [(pc, ALLD, c("one", 0, 64), True, False), (pc, PEN, lv(cc), False, False)] if rnd else []
+                mm(lst + [(pc, sl("KEYW", 15, s), c("A", F + 1024 * cc + s, 1024 - s, 16), s == 0 and not rnd, s == 15) for s in range(16)])
+            tt(c("K", H, 256), p(b, 0, 256), r("posc"), ADD)
+            tt(c("M1", 128 * f, 128), c("K", H, 128), c("K", H + 128, 128), ALU.min)
+            km = c("Km", 64 * f, 64)
+            tt(km, c("M1", 128 * f, 64), c("M1", 128 * f + 64, 64), ALU.min)
+            ts(c("Ko", 64 * f, 64), km, 4095, None, AND)
+            cp(c("ob", 64 * f, 64), c("Ko", 64 * f, 64))
+            for hf in range(2):
+                gather(c("Db", 1024 * f + 512 * hf, 512), c("D", F, 4096), c("ob", 64 * f + 32 * hf, 32))
+            for cc in range(4):
+                tt(c("best", H + 64 * cc, 64), c("K", H + 64 * cc, 64), km, EQ)
+            if rnd:
+                ts(c("dd", H, 256), c("K", H, 256), DEAD, None, ALU.is_ge)
+            for cc in range(4):
+                for hf in range(2):
+                    b = bank()
+                    a = F + 1024 * cc + 512 * hf
+                    mm([(p(b), IDN, c("D", a, 512), True, False), (p(b), NEG, c("Db", 1024 * f + 512 * hf, 512), False, True)])
+                    act(c("A2", a, 512), p(b), ACT.Abs)
+                pc = p(bank(), 0, 64)
+                lst = [(pc, sl("ONEW", 15, s), c("A2", F + 1024 * cc + s, 1024 - s, 16), s == 0, False) for s in range(16)]
+                if rnd:
+                    lst.append((pc, DED, c("dd", H + 64 * cc, 64), False, False))
+                mm(lst + [(pc, BST, c("best", H + 64 * cc, 64), False, True)])
+                tt(lv(cc), pc, c("thc", H + 64 * cc, 64), ALU.is_ge)
+            for cc in range(4):
+                for hf in range(2):
+                    b = bank()
+                    hp = c("h1p", 1024 * f + 512 * hf, 512)
+                    out = c("vw", F + 1024 * cc + 512 * hf, 512)
+                    bc = [c("BC", 128 * (8 * hf + s), 128) for s in range(8)]
+                    if EST["MASK"][2 * cc + hf]:
+                        mm([(p(b), SML, hp, True, False)] + [(p(b, 64 * s, 64), bc[s], lv(cc), False, s == 7) for s in range(8)])
+                        act(out, p(b), ACT.Relu, bias=-512.0, scale=512.0)
+                    else:
+                        mm([(p(b, 64 * s, 64), bc[s], lv(cc), True, True) for s in range(8)])
+                        tt(out, p(b), hp, MUL)
+            for part in range(NH):
+                rs = range(RH * part, RH * part + RH)
+                sm, se = bank(), bank()
+                n, hh, xx = 64 * RH, H + 64 * RH * part, X + 128 * RH * part
+                for k, rr in enumerate(rs):
+                    for hf in range(2):
+                        gather(c("vT", F + 1024 * rr + 512 * hf, 512), c("vw", F, 4096), c("posT", H + 64 * rr + 32 * hf, 32))
+                    mm([(p(se, 64 * k, 64), sl("SELW", 15, a), c("vT", F + 1024 * rr + 64 * a, 64), a == 0, a == 15) for a in range(16)])
+                    lst = [(p(sm, 0, 2 * n), r("Z"), c("h1p", 1024 * f, 2 * n), True, False)] if k == 0 else []
+                    mm(lst + [(p(sm, 128 * k, 128), sl("SUMW", 7, u), c("vT", F + 1024 * rr + 128 * u, 128), False, False) for u in range(8)])
+                ts(c("L", hh, n), p(se, 0, n), 0.5, None, ALU.is_lt)
+                b = bank()
+                mm([(p(b, 0, n), r("NW"), c("L", hh, n), True, True)])
+                ts(c("d8", hh, n), p(b, 0, n), 4.5, 8.0, ALU.is_gt, MUL)
+                tt(c("W8", hh, n), p(b, 0, n), c("d8", hh, n), ALU.max)
+                ot = S(4 * f + rs[0], 4 * f + rs[-1] + 1)
+                if last:
+                    b = bank()
+                    mm([(p(b, 0, n), r("NW"), c("L", hh, n), True, False), (p(b, 0, n), ID8, c("L", hh, n), False, True)])
+                    ts(r("OT", ALL, ot, S(128, 192)), p(b, 0, n), 4.5, None, ALU.is_lt)
+                cols = [(128 * k + 64 * w, w, hh + 64 * k) for k in range(RH) for w in range(2)]
+                mm([(p(sm, x, 64), c("XB", (512 if last else 256) + 128 * w, 128), c("d8", y, 64), False, x == 2 * n - 64) for (x, w, y) in cols])
+                if last:
+                    act(c("Sm", xx, 2 * n), p(sm, 0, 2 * n), ACT.Relu, bias=-0.4375, scale=0.125)
+                else:
+                    act(c("Sm", xx, 2 * n), p(sm, 0, 2 * n), ACT.Relu, bias=512.4375, scale=-0.125)
+                b = bank()
+                mm([(p(b, x, 64), c("XB", 768 + 128 * w, 128), c("W8", y, 64), True, True) for (x, w, y) in cols])
+                pw = p(b, 0, 2 * n)
+                tt(pw, pw, c("x1", xx, 2 * n), MUL)
+                tt(c("yi", xx, 2 * n), pw, c("Sm", xx, 2 * n), ADD if last else ALU.subtract)
+                if last:
+                    ts(r("OT", ALL, ot, S(0, 128)), c("yi", xx, 2 * n), -1.0, None, ADD)
+                else:
+                    ts(c("xm", xx, 2 * n), c("yi", xx, 2 * n), 511.0, None, ADD)
+                    ts(c("x1", xx, 2 * n), c("yi", xx, 2 * n), 511, None, AND)
+                    if not EST["WDMA"]:
+                        window(f, "xm", rs)
+            if EST["WDMA"] and not last:
+                window(f, "xm")
+        sem = "ao%d" % f
+        send(sem, {d: [(r("OT", ALL, 4 * f + d), r("OL", ALL, 4 * f + me))] for d in others})
+        put = lambda t, d, k: [(r("yx", S(32 * d + 16 * f, 32 * d + 16 * f + 16)), r(t, ALL, k, S(0, 128))),
+                               (r("yl", S(2 * d + f, 2 * d + f + 1)), r(t, ALL, k, S(128, 192)))]
+        dma(put("OT", me, 4 * f + me), engs="Y")
+        arrive(sem, [r("OL", ALL, 4 * f + d) for d in others], -1.0)
+        dma([x for d in others for x in put("OL", d, 4 * f + d)], engs="Y")
+
+    for f in range(2):
+        lead[0] = EST["LEAD"] * (1 - f)
+        stream(f)
+    return ops
+
+
+def hazards(ops):
+    seen = {}
+    deps = []
+    sends = {}
+    for i, op in enumerate(ops):
+        d = set()
+        both = [(x, False) for x in op["R"] if x[0] not in EXT] + [(x, True) for x in op["W"] if x[0] not in EXT]
+        for (x, wr) in both:
+            if x[0] == "@":
+                if seen.get(x[1], i) != i:
+                    d.add(seen[x[1]])
+                seen[x[1]] = i
+                continue
+            for (j, w2, a, b, e, f) in seen.get(x[0], ()):
+                if (wr or w2) and a <= x[3] and x[2] <= b and e <= x[5] and x[4] <= f:
+                    d.add(j)
+        for (x, wr) in both:
+            if x[0] == "@":
+                continue
+            old = seen.setdefault(x[0], [])
+            if wr and len(SCRATCH[x[0]][1]) == 2 and all(isinstance(s, slice) and s.step in (None, 1) for s in x[1]):
+                old[:] = [t for t in old if not (x[2] <= t[2] and t[3] <= x[3] and x[4] <= t[4] and t[5] <= x[5])]
+            old.append((i, wr, x[2], x[3], x[4], x[5]))
+        if op["kind"] == "r":
+            sends[op["sem"]] = i
+        if op["kind"] == "a" and op["at"] < 0:
+            op["after"] = sends[op["sem"]]
+        if "behind" in op:
+            d.add(sends[op["behind"]])
+        deps.append(d)
+    return deps
+
+
+def place(ops, deps, order, eng):
+    n = len(ops)
+    LAT = EST["LAT"]
+    first, lastuse = {}, {}
+    for i, op in enumerate(ops):
+        for x in op["R"] + op["W"]:
+            if x[0] == "@":
+                first.setdefault(x[1], i)
+                lastuse[x[1]] = i
+    opens = {i: vb for vb, i in first.items()}
+    holder = [None] * 8
+    bank_of = {}
+    deps = [set(d) for d in deps]
+    done = [None] * n
+    start = [0.0] * n
+    free = {e: 0.0 for e in "VSPGY"}
+    for i in order:
+        op, e = ops[i], eng[i]
+        t = max([done[j] + LAT for j in deps[i]] or [0.0])
+        if e is None:
+            start[i] = done[i] = max(t, op["at"] if op["at"] >= 0 else done[op["after"]] + 3000.0)
+            continue
+        if i in opens:
+            tb, bk = min((0.0 if holder[b] is None else done[lastuse[holder[b]]], b) for b in range(8)
+                         if holder[b] is None or done[lastuse[holder[b]]] is not None)
+            t = max(t, tb + LAT)
+            if holder[bk] is not None:
+                deps[i].add(lastuse[holder[bk]])
+            holder[bk] = opens[i]
+            bank_of[opens[i]] = bk
+        start[i] = max(t, free[e])
+        free[e] = start[i] + op["alts"][e][0]
+        done[i] = free[e] + op["lat"]
+    return order, eng, bank_of, deps, start, done
+
+
+DIGITS = "0123456789abcdefghijklmnopqrstuvwxyzABCDEFGHIJKLMNOPQRSTUVWXYZ"
+
+
+def planned(ops, deps):
+    v = [DIGITS.index(PLAN[k]) * 62 + DIGITS.index(PLAN[k + 1]) for k in range(0, len(PLAN), 2)]
+    order = [x >> 1 for x in v]
+    if sorted(order) != list(range(len(ops))):
+        raise ValueError("PLAN does not fit the calls")
+    eng = [None] * len(ops)
+    seen = set()
+    for x in v:
+        alts = sorted(ops[x >> 1]["alts"])
+        eng[x >> 1] = None if not alts else alts[0] if x & 1 else alts[-1]
+        if not deps[x >> 1] <= seen:
+            raise ValueError("PLAN breaks a hazard")
+        seen.add(x >> 1)
+    return place(ops, deps, order, eng)
+
+
+def split_engines(core, cores, topo):
+    peers = [x for x in cores if x != core]
+    for x in peers:
+        if not topo.may_write(core, x):
+            raise ValueError("no way to a rank")
+    allowed = {x: topo.engines(core, x) for x in peers}
+    few = min(len(v) for v in allowed.values())
+    tight = [x for x in peers if len(allowed[x]) == few]
+    k = 1
+    while 2 * k <= few // len(tight):
+        k *= 2
+    out, used = {}, []
+    for x in tight + [y for y in peers if y not in tight]:
+        left = [e for e in allowed[x] if e not in used]
+        out[x] = left[:k] if x in tight else left[::2][:k]
+        used += out[x]
+    return out
+
+
+def rank_program(g, core, T, topo):
+    me = T.rank_of(core)
+    if me is None:
+        return
+    cores = list(T.cores)
+    ops = build(me)
+    order, eng, bank_of, deps, start, done = planned(ops, hazards(ops))
+    queue = {"V": g.vector, "S": g.scalar, "P": g.tensor, "G": g, "Y": g.sync}
+    mine = split_engines(core, cores, topo)
+    inbound = sum(len(split_engines(x, cores, topo)[core]) for x in cores if x != core)
+
+    def ap(x):
+        if x[0] == "@":
+            return T["pb%d" % bank_of[x[1]]][:, x[2]:x[3]]
+        return T[x[0]][x[1]] if x[1] else T[x[0]][:]
+
+    count = {}
+    mark = {}
+    clock = {}
+    know = {e: {} for e in queue}
+    ndma = [0]
+    for i in order:
+        op, e = ops[i], eng[i]
+        if e is None:
+            count[op["sem"]] = inbound
+            mark[i] = (op["sem"], inbound)
+            clock[i] = {op["sem"]: inbound}
+            continue
+        q, kn = queue[e], know[e]
+        want = {}
+        for j in deps[i]:
+            if ops[j]["kind"] == "r":
+                if "behind" in op:
+                    continue
+                raise ValueError("a source of a remote write is written again")
+            if e == "P" and eng[j] == "P":
+                continue
+            s, v = mark[j]
+            if want.get(s, (0, 0))[0] < v:
+                want[s] = (v, j)
+        for s in sorted(want, key=lambda s: (-done[want[s][1]], s)):
+            v, j = want[s]
+            if kn.get(s, 0) < v:
+                q.wait_ge(T.sem[s], v)
+                for s2, v2 in clock[j].items():
+                    if kn.get(s2, 0) < v2:
+                        kn[s2] = v2
+        f = op["alts"][e][1]
+        if op["kind"] == "c":
+            s = "c" + e
+            count[s] = count.get(s, 0) + 1
+            f(q, ap).then_inc(T.sem[s], 1)
+        elif op["kind"] == "d":
+            s = "d%d" % ndma[0]
+            ndma[0] += 1
+            count[s] = 0
+            for ins in f(q, ap):
+                ins.then_inc(T.sem[s], 16)
+                count[s] += 16
+        else:
+            s = "sent"
+            trs = []
+            for d in sorted(f):
+                rid, pid = topo.addr(cores[d])[:2]
+                es = mine[cores[d]]
+                k = len(es) // len(f[d])
+                for n, (src, dst) in enumerate(f[d]):
+                    mask = sum(1 << x for x in es[n * k:n * k + k])
+                    trs.append(RemoteDMATransfer(dst_ids=[DstId(rid=rid, pnc=pid)], dma_engine_mask=mask, remote_sem=T.sem[op["sem"]], src=ap(src), dst=ap(dst)))
+                    count[s] = count.get(s, 0) + k
+            q.remote_dma_fused(trs, local_sem=T.sem[s])
+        mark[i] = (s, count[s])
+        clock[i] = dict(kn)
+        clock[i][s] = count[s]
+    for s in sorted(count):
+        g.wait_ge(T.sem[s], count[s])

@@ -5,30 +5,30 @@ RO = 3
 BF, F32, I32, U16 = "bfloat16", "float32", "int32", "uint16"
 SCRATCH = {}
 for _where, _dt, _list in (
-    ("dram", I32, (("ocl", 512, 128), ("dcl", 4, 128, 128))),
-    ("dram", BF, (("ofx", 1024, 128), ("ohv", 512, 512), ("dhv", 4, 128, 512), ("dth", 8, 128, 64))),
-    ("sbuf", I32, (("hs", 512), ("hq", 512), ("hr", 512), ("ths", 64), ("clc", 4, 128), ("s1", 512), ("s2", 256), ("cls", 512), ("clw", 1024),
-                   ("z1", 512), ("z2", 512), ("Km", 128), ("Ko", 128), ("x1", 1024), ("yi", 1024), ("pi", 16))),
-    ("sbuf", U16, (("hbo", 512), ("posT", 512), ("clu", 512), ("clx", 512), ("ob", 128))),
-    ("sbuf", F32, (("thc", 512), ("tio", 4096), ("z3", 512), ("K", 512), ("M1", 256), ("Sm", 1024), ("pf", 24), ("row", 192), ("io3", 128),
-                   ("posc", 256), ("pos0", 256))),
-    ("sbuf", BF, (("hu", 4, 256), ("hb", 1024), ("thh", 64), ("thl", 64), ("thw", 4096), ("one", 1024), ("xw", 8192), ("hh", 2048), ("h1p", 2048),
-                  ("D", 8192), ("A", 8192), ("A2", 8192), ("Db", 2048), ("vw", 8192), ("vT", 8192), ("best", 512), ("dd", 512), ("live", 16, 32),
-                  ("L", 512), ("d8", 512), ("W8", 512), ("xc", 1024), ("xm", 1024), ("OT", 8, 192), ("OL", 8, 192), ("KEYW", 144), ("ONEW", 144),
-                  ("INVW", 288), ("THW", 288), ("SUMW", 144), ("SELW", 144), ("RW", 768), ("ID", 1024), ("BC", 2048), ("NW", 128), ("XB", 1024),
-                  ("WX", 1024), ("Z", 128))),
+    ("dram", I32, (("ocl", 8, 128, 64), ("dcl", 8, 128, 64))),
+    ("dram", BF, (("ofx", 8, 128, 128), ("ohv", 8, 128, 256), ("dhv", 8, 128, 256), ("dth", 8, 128, 64), ("xd0", 16, 4, 1024), ("xd1", 16, 4, 1024),
+                  ("lx", 8, 128, 128), ("ll", 8, 128, 64))),
+    ("sbuf", I32, (("hs", 512), ("hq", 512), ("hr", 512), ("ths", 64), ("clc", 8, 64), ("s1", 512), ("s2", 256), ("cls", 512), ("clw", 1024),
+                   ("U", 1024), ("yi", 1024), ("pi", 16))),
+    ("sbuf", U16, (("hbo", 512), ("posT", 512), ("clu", 512), ("ob", 128))),
+    ("sbuf", F32, (("tio", 4096), ("K", 256), ("M1", 256), ("Km", 128), ("pf", 32), ("row", 192), ("io3", 128), ("io2", 128))),
+    ("sbuf", BF, (("hu", 4, 256), ("hb", 1024), ("thh", 64), ("thl", 64), ("thw", 4096), ("one", 1024), ("big", 1024), ("xw", 8192), ("hh", 2048),
+                  ("D", 8192), ("A", 8192), ("A2", 8192), ("Db", 2048), ("vw", 8192), ("vT", 8192), ("bt", 1056), ("lv", 18, 64),
+                  ("tch", 512), ("tcl", 512), ("L", 512), ("d8", 512), ("qn", 1024), ("dx", 1024), ("CST", 256), ("XT", 256), ("xc", 1024),
+                  ("OX", 8, 128), ("OY", 8, 64), ("GW", 240), ("ONEW", 144), ("INVW", 288), ("THW", 288), ("SUMW", 144), ("SELW", 144),
+                  ("RW", 1152), ("ID", 1408), ("BC", 2048), ("NW", 128), ("XB", 512), ("WX", 1024), ("CK", 256), ("XI", 64))),
     ("psum", F32, tuple(("pb%d" % _b, 512) for _b in range(8))),
 ):
     for _x in _list:
         SCRATCH[_x[0]] = (_where, ([] if _where == "dram" else [128]) + list(_x[1:]), _dt)
-SEMAPHORES = ["cV", "cS", "cP", "cG", "sent", "acl", "ahl", "ath", "afx", "ahv", "ao0", "ao1"] + ["d%d" % _k for _k in range(40)]
+SEMAPHORES = (["cV", "cS", "cP", "cG", "sent", "acl0", "afx0", "ahv0", "ath", "acl1", "afx1", "ahl", "ahv1", "ao0", "ao1", "ay0", "ay1"]
+              + ["d%d" % _k for _k in range(60)])
 
-EST = {"CY": 1.04, "GA": 1.56, "PE": 0.52, "FIX": 60.0, "LAT": 90.0, "TT": 2.0, "DQ": 70.0, "MASK": (0, 1, 0, 1, 0, 1, 0, 1),
-       "LEAD": 10000.0, "Q": 50.0, "CONST": 1e6, "WDMA": 0, "WLAT": 7000.0, "NH": 2, "VB": 0.0}
-PLAN = "1e0k1q1A1m1U1o0200080c040g0a0e061i1g1s1y1G1w1K2Q1Q0w0q0s0o0m1k0u0U140y0A0C0Q0W0S2O12104g4s4o0i1S1C221E20261Y0E1W242y2c2e0I2i280G4k4cgM161u2F182g2I2n2N4j4w4A4v4r4n4E0K4z4f4H3i3g2a2A2D4DgIh21ah5gAgY4KgP4N0M0Y2W2U3q1I3m2s3o3k3s1O3ugQ3630320O3w4W3y4OgU4Q2kgD4S3A503Z4Y1c4Ugj5854gWh02o3C52342YgE5agqfW5cgn563E5eh83G5g3K5i1M5k5m2w5ogT3V2rgLgG3O3chg3X5t3I423M445G415r465I5whshk5A645C485u4ahi5E66gl60623Qhw5O5Q6c5K6ghmhofY5y5Mg45Sgs68hy6i6ehq6shA6o3S2u6ahuhbhC6E6k5Ug8396q6GhE6m5W5Y6M6Q6w2ShG2LhIhK6ugphM6y6OhR2GhO3e3bg0hSgc6ShWguhc6Ahf6CiE6I6K727O746X6Vgwis7WiG7NgzhYi4icieiAg2i66Yg670ioiC4I7V7Q7Si076787a7c80gai27ehU7giu7Y7i827k7m7o7qi884867s88iaiqig8aii7A8eiwik8ch68g8iimiy7w7D7IiU7LiQ7E7HiW8kiM8w8o8q8ziS7zj28sj4iIiK8AjagejeiOjcj6iY8v8Dgg8E8Mjgj8j0kckbjkki7u8Ikl8Gjjjrjtkgkekokm8Ujmkq8O8K8Q8Sksjojukujykw8WkCjAky8Y90kAkEjCkGkIjE9294jwjKjGjIjM96jO98jQ9akUkMkQkY8m9e9i9mkX9ol09gkT9dk2jYk6k1k99q9s9ukO9SjUjW9Ga49Ck59kl2la9wa09I9y9Oa69Ea2l49U9Aa89Kaa9Ml6le9QaEaGlc9WacaoagaAl8liak9YawlkasaiaqlgaylmaCamaeauaKlobAaJbDbLaRaTaOaMbEbGlqbIlslulwlElylBlDbMbOlGbQlIlKbSaUbUbWaYlMmclOb0kKb2moaWjSb4mgb6bYbac2memim4lSb8c0bcc4bem6mqlUlQmsm0c6bgc8cccgbkmulWbsbvm2lYbomkmwmmmycockcfbrcnm8mAbwmQcrbzcibmmamCmSmUmMmImEn2mYmWcscwmKmOcumGn4n0n6nYcIcAn9cEo1nhnfcyo9nco2nanicKnmo6nooanqoenscCcMognycGcOoinAokcQnknuo4oqcSnwocomcUcWd4cYosd1oonCnEdadCoud6owoynUnMnQoInSnOoMd3dGoEnIoLdqoAdcnWdEoHoDdIoOnKd8dSdUdOdQdidup2caoQoUdkdedWdKdwdgdsdmdydYdooSp6esdAe8e4e0p4oWoYdMbie2eaeup0eoegekp8ece6emeepaeqeiewezfdeFeHpceCeAfapefjfefgeKeIpgpipspkfkpmpopAprnGpwpyfofmfqeMq0qcq4fsq2qeq6fupuqgeOqipOpSpQpUpCfCq8eQpGqafEpEpIpWqEpKpYqAqkqweYqmfwqGpMqIqMqyqOqsqCqKqQqoeSqqf2fyquqSqUf4fGf0eUqXryrBr5r3r0qYrGfIrJeWf6fArCr6rKrafKrircr8rOrerQrgfMrSf8rkrqrErUrmrMs4ros0rWs2rsrus6rYs8rwsafOfSscsgfQsefUsi"
-ARRIVE = {"acl": 6000.0, "ahl": 12000.0, "ath": 6000.0, "afx": 8000.0, "ahv": 10000.0}
+EST = {"CY": 0.86, "GA": 1.56, "PE": 0.43, "FIX": 60.0, "LAT": 90.0, "TT": 2.0, "DQ": 70.0, "DFIX": 2000.0, "ROW": 50.0, "RATE": 14.0,
+       "RELU": (0, 0, 0, 0), "NE": 1, "WIN0": "PD", "WIN": "PP", "PARTS": ((0, 2), (2, 4)), "LEAD": 0.0, "LATE": 0.0}
+PLAN = "0q1K1Y460a28000602041M1W2y080o0m2G2a3k2Q1U2c0F0c3I3x202o2q3z0y0I2K223B0O0s2I0K0M0H1m0Q2s0S1k4S5c2M4W2S30343r54242e1i261o0u2A2u0i2C0U583W1q0e1S0B320D4V2O1O3U3Y1Q40502W0W0w0Y3d5b5f3O2g0g2Y2U1u12573p3F1w1C0k2E103e14165o4C4E4G4w4I4y424K4M4O4A3m3v5k5g5j5n534Z181a4Q36394a2i6c4c4u666o686a6e6q1g1c6i5KgSgU3G1e1G1s1y6khc6g6m4gh04q6sgM4i6vgY4kh2454oh46w6y6AgW6C5tgO1I5r6E6GhygQ3a5M6I6N5y5S5O5A606P7i7c6W4s5x5vh8hf5QhA5U5WhC1A1E5C5E5H7E6Q7k7G7e7yh65Y627A6K5Ihh7C7I7K7U7g7m4m7Qhl3ghG80ha646S82i0hUi67SichEhIhm6Y7o7u6U707M7Wi2727Y7884hWhY86747a88768aho8c8ehjhqhs7O7w7q7s8gi8i4ia8iieigiiikhvhwim2wioiq3Q8k8p8n8V8q918sisiu8u3s8T8W8w8Ziw8y8I928MhO94968A8EiD8LiBj68H8D8P2kjI989a9o9k9r9g9j9niyhK9c9ej03KjsjmjOjuiKj2j4jojqj8iE9u9wjwjajyjc9M9AjejAhMjgjK9GjCiGiM9CiIjiiOiQjEjMiWiSiYiUjQjS4fjUjWk0k2jG9O9t9yhQjkjYhS9E9I9K9Q9Tk59Uk69W9Ya0kGa2k8kMkbkdkekga4a6kikkkmkJkKkPkQkSkUkWkYkAkskwa8abad3MkubolckokqkDl0kzlfl33Cl4l8lal7lilAaAaCbibk8RakaGaIaEbqlulobmaeaKamagaWaYaMbsbub2aib4aoaqbAaSaObCaUbwawaylklwb0b6b8bybeasaubabcbglmaQlqlslylClhlElHlIbFcjlKcgcpbLbNlMcmlO3SlQbGckcqcslSbIbOlUlZm1cucwcycAcIcE2mbQcDcHmKcMcPbSbUbWc6cacKcdc2bYc1kEmMncc8nemomun6mwmqn8c4mQmSm2m4m8msmymAmOnamUnglWm6d4cSdacYcUmWn2nimanonqmYn0mCmEn4nkd0mcmemgminmmGmImkmmd6cWd2d8dcdedhdioanvntdkdmnAdonwdqdso4dunznCnEnGo7o8odoenInKnYnMogoioknUnQdzdBdwdIomoooAo1nXnPnSowor3iosovoCdKeMekemeOdCoyoMeqeGdEeIdGdMoOdOeKeQeSe4eooGoIoKdQoQoSeUoUcfoWdYoYp0p2eYeseudSeWe0p4p6dUp8papcpee6e2e8pgeweCeaegecpkpipneypoquqwpMdWeipSpUeEeAf0pOeeqApqpsq8f4faqaqCg8qeqypwpyqgpuqEqGqcpAqiqMqkfc48pQqOqIqmqopWf3f8qKpYcQpCq4qqpEq6pGo2qspIf6fDfFfGq0pKfegbfgfKfifSfMgcfIq2rtrqrufofkqTqQfUfWrZrwfsryrKqZfqfYfufmoErGqUfOrWg0g2qWr1rIfwfyr2rMr7fQgEgGg4fAr4rcrgrOrQr8ghrerirAg6s0rSrarkrCrEgissrmrorUgegkgIgAs5s6gms8sogqgosascgss2sesggKgugwgysiskgCsmsqsuswsy"
+ARRIVE = {"acl0": 5500.0, "afx0": 7500.0, "ahv0": 8500.0, "ath": 9500.0, "acl1": 10500.0, "afx1": 12000.0, "ahl": 13500.0, "ahv1": 15000.0}
 EXT = ("fx", "hv", "hl", "cl", "th", "yx", "yl")
-DEAD = float(1 << 24)
 
 
 def r(name, *idx):
@@ -67,8 +67,8 @@ def build(me):
         nvb[0] += 1
         return nvb[0]
 
-    def add(alts, R, W, kind="c", lat=0.0, sem=None, at=0.0, prio=0.0):
-        ops.append(dict(alts=alts, R=R, W=W, kind=kind, lat=lat, sem=sem, at=at, prio=prio + lead[0]))
+    def add(alts, R, W, kind="c", lat=0.0, sem=None, at=0.0, prio=0.0, ring=0.0):
+        ops.append(dict(alts=alts, R=R, W=W, kind=kind, lat=lat, sem=sem, at=at, prio=prio + lead[0], ring=ring))
 
     def width(x):
         if x[0] == "@":
@@ -93,12 +93,18 @@ def build(me):
     def val(ap, s):
         return ap(s) if isinstance(s, tuple) else s
 
-    def ts(out, in0, s1, s2, op0, op1=None):
+    def tsf(out, in0, s1, s2, op0, op1):
         def f(q, ap):
             if op1 is None:
                 return q.tensor_scalar(ap(out), ap(in0), val(ap, s1), None, op0)
             return q.tensor_scalar(ap(out), ap(in0), val(ap, s1), val(ap, s2), op0, op1)
-        add({"V": (vc(out, in0), f)}, [in0] + [s for s in (s1, s2) if isinstance(s, tuple)], [out])
+        return (vc(out, in0), f)
+
+    def actf(out, in_, fn, bias, scale):
+        return (vcost(width(in_), 1.0), lambda q, ap: q.activation(ap(out), ap(in_), fn, bias=bias, scale=val(ap, scale)))
+
+    def ts(out, in0, s1, s2, op0, op1=None):
+        add({"V": tsf(out, in0, s1, s2, op0, op1)}, [in0] + [s for s in (s1, s2) if isinstance(s, tuple)], [out])
 
     def tt(out, in0, in1, op):
         per = 1.0 if "@" in (in0[0], in1[0]) else EST["TT"]
@@ -111,15 +117,13 @@ def build(me):
         add({"V": (vc(out, out), lambda q, ap: q.memset(ap(out), v))}, [], [out])
 
     def act(out, in_, fn, bias=0.0, scale=1.0):
-        add({"S": (vcost(width(in_), 1.0), lambda q, ap: q.activation(ap(out), ap(in_), fn, bias=bias, scale=scale))}, [in_], [out])
+        add({"S": actf(out, in_, fn, bias, scale)}, [in_], [out])
 
-    def plus(out, in_, bias):
-        add({"V": (vc(out, in_), lambda q, ap: q.tensor_scalar(ap(out), ap(in_), bias, None, ALU.add)),
-             "S": (vcost(width(in_), 1.0), lambda q, ap: q.activation(ap(out), ap(in_), ACT.Identity, bias=bias))}, [in_], [out])
+    def move(out, in_):
+        add({"V": (vc(out, in_), lambda q, ap: q.tensor_copy(ap(out), ap(in_))), "S": actf(out, in_, ACT.Identity, 0.0, 1.0)}, [in_], [out])
 
     def times(out, in_, s):
-        add({"V": (vc(out, in_), lambda q, ap: q.tensor_scalar(ap(out), ap(in_), val(ap, s), None, ALU.mult)),
-             "S": (vcost(width(in_), 1.0), lambda q, ap: q.activation(ap(out), ap(in_), ACT.Identity, scale=val(ap, s)))},
+        add({"V": tsf(out, in_, s, None, ALU.mult, None), "S": actf(out, in_, ACT.Identity, 0.0, s)},
             [in_] + ([s] if isinstance(s, tuple) else []), [out])
 
     def gather(out, win, off):
@@ -142,85 +146,111 @@ def build(me):
             R += [t for t in (l, x) if t not in R]
         add({"P": (30.0 + sum(max(64, width(x)) for (o, l, x, a, b) in lst) * PEC, f)}, R, [lst[0][0]])
 
-    def iota(out, pat, base, mult):
+    def iota(out, pat, base, mult, behind=False):
         if SCRATCH[out[0]][2] == I32:
             f = lambda q, ap: q.iota(ap(out), pat, base, mult)
         else:
             f = lambda q, ap: q.iota(ap(out), pat, base, mult, allow_small_or_imprecise_dtypes=True)
-        add({"G": (160.0 + 2 * width(out) * CY, f)}, [], [out])
+        add({"G": (140.0 + 2 * width(out) * CY, f)}, [], [out])
+        if behind:
+            ops[-1]["behind"] = "ahv1"
 
-    def select(out, pat, base):
+    def select(out, src, pat, base, behind=True):
         n = width(out)
-        add({"G": (200.0 + 2 * n * CY, lambda q, ap: q.affine_select(ap(out), ap(c("one", 0, n)), pat, ALU.is_equal, 0.0, base, -1))}, [c("one", 0, n)], [out])
-        ops[-1]["behind"] = "ahv"
+        add({"G": (180.0 + 2 * n * CY, lambda q, ap: q.affine_select(ap(out), ap(c(src, 0, n)), pat, ALU.is_equal, 0.0, base, -1))}, [c(src, 0, n)], [out])
+        if behind:
+            ops[-1]["behind"] = "ahv1"
 
-    def dma(pairs, lat=2200.0, engs="YS", prio=0.0):
+    def dma(pairs, rows, size, engs="YS", prio=0.0):
         f = lambda q, ap: [q.dma_start(ap(o), ap(i)) for (o, i) in pairs]
-        add({e: (EST["DQ"] * len(pairs), f) for e in engs}, [i for (o, i) in pairs], [o for (o, i) in pairs], kind="d", lat=lat, prio=prio)
+        add({e: (EST["DQ"] * len(pairs), f) for e in engs}, [i for (o, i) in pairs], [o for (o, i) in pairs], kind="d", lat=EST["DFIX"], prio=prio,
+            ring=rows / 16.0 * (EST["ROW"] + size / EST["RATE"]))
 
-    def send(sem, pieces):
+    sent = []
+
+    def send(sem, pieces, in_line=True):
         add({"G": (500.0, pieces)}, [s for d in pieces for (s, t) in pieces[d]], [], kind="r", sem=sem, prio=1e6)
+        if sent and in_line:
+            ops[-1]["behind"] = sent[-1]
+        sent.append(sem)
 
-    def arrive(sem, W, at):
-        add({}, [], W, kind="a", sem=sem, at=at)
+    def arrive(sem, W):
+        add({}, [], W, kind="a", sem=sem, at=ARRIVE.get(sem, -1.0))
 
     others = [d for d in range(4) if d != me]
-    runs = [(a, b) for (a, b) in ((0, me), (me + 1, 4)) if b > a]
     S = slice
     ALL = slice(None)
+    SHR, AND, MUL, ADD, EQ, MIN = ALU.arith_shift_right, ALU.bitwise_and, ALU.mult, ALU.add, ALU.is_equal, ALU.min
+    rows = lambda d, f: S(32 * d + 16 * f, 32 * d + 16 * f + 16)
 
-    dma([(r("ocl", S(128 * a, 128 * b)), r("cl", S(32 * a, 32 * b))) for (a, b) in runs], engs="Y", prio=9e6)
-    dma([(r("ths"), r("th"))], engs="S", prio=9e6)
+    def loads(f, pr):
+        box = lambda t, d: r("o" + t, 4 * f + d) if d != me else r("d" + t, 4 * f + d)
+        dma([(box("cl", d), r("cl", rows(d, f))) for d in others], 48, 2048, engs="Y", prio=pr + 9e5)
+        dma([(r("ofx", 4 * f + d), r("fx", rows(d, f))) for d in others], 48, 2048, engs="S", prio=pr + 9e5)
+        hv = lambda d, m: (box("hv", d)[0], (4 * f + d, S(64 * m, 64 * m + 64))) + box("hv", d)[2:]
+        dma([(hv(d, m), r("hv", rows(d, f), S(1024 * m, 1024 * m + 1024))) for d in others for m in range(2)], 96, 2048, engs="Y", prio=pr + 8e5)
+        dma([(box("cl", me), r("cl", rows(me, f)))] + [(hv(me, m), r("hv", rows(me, f), S(1024 * m, 1024 * m + 1024))) for m in range(2)],
+            48, 2048, engs="Y", prio=pr + 7e5)
+        dma([(c("xc", 512 * f + 128 * me, 128), r("fx", rows(me, f)))], 128, 256, engs="S", prio=pr + 7e5)
+
+    def sends(f):
+        send("acl%d" % f, {d: [(r("ocl", 4 * f + d), r("dcl", 4 * f + me))] for d in others})
+        send("afx%d" % f, {d: [(r("ofx", 4 * f + d), c("xc", 512 * f + 128 * me, 128))] for d in others})
+
+    def sendhv(f):
+        send("ahv%d" % f, {d: [(r("ohv", 4 * f + d), r("dhv", 4 * f + me))] for d in others})
+
+    loads(0, 9e6)
+    dma([(r("ths"), r("th"))], 128, 256, engs="S", prio=9.75e6)
+    loads(1, 7e6)
     for half in range(2):
         dma([(r("hs", S(32 * q, 32 * q + 32), S(128 * d, 128 * d + 128)), r("hl", S(32 * d, 32 * d + 32), S(128 * q, 128 * q + 128)))
-             for q in (2 * half, 2 * half + 1) for d in range(4)], engs="YS"[half], prio=8e6)
-    dma([(r("dcl", me), r("cl", S(32 * me, 32 * me + 32)))], engs="Y", prio=7e6)
-    dma([(r("ofx", S(256 * a, 256 * b)), r("fx", S(32 * a, 32 * b))) for (a, b) in runs], lat=3000.0, engs="S", prio=6e6)
-    dma([(r("ohv", S(128 * a, 128 * b)), r("hv", S(32 * a, 32 * b))) for (a, b) in runs], lat=4000.0, engs="Y", prio=5e6)
-    dma([(c("xc", 512 * f + 128 * me, 128), r("fx", S(32 * me + 16 * f, 32 * me + 16 * f + 16))) for f in range(2)], engs="S", prio=4e6)
-    dma([(r("dhv", me), r("hv", S(32 * me, 32 * me + 32)))], engs="Y", prio=4e6)
+             for q in (2 * half, 2 * half + 1) for d in range(4)], 256, 512, engs="YS"[half], prio=8e6)
     lead[0] = 1e6
-    fill(r("clw"), 0)
     fill(r("one"), 1.0)
+    fill(r("clw"), 0)
+    fill(r("big"), 32768.0)
+    fill(r("lv"), 0.0)
+    fill(r("bt"), 0.0)
     for k in range(4):
-        act(c("thw", 1024 * k, 1024), r("one"), ACT.Copy)
-    send("acl", {d: [(r("ocl", S(128 * d, 128 * d + 128)), r("dcl", me))] for d in others})
+        move(c("thw", 1024 * k, 1024), r("one"))
+    sends(0)
+    sendhv(0)
     cp(r("thh"), r("ths"))
     tt(r("thl"), r("ths"), r("thh"), ALU.subtract)
     send("ath", {d: [(r("thh"), r("dth", me)), (r("thl"), r("dth", 4 + me))] for d in others})
-    dma([(r("dth", me), r("thh")), (r("dth", 4 + me), r("thl"))], engs="Y")
-    ts(r("hq"), r("hs"), 15, None, ALU.bitwise_and)
-    ts(r("hr"), r("hs"), 4, None, ALU.arith_shift_right)
+    dma([(r("dth", me), r("thh")), (r("dth", 4 + me), r("thl"))], 256, 128, engs="Y")
+    sends(1)
+    ts(r("hq"), r("hs"), 15, None, AND)
+    ts(r("hr"), r("hs"), 4, None, SHR)
     cp(r("hu", ALL, ALL, S(0, 128)), r("hq"))
     cp(r("hu", ALL, ALL, S(128, 256)), r("hr"))
     send("ahl", {d: [(r("hu", ALL, d), c("hb", 256 * me, 256))] for d in others})
+    sendhv(1)
     cp(c("hb", 256 * me, 256), r("hu", ALL, me))
-    send("afx", {d: [(r("ofx", S(256 * d + 128 * f, 256 * d + 128 * f + 128)), c("xc", 512 * f + 128 * me, 128)) for f in range(2)] for d in others})
-    send("ahv", {d: [(r("ohv", S(128 * d, 128 * d + 128)), r("dhv", me))] for d in others})
     lead[0] = 0.0
-    arrive("acl", [r("dcl", d) for d in others], ARRIVE["acl"])
-    arrive("ath", [r("dth", k + d) for d in others for k in (0, 4)], ARRIVE["ath"])
-    arrive("ahl", [c("hb", 256 * d, 256) for d in others], ARRIVE["ahl"])
-    arrive("afx", [c("xc", 512 * f + 128 * d, 128) for d in others for f in range(2)], ARRIVE["afx"])
-    arrive("ahv", [r("dhv", d) for d in others], ARRIVE["ahv"])
-    dma([(r("clc", S(64 * m, 64 * m + 64), ALL, S(64 * f, 64 * f + 64)), r("dcl", ALL, S(64 * f, 64 * f + 64), S(64 * m, 64 * m + 64)))
-         for f in range(2) for m in range(2)], engs="S", prio=3e6)
-    dma([(r("clw", S(64 * m + 4 * f + cc, 64 * m + 64, 16)), r("dcl", ALL, S(64 * f + cc, 64 * f + 64, 4), S(64 * m, 64 * m + 64)))
-         for f in range(2) for m in range(2) for cc in range(4)], engs="Y", prio=3e6)
-    dma([(r("thw", S(16 * gg + 2 * f, 16 * gg + 2 * f + 2)), r("dth", ALL, S(32 * me + 16 * f, 32 * me + 16 * f + 16)))
-         for f in range(2) for gg in range(8)], engs="S", prio=2e6)
+    arrive("ath", [r("dth", k + d) for d in others for k in (0, 4)])
+    arrive("ahl", [c("hb", 256 * d, 256) for d in others])
     for f in range(2):
-        dma([(r("hh", S(64 * m, 64 * m + 64), S(1024 * f + 512 * hf, 1024 * f + 512 * hf + 512)), r("dhv", ALL, S(64 * f + 2 * m + hf, 64 * f + 64, 4)))
-             for m in range(2) for hf in range(2)], engs="Y", prio=1e6 - f)
+        arrive("acl%d" % f, [r("dcl", 4 * f + d) for d in others])
+        arrive("afx%d" % f, [c("xc", 512 * f + 128 * d, 128) for d in others])
+        arrive("ahv%d" % f, [r("dhv", 4 * f + d) for d in others])
+        four = S(4 * f, 4 * f + 4)
+        dma([(r("clc", S(64 * m, 64 * m + 64), four), r("dcl", four, S(m, 128, 2))) for m in range(2)], 512, 256, engs="S", prio=3e6 - 2e6 * f)
+        dma([(r("hh", S(64 * m, 64 * m + 64), S(1024 * f, 1024 * f + 1024)), r("dhv", four, S(64 * m, 64 * m + 64))) for m in range(2)],
+            128, 2048, engs="Y", prio=2.5e6 - 2e6 * f)
+        dma([(r("thw", S(16 * gg + 2 * f, 16 * gg + 2 * f + 2)), r("dth", ALL, rows(me, f))) for gg in range(8)], 64, 2048, engs="Y", prio=2e6 - 1e6 * f)
+        dma([(r("clw", S(64 * m + 4 * f + cc, 64 * m + 64, 16)), r("dcl", four, S(2 * cc + m, 128, 8))) for m in range(2) for cc in range(4)],
+            512, 256, engs="Y", prio=1.5e6 - 1e6 * f)
 
-    lead[0] = EST["CONST"]
+    lead[0] = 1e6
     iota(c("pi", 0, 1), [[0, 1]], 0, 1)
     iota(r("row"), [[1, 192]], 0, 0)
-    iota(r("pos0"), [[1024, 4], [16, 64]], 0, 0)
     iota(r("io3"), [[0, 8], [1, 16]], 0, 0)
+    iota(r("io2"), [[0, 16], [2, 8]], 0, 0)
+    iota(r("CK"), [[1, 4], [0, 64]], 0, 0)
     pi = lambda k: c("pi", k, 1)
     pf = lambda k: c("pf", k, 1)
-    SHR, AND, MUL, ADD, EQ = ALU.arith_shift_right, ALU.bitwise_and, ALU.mult, ALU.add, ALU.is_equal
     ts(pi(1), pi(0), 4, None, SHR)
     ts(pi(2), pi(0), 15, None, AND)
     ts(pi(3), pi(0), 4, 1, SHR, AND)
@@ -238,197 +268,235 @@ def build(me):
     ts(pf(6), pi(2), 0.0, None, EQ)
     ts(pf(7), pi(2), 64.0, None, ADD)
     ts(pf(8), pi(4), 16.0, pf(7), MUL, ADD)
+    ts(pf(9), pi(1), 8.0, 7.0, MUL, ADD)
+    ts(pf(10), pi(2), 64.0, None, MUL)
+    ts(pf(11), pi(2), -1.0, None, ADD)
     for f in range(2):
-        ts(pf(9 + 2 * f), pi(3), float(f), 64.0, EQ, MUL)
-        ts(pf(10 + 2 * f), pi(3), float(f), None, EQ)
-        ts(pf(13 + f), pi(7), float(f), 1024.0, EQ, MUL)
-        ts(pf(15 + f), pi(8), float(f), None, EQ)
-    for k in range(4):
-        ts(c("RW", 192 * k, 192), r("row"), pf(8), pf(9 + k), EQ, MUL)
+        for k, wgt in enumerate((64.0, 1.0, 16.0)):
+            ts(pf(12 + 3 * f + k), pi(3), float(f), wgt, EQ, MUL)
+        ts(pf(18 + f), pi(7), float(f), 1024.0, EQ, MUL)
+        ts(pf(20 + f), pi(8), float(f), None, EQ)
+    for k in range(6):
+        ts(c("RW", 192 * k, 192), r("row"), pf(8), pf(12 + k), EQ, MUL)
     ts(r("ONEW"), c("row", 0, 144), pf(1), None, EQ)
-    times(r("KEYW"), r("ONEW"), 4096.0)
+    for k, wgt in enumerate((4.0, 8.0, -4.0)):
+        if k == 0 or any(EST["RELU"]):
+            ts(c("GW", 80 * k, 72), c("row", 0, 72), pf(9), wgt, EQ, MUL)
     for f in range(2):
-        times(c("INVW", 144 * f, 144), r("ONEW"), pf(13 + f))
-        times(c("THW", 144 * f, 144), r("ONEW"), pf(15 + f))
-    ts(r("SUMW"), c("row", 0, 144), pf(3), None, EQ)
+        times(c("INVW", 144 * f, 144), r("ONEW"), pf(18 + f))
+        times(c("THW", 144 * f, 144), r("ONEW"), pf(20 + f))
+    ts(r("SUMW"), c("row", 0, 144), pf(3), -0.125, EQ, MUL)
     ts(r("SELW"), c("row", 0, 144), pf(5), pf(6), EQ, MUL)
     ts(c("ID", 0, 128), c("row", 0, 128), pf(0), None, EQ)
-    for k, wgt in enumerate((-1.0, -DEAD, 8192.0, -32768.0, 1.0 / 512.0, 8.0, DEAD)):
-        times(c("ID", 128 * k + 128, 128), c("ID", 0, 128), wgt)
-    IDN, NEG, PEN, BST, DED, SML, ID8, ALLD = [c("ID", 128 * k, 128) for k in range(8)]
-    if not EST["WDMA"]:
-        select(r("WX"), [[1, 8], [0, 8], [8, 16]], 0)
-    ts(r("posc"), r("pos0"), pf(2), None, ADD)
+    wts = (1.0, -1.0, -float(1 << 20), 8192.0, 32768.0, 8.0, 1024.0, 2048.0, 3072.0, 128.0, -4096.0)
+    for k in range(1, 11):
+        times(c("ID", 128 * k, 128), c("ID", 0, 128), wts[k])
+    IDN, NEG, PEN, BST, LVI, ID8, K1, K2, K3, KD, KQ = [c("ID", 128 * k, 128) for k in range(11)]
+    cp(r("XI"), c("row", 0, 64))
+    select(r("WX"), "one", [[1, 8], [0, 8], [8, 16]], 0, False)
     ts(r("NW"), r("io3"), pf(2), None, EQ)
-    lead[0] = 0.0
-    for k in range(4):
-        iota(c("tio", 1024 * k, 1024), [[1, 1024]], 1024 * k, 0)
-        ops[-1]["behind"] = "ahv"
+    for w in range(2):
+        ts(c("XB", 128 * w, 128), r("io2"), pf((2, 11)[w]), -4096.0, EQ, MUL)
+        ts(c("XB", 256 + 128 * w, 128), r("io2"), pf((2, 11)[w]), 1024.0, EQ, MUL)
+    ts(pf(22), pi(0), 0.0, float(1 << 19), EQ, MUL)
+    ts(pf(23), pi(0), 1.0, -0.4375, EQ, MUL)
+    tt(pf(22), pf(22), pf(23), ADD)
     for k in range(2):
-        select(c("BC", 1024 * k, 1024), [[1, 8], [16, 8], [0, 16]], 8 * k)
-    select(c("XB", 0, 256), [[1, 2], [0, 16], [2, 8]], 0)
-    times(c("XB", 768, 256), c("XB", 0, 256), 0.125)
-    times(c("XB", 256, 256), c("XB", 0, 256), 512.0)
-    times(c("XB", 512, 256), c("XB", 0, 256), -512.0)
-    fill(r("Z"), 0.0)
-    sl = lambda name, top, k: c(name, top - k, 128)
+        ts(pf(23 + k), pi(0), 2.0, 1024.0 - 512.0 * k, EQ, MUL)
+        tt(pf(25 + k), pf(22), pf(23 + k), ADD)
+        times(c("CST", 128 * k, 128), c("one", 0, 128), pf(25 + k))
+        ts(pf(27 + k), pi(0), 2.0, float(k), MUL, ADD)
+        ts(c("XT", 128 * k, 128), r("io3"), pf(27 + k), 1.0 / 32.0, EQ, MUL)
+    lead[0] = 0.0
+    for k in range(2):
+        select(c("BC", 1024 * k, 1024), "big", [[1, 8], [16, 8], [0, 16]], 8 * k)
+    for k in range(4):
+        iota(c("tio", 1024 * k, 1024), [[1, 1024]], 1024 * k, 0, True)
+    sl = lambda name, top, k, n=128: c(name, top - k, n)
 
-    lead[0] = 1e6
-    tt(c("s1", 0, 256), r("clc", ALL, S(0, 2)), r("clc", ALL, S(2, 4)), ALU.min)
-    tt(c("s1", 256, 256), r("clc", ALL, S(0, 2)), r("clc", ALL, S(2, 4)), ALU.max)
-    tt(c("s2", 0, 128), c("s1", 0, 128), c("s1", 128, 128), ALU.max)
-    tt(c("s2", 128, 128), c("s1", 256, 128), c("s1", 384, 128), ALU.min)
-    tt(c("cls", 0, 128), c("s1", 0, 128), c("s1", 128, 128), ALU.min)
-    tt(c("cls", 384, 128), c("s1", 256, 128), c("s1", 384, 128), ALU.max)
-    tt(c("cls", 128, 128), c("s2", 0, 128), c("s2", 128, 128), ALU.min)
-    tt(c("cls", 256, 128), c("s2", 0, 128), c("s2", 128, 128), ALU.max)
-    cp(r("clu"), r("cls"))
-    if EST["WDMA"]:
-        ts(r("z1"), r("cls"), 7, 7, SHR, AND)
-        ts(r("z2"), r("cls"), 10, None, SHR)
-        b = bank()
-        ts(p(b), r("z1"), 384.0, None, MUL)
-        tt(p(b), p(b), r("cls"), ADD)
-        ts(r("z3"), r("z2"), -896.0, None, MUL)
-        tt(r("z1"), p(b), r("z3"), ADD)
-        cp(r("clx"), r("z1"))
-
-    def window(f, src, rs=range(4)):
-        if EST["WDMA"]:
-            dma([(r("xw", S(16 * l, 16 * l + 16), S(4096 * f, 4096 * f + 4096)), c(src, 512 * f, 512)) for l in range(8)], lat=EST["WLAT"], engs="Y")
+    def window(f, a, b, how):
+        if how == "D":
+            xd = "xd%d" % f
+            dma([(r(xd, ALL, rr), c("xc", 512 * f + 128 * rr, 128)) for rr in range(a, b)], 128 * (b - a), 256, engs="Y")
+            dma([(r("xw", S(16 * l, 16 * l + 16), S(4096 * f + 1024 * a, 4096 * f + 1024 * b)), r(xd, ALL, S(a, b))) for l in range(8)],
+                128, 2048 * (b - a), engs="Y")
             return
-        for rr in rs:
+        for rr in range(a, b):
             for up in range(2):
-                b = bank()
-                mm([(p(b, 128 * u, 128), c("WX", 128 * (4 * up + u), 128), c(src, 512 * f + 128 * rr, 128), True, True) for u in range(4)])
-                plus(c("xw", 4096 * f + 1024 * rr + 512 * up, 512), p(b), 0.0)
+                bk = bank()
+                mm([(p(bk, 128 * u, 128), c("WX", 128 * (4 * up + u), 128), c("xc", 512 * f + 128 * rr, 128), True, True) for u in range(4)])
+                move(c("xw", 4096 * f + 1024 * rr + 512 * up, 512), p(bk))
 
     def stream(f):
         F = 4096 * f
         X = 512 * f
         H = 256 * f
-        NH = EST["NH"]
-        RH = 4 // NH
-        lv = lambda cc: r("live", ALL, S(8 * f + 2 * cc, 8 * f + 2 * cc + 2))
+        NE = EST["NE"]
+        lv = lambda cc: r("lv", ALL, 9 * f + 2 * cc + 1)
+        lvp = lambda cc, par: r("lv", ALL, S(9 * f + 2 * cc + 1 - par, 9 * f + 2 * cc + 3 - par))
+        btp = lambda cc, par: c("bt", 528 * f + 128 * cc + 1 - par, 128)
+        half = lambda m, par: c("ID", m[4] + 64 * par, 64)
+        clu = lambda cc: c("clu", H + 64 * cc, 64)
 
-        def base(b, rr, closes):
-            return [(p(b, 64 * rr, 64), c("RW", 192 * (2 * f + t) + 64 - 64 * m, 128), c("hb", 256 * rr + 128 * t + 64 * m, 64),
+        def base(b, rr, ks, closes):
+            return [(p(b, 64 * rr, 64), c("RW", 192 * (3 * f + ks[t]) + 64 - 64 * m, 128), c("hb", 256 * rr + 128 * t + 64 * m, 64),
                      (t, m) == (0, 0), closes and (t, m) == (1, 1)) for t in range(2) for m in range(2)]
+        s1, s2, cls = [lambda k, n=1, t=t, a=a: c(t, a + 64 * k, 64 * n) for (t, a) in (("s1", H), ("s2", 128 * f), ("cls", H))]
+        lo, hi = r("clc", ALL, S(4 * f, 4 * f + 2)), r("clc", ALL, S(4 * f + 2, 4 * f + 4))
+        tt(s1(0, 2), lo, hi, MIN)
+        tt(cls(0), s1(0), s1(1), MIN)
+        cp(clu(0), cls(0))
+        tt(s1(2, 2), lo, hi, ALU.max)
+        tt(cls(3), s1(2), s1(3), ALU.max)
+        cp(clu(3), cls(3))
+        tt(s2(0), s1(0), s1(1), ALU.max)
+        tt(s2(1), s1(2), s1(3), MIN)
+        tt(cls(1), s2(0), s2(1), MIN)
+        tt(cls(2), s2(0), s2(1), ALU.max)
+        cp(c("clu", H + 64, 128), cls(1, 2))
+        window(f, 0, 4, EST["WIN0"][f])
+        ts(c("U", X, 512), c("xc", X, 512), 1536.0, None, ADD)
+        keep = lead[0]
+        lead[0] = keep - EST["LATE"]
+        for cc in range(4):
+            gather(c("A2", F + 1024 * cc, 1024), r("thw"), clu(cc))
         b = bank()
-        mm([x for rr in range(4) for x in base(b, rr, True)])
+        for cc in range(4):
+            mm([(p(b, 64 * cc, 64), sl("THW", 144 * f + 15, s), c("A2", F + 1024 * cc + 64 * s, 64), s == 0, s == 15) for s in range(16)])
+        move(c("tch", H, 256), p(b, 0, 256))
+        tt(c("tcl", H, 256), p(b, 0, 256), c("tch", H, 256), ALU.subtract)
+        b = bank()
+        mm([x for rr in range(4) for x in base(b, rr, (0, 1), True)])
         cp(c("hbo", H, 256), p(b, 0, 256))
         b = bank()
         for rr in range(4):
             gather_op(c("vT", F + 1024 * rr, 1024), r("clw"), c("hbo", H + 64 * rr, 64), c("tio", 1024 * rr, 1024), ALU.is_lt)
-            mm(base(b, rr, False) + [(p(b, 64 * rr, 64), sl("INVW", 144 * f + 15, s), c("vT", F + 1024 * rr + s, 1024 - s, 16), False, s == 15) for s in range(16)])
+            mm(base(b, rr, (1, 2), False) + [(p(b, 64 * rr, 64), sl("INVW", 144 * f + 15, s), c("vT", F + 1024 * rr + s, 1024 - s, 16), False, s == 15) for s in range(16)])
         cp(c("posT", H, 256), p(b, 0, 256))
-        for cc in range(4):
-            gather(c("A2", F + 1024 * cc, 1024), r("thw"), c("clu", 128 * cc + 64 * f, 64))
-        b = bank()
-        for cc in range(4):
-            mm([(p(b, 64 * cc, 64), sl("THW", 144 * f + 15, s), c("A2", F + 1024 * cc + s, 1024 - s, 16), s == 0, s == 15) for s in range(16)])
-        plus(c("thc", H, 256), p(b, 0, 256), 0.0)
-        window(f, "xc")
-        ts(c("x1", X, 512), c("xc", X, 512), 1.0, None, ADD)
-        for hf in range(2):
-            b = bank()
-            mm([(p(b, 64 * s, 64), IDN, c("hh", 1024 * f + 8 * hf + s, 1024 - 8 * hf - s, 16), True, True) for s in range(8)])
-            plus(c("h1p", 1024 * f + 512 * hf, 512), p(b), 1.0)
+        lead[0] = keep
 
         for rnd in range(RO):
             last = rnd == RO - 1
-            for cc in range(4):
+            kb = bank()
+            lst = [(p(kb, 0, 256), IDN, r("CK"), True, False)]
+            if rnd:
+                lst += [(p(kb, 64 * cc, 64), lvp(cc, par), c("ID", PEN[4] + par, 128 - par, 2), False, False) for cc in range(4) for par in range(2)]
+            order = (0, 3, 1, 2)
+            for cc in order:
                 a = F + 1024 * cc
-                gather_op(c("D", a, 1024), c("xw", F, 4096), c("clx" if EST["WDMA"] else "clu", 128 * cc + 64 * f, 64), c("hh", 1024 * f, 1024), ALU.subtract)
-                act(c("A", a, 1024), c("D", a, 1024), ACT.Abs)
-            b = bank()
-            for cc in range(4):
-                pc = p(b, 64 * cc, 64)
-                lst = [(pc, ALLD, c("one", 0, 64), True, False), (pc, PEN, lv(cc), False, False)] if rnd else []
-                mm(lst + [(pc, sl("KEYW", 15, s), c("A", F + 1024 * cc + s, 1024 - s, 16), s == 0 and not rnd, s == 15) for s in range(16)])
-            tt(c("K", H, 256), p(b, 0, 256), r("posc"), ADD)
-            tt(c("M1", 128 * f, 128), c("K", H, 128), c("K", H + 128, 128), ALU.min)
+                gather_op(c("D", a, 1024), c("xw", F, 4096), clu(cc), c("hh", 1024 * f, 1024), ALU.subtract)
+                ops[-1]["tag"] = ("D", f, rnd, cc)
+                pc = p(kb, 64 * cc, 64)
+                if EST["RELU"][cc]:
+                    ts(c("A", a, 1024), c("D", a, 1024), 0.0, None, ALU.max)
+                    mm(lst + [(pc, c("D", a + 128 * k, 128), sl("GW", 167, k, 64), False, False) for k in range(8)])
+                    lst = []
+                else:
+                    act(c("A", a, 1024), c("D", a, 1024), ACT.Abs)
+                top = 87 if EST["RELU"][cc] else 7
+                mm(lst + [(pc, c("A", a + 128 * k, 128), sl("GW", top, k, 64), False, cc == order[-1] and k == 7) for k in range(8)])
+                lst = []
+            move(c("K", 128 * f, 128), p(kb, 128, 128))
+            tt(c("M1", 128 * f, 128), p(kb, 0, 128), c("K", 128 * f, 128), MIN)
             km = c("Km", 64 * f, 64)
-            tt(km, c("M1", 128 * f, 64), c("M1", 128 * f + 64, 64), ALU.min)
-            ts(c("Ko", 64 * f, 64), km, 4095, None, AND)
-            cp(c("ob", 64 * f, 64), c("Ko", 64 * f, 64))
+            tt(km, c("M1", 128 * f, 64), c("M1", 128 * f + 64, 64), MIN)
+            for cc in (1, 2, 3, 0):
+                tt(c("bt", 528 * f + 128 * cc + 1, 128, 2), p(kb, 64 * cc, 64), km, EQ)
+                if cc == 3:
+                    b = bank()
+                    mm([(p(b, 0, 64), IDN, r("XI"), True, False)]
+                       + [(p(b, 0, 64), btp(k, par), half((K1, K2, K3)[k - 1], par), False, (k, par) == (3, 1)) for k in (1, 2, 3) for par in range(2)])
+                    ts(c("ob", 64 * f, 64), p(b, 0, 64), pf(10), 4095.0, ADD, MIN)
             for hf in range(2):
                 gather(c("Db", 1024 * f + 512 * hf, 512), c("D", F, 4096), c("ob", 64 * f + 32 * hf, 32))
-            for cc in range(4):
-                tt(c("best", H + 64 * cc, 64), c("K", H + 64 * cc, 64), km, EQ)
-            if rnd:
-                ts(c("dd", H, 256), c("K", H, 256), DEAD, None, ALU.is_ge)
-            for cc in range(4):
-                for hf in range(2):
-                    b = bank()
-                    a = F + 1024 * cc + 512 * hf
-                    mm([(p(b), IDN, c("D", a, 512), True, False), (p(b), NEG, c("Db", 1024 * f + 512 * hf, 512), False, True)])
-                    act(c("A2", a, 512), p(b), ACT.Abs)
-                pc = p(bank(), 0, 64)
-                lst = [(pc, sl("ONEW", 15, s), c("A2", F + 1024 * cc + s, 1024 - s, 16), s == 0, False) for s in range(16)]
-                if rnd:
-                    lst.append((pc, DED, c("dd", H + 64 * cc, 64), False, False))
-                mm(lst + [(pc, BST, c("best", H + 64 * cc, 64), False, True)])
-                tt(lv(cc), pc, c("thc", H + 64 * cc, 64), ALU.is_ge)
-            for cc in range(4):
-                for hf in range(2):
-                    b = bank()
-                    hp = c("h1p", 1024 * f + 512 * hf, 512)
-                    out = c("vw", F + 1024 * cc + 512 * hf, 512)
-                    bc = [c("BC", 128 * (8 * hf + s), 128) for s in range(8)]
-                    if EST["MASK"][2 * cc + hf]:
-                        mm([(p(b), SML, hp, True, False)] + [(p(b, 64 * s, 64), bc[s], lv(cc), False, s == 7) for s in range(8)])
-                        act(out, p(b), ACT.Relu, bias=-512.0, scale=512.0)
-                    else:
-                        mm([(p(b, 64 * s, 64), bc[s], lv(cc), True, True) for s in range(8)])
-                        tt(out, p(b), hp, MUL)
-            for part in range(NH):
-                rs = range(RH * part, RH * part + RH)
-                sm, se = bank(), bank()
-                n, hh, xx = 64 * RH, H + 64 * RH * part, X + 128 * RH * part
-                for k, rr in enumerate(rs):
+            for c0 in range(0, 4, NE):
+                eb = bank()
+                n = 64 * NE
+                lst = [(p(eb, 0, n), NEG, c(t, H + 64 * c0, n), t == "tch", False) for t in ("tch", "tcl")]
+                for k in range(NE):
+                    pc = p(eb, 64 * k, 64)
+                    lst += [(pc, btp(c0 + k, par), half(BST, par), False, False) for par in range(2)]
+                    if rnd:
+                        lst.append((pc, LVI, lv(c0 + k), False, False))
+                for k in range(NE):
+                    cc = c0 + k
+                    for hf in range(2):
+                        b = bank()
+                        a = F + 1024 * cc + 512 * hf
+                        mm([(p(b), IDN, c("D", a, 512), True, False)]
+                           + [(p(b, 64 * s, 64), NEG, c("Db", 1024 * f + 8 * hf + s, 1024 - 8 * hf - s, 16), False, s == 7) for s in range(8)])
+                        act(c("A2", a, 512), p(b), ACT.Abs)
+                        mm(lst + [(p(eb, 64 * k, 64), sl("ONEW", 15, 8 * hf + s), c("A2", a + 64 * s, 64), False, (k, hf, s) == (NE - 1, 1, 7)) for s in range(8)])
+                        lst = []
+                act(r("lv", ALL, S(9 * f + 2 * c0 + 1, 9 * f + 2 * (c0 + NE), 2)), p(eb, 0, n), ACT.Sign, bias=0.5 - (32768.0 if rnd else 0.0))
+                for cc in range(c0, c0 + NE):
+                    for hf in range(2):
+                        b = bank()
+                        a = F + 1024 * cc + 512 * hf
+                        mm([(p(b, 64 * s, 64), c("BC", 128 * (8 * hf + s), 128), lv(cc), True, True) for s in range(8)])
+                        tt(c("vw", a, 512), p(b), c("D", a, 512), MIN)
+                        ops[-1]["tag"] = ("M", f, rnd, 2 * cc + hf)
+            parts = EST["PARTS"]
+            if last:
+                pair = (1, 2, 0, 0)[me]
+                parts = [(pair, pair + 2)] + [(d, d + 1) for d in others if d not in (pair, pair + 1)] + [(me, me + 1)]
+            for part, (ra, rb) in enumerate(parts):
+                sm, se = bank(), (bank() if last else None)
+                n, hh, xx = 64 * (rb - ra), H + 64 * ra, X + 128 * ra
+                ps = p(sm, 0, 2 * n)
+                for k, rr in enumerate(range(ra, rb)):
                     for hf in range(2):
                         gather(c("vT", F + 1024 * rr + 512 * hf, 512), c("vw", F, 4096), c("posT", H + 64 * rr + 32 * hf, 32))
-                    mm([(p(se, 64 * k, 64), sl("SELW", 15, a), c("vT", F + 1024 * rr + 64 * a, 64), a == 0, a == 15) for a in range(16)])
-                    lst = [(p(sm, 0, 2 * n), r("Z"), c("h1p", 1024 * f, 2 * n), True, False)] if k == 0 else []
-                    mm(lst + [(p(sm, 128 * k, 128), sl("SUMW", 7, u), c("vT", F + 1024 * rr + 128 * u, 128), False, False) for u in range(8)])
-                ts(c("L", hh, n), p(se, 0, n), 0.5, None, ALU.is_lt)
-                b = bank()
-                mm([(p(b, 0, n), r("NW"), c("L", hh, n), True, True)])
-                ts(c("d8", hh, n), p(b, 0, n), 4.5, 8.0, ALU.is_gt, MUL)
-                tt(c("W8", hh, n), p(b, 0, n), c("d8", hh, n), ALU.max)
-                ot = S(4 * f + rs[0], 4 * f + rs[-1] + 1)
+                    if last:
+                        mm([(p(se, 64 * k, 64), sl("SELW", 15, a), c("vT", F + 1024 * rr + 64 * a, 64), a == 0, a == 15) for a in range(16)])
+                    lst = []
+                    if k == 0:
+                        lst = [(ps, IDN, c("xc", xx, 2 * n), True, False)]
+                        if not last:
+                            lst.append((ps, c("CST", 128 * rnd, 128), c("one", 0, 2 * n), False, False))
+                        if rnd == 1:
+                            lst.append((ps, KD, c("dx", xx, 2 * n), False, False))
+                    mm(lst + [(p(sm, 128 * k, 128), sl("SUMW", 7, u), c("vT", F + 1024 * rr + 128 * u, 128), False, not last and (rr, u) == (rb - 1, 7))
+                              for u in range(8)])
+                ot = S(4 * f + ra, 4 * f + rb)
+                cols = [(128 * k + 64 * w, w, 64 * k) for k in range(rb - ra) for w in range(2)]
                 if last:
-                    b = bank()
-                    mm([(p(b, 0, n), r("NW"), c("L", hh, n), True, False), (p(b, 0, n), ID8, c("L", hh, n), False, True)])
-                    ts(r("OT", ALL, ot, S(128, 192)), p(b, 0, n), 4.5, None, ALU.is_lt)
-                cols = [(128 * k + 64 * w, w, hh + 64 * k) for k in range(RH) for w in range(2)]
-                mm([(p(sm, x, 64), c("XB", (512 if last else 256) + 128 * w, 128), c("d8", y, 64), False, x == 2 * n - 64) for (x, w, y) in cols])
-                if last:
-                    act(c("Sm", xx, 2 * n), p(sm, 0, 2 * n), ACT.Relu, bias=-0.4375, scale=0.125)
+                    Lt, dt = c("L", hh, n), c("d8", hh, n)
+                    add({"V": tsf(Lt, p(se, 0, n), -16384.0, None, ALU.is_lt, None), "S": actf(Lt, p(se, 0, n), ACT.Relu, -1.0, -1.0 / 16384.0)}, [p(se, 0, n)], [Lt])
+                    for again in (1, 0):
+                        b = bank()
+                        mm([(p(b, 0, n), r("NW"), Lt, True, False)] + ([(p(b, 0, n), ID8, Lt, False, False)] if again else [])
+                           + [(p(b, y, 64), c("XT", 128 * w, 128), c("dx", xx + x, 64), False, x == 2 * n - 64) for (x, w, y) in cols])
+                        if again:
+                            ts(r("OY", ALL, ot), p(b, 0, n), 4.5, None, ALU.is_lt)
+                            if part == 1:
+                                send("ay%d" % f, {d: [(r("OY", ALL, 4 * f + d), r("ll", 4 * f + me))] for d in others}, False)
+                        else:
+                            ts(dt, p(b, 0, n), 4.5, -7.0 / (1 << 17), ALU.is_gt, ADD)
+                    mm([(p(sm, x, 64), c("XB", 128 * w, 128), c("L", hh + y, 64), False, False) for (x, w, y) in cols])
+                    mm([(p(sm, x, 64), c("XB", 256 + 128 * w, 128), c("d8", hh + y, 64), False, x == 2 * n - 64) for (x, w, y) in cols])
                 else:
-                    act(c("Sm", xx, 2 * n), p(sm, 0, 2 * n), ACT.Relu, bias=512.4375, scale=-0.125)
-                b = bank()
-                mm([(p(b, x, 64), c("XB", 768 + 128 * w, 128), c("W8", y, 64), True, True) for (x, w, y) in cols])
-                pw = p(b, 0, 2 * n)
-                tt(pw, pw, c("x1", xx, 2 * n), MUL)
-                tt(c("yi", xx, 2 * n), pw, c("Sm", xx, 2 * n), ADD if last else ALU.subtract)
+                    ts(c("qn", xx, 2 * n), ps, float((1 << 19) + 18000), None, MIN)
+                    tt(ps, ps, c("qn", xx, 2 * n), ALU.subtract)
+                u = c("U", xx, 2 * n)
+                tt(u, ps, u, MIN)
                 if last:
-                    ts(r("OT", ALL, ot, S(0, 128)), c("yi", xx, 2 * n), -1.0, None, ADD)
+                    ts(c("yi", xx, 2 * n), u, 511, None, AND)
+                    cp(r("OX", ALL, ot), c("yi", xx, 2 * n))
                 else:
-                    ts(c("xm", xx, 2 * n), c("yi", xx, 2 * n), 511.0, None, ADD)
-                    ts(c("x1", xx, 2 * n), c("yi", xx, 2 * n), 511, None, AND)
-                    if not EST["WDMA"]:
-                        window(f, "xm", rs)
-            if EST["WDMA"] and not last:
-                window(f, "xm")
-        sem = "ao%d" % f
-        send(sem, {d: [(r("OT", ALL, 4 * f + d), r("OL", ALL, 4 * f + me))] for d in others})
-        put = lambda t, d, k: [(r("yx", S(32 * d + 16 * f, 32 * d + 16 * f + 16)), r(t, ALL, k, S(0, 128))),
-                               (r("yl", S(2 * d + f, 2 * d + f + 1)), r(t, ALL, k, S(128, 192)))]
-        dma(put("OT", me, 4 * f + me), engs="Y")
-        arrive(sem, [r("OL", ALL, 4 * f + d) for d in others], -1.0)
-        dma([x for d in others for x in put("OL", d, 4 * f + d)], engs="Y")
+                    xa, da = c("xc", xx, 2 * n), c("dx", xx, 2 * n)
+                    ts(xa, u, -512.0 * (2 - rnd), None, ADD)
+                    window(f, ra, rb, EST["WIN"][part])
+                    add({"V": tsf(da, xa, -256.0, 0.0, ADD, ALU.max), "S": actf(da, xa, ACT.Relu, -256.0, 1.0)}, [xa], [da])
+                if last and part == 1:
+                    send("ao%d" % f, {d: [(r("OX", ALL, 4 * f + d), r("lx", 4 * f + me))] for d in others}, False)
+        yl = lambda d: r("yl", S(2 * d + f, 2 * d + f + 1))
+        dma([(yl(me), r("OY", ALL, 4 * f + me))], 128, 128, engs="Y")
+        dma([(r("yx", rows(me, f)), r("OX", ALL, 4 * f + me))], 128, 256, engs="S")
+        arrive("ay%d" % f, [r("ll", 4 * f + d) for d in others])
+        dma([(yl(d), r("ll", 4 * f + d)) for d in others], 48, 1024, engs="Y")
+        arrive("ao%d" % f, [r("lx", 4 * f + d) for d in others])
+        dma([(r("yx", rows(d, f)), r("lx", 4 * f + d)) for d in others], 48, 2048, engs="Y")
 
     for f in range(2):
         lead[0] = EST["LEAD"] * (1 - f)
@@ -439,7 +507,7 @@ def build(me):
 def hazards(ops):
     seen = {}
     deps = []
-    sends = {}
+    sends = {op["sem"]: i for i, op in enumerate(ops) if op["kind"] == "r"}
     for i, op in enumerate(ops):
         d = set()
         both = [(x, False) for x in op["R"] if x[0] not in EXT] + [(x, True) for x in op["W"] if x[0] not in EXT]
@@ -459,10 +527,8 @@ def hazards(ops):
             if wr and len(SCRATCH[x[0]][1]) == 2 and all(isinstance(s, slice) and s.step in (None, 1) for s in x[1]):
                 old[:] = [t for t in old if not (x[2] <= t[2] and t[3] <= x[3] and x[4] <= t[4] and t[5] <= x[5])]
             old.append((i, wr, x[2], x[3], x[4], x[5]))
-        if op["kind"] == "r":
-            sends[op["sem"]] = i
-        if op["kind"] == "a" and op["at"] < 0:
-            op["after"] = sends[op["sem"]]
+        if op["kind"] == "a":
+            d.add(sends[op["sem"]])
         if "behind" in op:
             d.add(sends[op["behind"]])
         deps.append(d)
@@ -470,7 +536,6 @@ def hazards(ops):
 
 
 def place(ops, deps, order, eng):
-    n = len(ops)
     LAT = EST["LAT"]
     first, lastuse = {}, {}
     for i, op in enumerate(ops):
@@ -479,49 +544,59 @@ def place(ops, deps, order, eng):
                 first.setdefault(x[1], i)
                 lastuse[x[1]] = i
     opens = {i: vb for vb, i in first.items()}
-    holder = [None] * 8
-    bank_of = {}
-    deps = [set(d) for d in deps]
-    done = [None] * n
-    start = [0.0] * n
+    done = [-1.0] * len(ops)
+    holder = [-1] * 8
     free = {e: 0.0 for e in "VSPGY"}
+    rfree = 0.0
+    bank_of, after = {}, {}
     for i in order:
         op, e = ops[i], eng[i]
         t = max([done[j] + LAT for j in deps[i]] or [0.0])
         if e is None:
-            start[i] = done[i] = max(t, op["at"] if op["at"] >= 0 else done[op["after"]] + 3000.0)
+            done[i] = t + 2500.0 if op["at"] < 0 else max(t + 2000.0, op["at"])
             continue
         if i in opens:
-            tb, bk = min((0.0 if holder[b] is None else done[lastuse[holder[b]]], b) for b in range(8)
-                         if holder[b] is None or done[lastuse[holder[b]]] is not None)
+            tb, bk = min((-LAT if h < 0 else done[h], b) for b, h in enumerate(holder) if h < 0 or done[h] >= 0.0)
             t = max(t, tb + LAT)
-            if holder[bk] is not None:
-                deps[i].add(lastuse[holder[bk]])
-            holder[bk] = opens[i]
+            if holder[bk] >= 0:
+                after[i] = holder[bk]
+            holder[bk] = lastuse[opens[i]]
             bank_of[opens[i]] = bk
-        start[i] = max(t, free[e])
-        free[e] = start[i] + op["alts"][e][0]
-        done[i] = free[e] + op["lat"]
-    return order, eng, bank_of, deps, start, done
+        t = free[e] = max(t, free[e]) + op["alts"][e][0]
+        if op["ring"]:
+            rfree = max(rfree, t) + op["ring"]
+            t = rfree + op["lat"]
+        done[i] = t
+    return done, bank_of, after
 
 
 DIGITS = "0123456789abcdefghijklmnopqrstuvwxyzABCDEFGHIJKLMNOPQRSTUVWXYZ"
+MADE = {}
 
 
-def planned(ops, deps):
-    v = [DIGITS.index(PLAN[k]) * 62 + DIGITS.index(PLAN[k + 1]) for k in range(0, len(PLAN), 2)]
-    order = [x >> 1 for x in v]
-    if sorted(order) != list(range(len(ops))):
-        raise ValueError("PLAN does not fit the calls")
-    eng = [None] * len(ops)
-    seen = set()
-    for x in v:
-        alts = sorted(ops[x >> 1]["alts"])
-        eng[x >> 1] = None if not alts else alts[0] if x & 1 else alts[-1]
-        if not deps[x >> 1] <= seen:
-            raise ValueError("PLAN breaks a hazard")
-        seen.add(x >> 1)
-    return place(ops, deps, order, eng)
+def planned(plan):
+    if not MADE:
+        alls = [build(d) for d in range(4)]
+        hz = [hazards(ops) for ops in alls]
+        deps = [set().union(*[h[i] for h in hz]) for i in range(len(alls[0]))]
+        v = [DIGITS.index(plan[k]) * 62 + DIGITS.index(plan[k + 1]) for k in range(0, len(plan), 2)]
+        order = [x >> 1 for x in v]
+        if sorted(order) != list(range(len(deps))):
+            raise ValueError("the plan does not fit the calls")
+        eng = [None] * len(deps)
+        seen = set()
+        for x in v:
+            alts = sorted(alls[0][x >> 1]["alts"])
+            eng[x >> 1] = None if not alts else alts[0] if x & 1 else alts[-1]
+            if not deps[x >> 1] <= seen:
+                raise ValueError("the plan breaks a hazard")
+            seen.add(x >> 1)
+        done, bank_of, after = place(alls[0], deps, order, eng)
+        for i, h in after.items():
+            for x in hz:
+                x[i].add(h)
+        MADE.update(ops=alls, deps=hz, order=order, eng=eng, done=done, bank=bank_of)
+    return MADE
 
 
 def split_engines(core, cores, topo):
@@ -548,8 +623,8 @@ def rank_program(g, core, T, topo):
     if me is None:
         return
     cores = list(T.cores)
-    ops = build(me)
-    order, eng, bank_of, deps, start, done = planned(ops, hazards(ops))
+    plan = planned(PLAN)
+    ops, deps, order, eng, done, bank_of = plan["ops"][me], plan["deps"][me], plan["order"], plan["eng"], plan["done"], plan["bank"]
     queue = {"V": g.vector, "S": g.scalar, "P": g.tensor, "G": g, "Y": g.sync}
     mine = split_engines(core, cores, topo)
     inbound = sum(len(split_engines(x, cores, topo)[core]) for x in cores if x != core)

@@ -11,12 +11,12 @@ for _where, _dt, _list in (
     ("sbuf", I32, (("hs", 512), ("hq", 512), ("hr", 512), ("ths", 64), ("clc", 8, 64), ("s1", 512), ("s2", 256), ("cls", 512), ("clw", 1024),
                    ("U", 1024), ("yi", 1024), ("pi", 16))),
     ("sbuf", U16, (("hbo", 512), ("posT", 512), ("clu", 512), ("ob", 128))),
-    ("sbuf", F32, (("tio", 4096), ("K", 256), ("M1", 256), ("Km", 128), ("pf", 32), ("row", 192), ("io3", 128), ("io2", 128))),
-    ("sbuf", BF, (("hu", 4, 256), ("hb", 1024), ("thh", 64), ("thl", 64), ("thw", 4096), ("one", 1024), ("big", 1024), ("xw", 8192), ("hh", 2048),
-                  ("D", 8192), ("A", 8192), ("A2", 8192), ("Db", 2048), ("vw", 8192), ("vT", 8192), ("bt", 1056), ("lv", 18, 64),
-                  ("tch", 512), ("tcl", 512), ("L", 512), ("d8", 512), ("qn", 1024), ("dx", 1024), ("CST", 256), ("XT", 256), ("xc", 1024),
-                  ("OX", 8, 128), ("OY", 8, 64), ("GW", 240), ("ONEW", 144), ("INVW", 288), ("THW", 288), ("SUMW", 144), ("SELW", 144),
-                  ("RW", 1152), ("ID", 1408), ("BC", 2048), ("NW", 128), ("XB", 512), ("WX", 1024), ("CK", 256), ("XI", 64))),
+    ("sbuf", F32, (("tio", 4096), ("K", 256), ("M1", 256), ("Km", 128), ("pf", 32), ("row", 192), ("io3", 128))),
+    ("sbuf", BF, (("hu", 4, 256), ("hb", 1024), ("thh", 64), ("thl", 64), ("thw", 4096), ("one", 1152), ("big", 1024), ("xw", 8192), ("hh", 2048),
+                  ("D", 8192), ("A", 8192), ("A2", 8192), ("Db", 2048), ("vw", 8192), ("vT", 8192), ("bt", 1056), ("lt", 1056), ("lv", 512),
+                  ("tch", 512), ("tcl", 512), ("L", 512), ("qn", 1024), ("dx", 1024), ("CST", 384), ("XT", 256), ("xc", 1024),
+                  ("OX", 8, 128), ("OY", 8, 64), ("GW", 320), ("ONEW", 144), ("INVW", 288), ("THW", 160), ("SUMW", 144), ("SELW", 144),
+                  ("RW", 1152), ("ID", 1536), ("BC", 2048), ("NW", 128), ("WX", 1024), ("CK", 256), ("XI", 64))),
     ("psum", F32, tuple(("pb%d" % _b, 512) for _b in range(8))),
 ):
     for _x in _list:
@@ -24,10 +24,24 @@ for _where, _dt, _list in (
 SEMAPHORES = (["cV", "cS", "cP", "cG", "sent", "acl0", "afx0", "ahv0", "ath", "acl1", "afx1", "ahl", "ahv1", "ao0", "ao1", "ay0", "ay1"]
               + ["d%d" % _k for _k in range(60)])
 
-EST = {"CY": 0.86, "GA": 1.56, "PE": 0.43, "FIX": 60.0, "LAT": 90.0, "TT": 2.0, "DQ": 70.0, "DFIX": 2000.0, "ROW": 50.0, "RATE": 14.0,
-       "RELU": (0, 0, 0, 0), "NE": 1, "WIN0": "PD", "WIN": "PP", "PARTS": ((0, 2), (2, 4)), "LEAD": 0.0, "LATE": 0.0}
-PLAN = "0q1K1Y460a28000602041M1W2y080o0m2G2a3k2Q1U2c0F0c3I3x202o2q3z0y0I2K223B0O0s2I0K0M0H1m0Q2s0S1k4S5c2M4W2S30343r54242e1i261o0u2A2u0i2C0U583W1q0e1S0B320D4V2O1O3U3Y1Q40502W0W0w0Y3d5b5f3O2g0g2Y2U1u12573p3F1w1C0k2E103e14165o4C4E4G4w4I4y424K4M4O4A3m3v5k5g5j5n534Z181a4Q36394a2i6c4c4u666o686a6e6q1g1c6i5KgSgU3G1e1G1s1y6khc6g6m4gh04q6sgM4i6vgY4kh2454oh46w6y6AgW6C5tgO1I5r6E6GhygQ3a5M6I6N5y5S5O5A606P7i7c6W4s5x5vh8hf5QhA5U5WhC1A1E5C5E5H7E6Q7k7G7e7yh65Y627A6K5Ihh7C7I7K7U7g7m4m7Qhl3ghG80ha646S82i0hUi67SichEhIhm6Y7o7u6U707M7Wi2727Y7884hWhY86747a88768aho8c8ehjhqhs7O7w7q7s8gi8i4ia8iieigiiikhvhwim2wioiq3Q8k8p8n8V8q918sisiu8u3s8T8W8w8Ziw8y8I928MhO94968A8EiD8LiBj68H8D8P2kjI989a9o9k9r9g9j9niyhK9c9ej03KjsjmjOjuiKj2j4jojqj8iE9u9wjwjajyjc9M9AjejAhMjgjK9GjCiGiM9CiIjiiOiQjEjMiWiSiYiUjQjS4fjUjWk0k2jG9O9t9yhQjkjYhS9E9I9K9Q9Tk59Uk69W9Ya0kGa2k8kMkbkdkekga4a6kikkkmkJkKkPkQkSkUkWkYkAkskwa8abad3MkubolckokqkDl0kzlfl33Cl4l8lal7lilAaAaCbibk8RakaGaIaEbqlulobmaeaKamagaWaYaMbsbub2aib4aoaqbAaSaObCaUbwawaylklwb0b6b8bybeasaubabcbglmaQlqlslylClhlElHlIbFcjlKcgcpbLbNlMcmlO3SlQbGckcqcslSbIbOlUlZm1cucwcycAcIcE2mbQcDcHmKcMcPbSbUbWc6cacKcdc2bYc1kEmMncc8nemomun6mwmqn8c4mQmSm2m4m8msmymAmOnamUnglWm6d4cSdacYcUmWn2nimanonqmYn0mCmEn4nkd0mcmemgminmmGmImkmmd6cWd2d8dcdedhdioanvntdkdmnAdonwdqdso4dunznCnEnGo7o8odoenInKnYnMogoioknUnQdzdBdwdIomoooAo1nXnPnSowor3iosovoCdKeMekemeOdCoyoMeqeGdEeIdGdMoOdOeKeQeSe4eooGoIoKdQoQoSeUoUcfoWdYoYp0p2eYeseudSeWe0p4p6dUp8papcpee6e2e8pgeweCeaegecpkpipneypoquqwpMdWeipSpUeEeAf0pOeeqApqpsq8f4faqaqCg8qeqypwpyqgpuqEqGqcpAqiqMqkfc48pQqOqIqmqopWf3f8qKpYcQpCq4qqpEq6pGo2qspIf6fDfFfGq0pKfegbfgfKfifSfMgcfIq2rtrqrufofkqTqQfUfWrZrwfsryrKqZfqfYfufmoErGqUfOrWg0g2qWr1rIfwfyr2rMr7fQgEgGg4fAr4rcrgrOrQr8ghrerirAg6s0rSrarkrCrEgissrmrorUgegkgIgAs5s6gms8sogqgosascgss2sesggKgugwgysiskgCsmsqsuswsy"
-ARRIVE = {"acl0": 5500.0, "afx0": 7500.0, "ahv0": 8500.0, "ath": 9500.0, "acl1": 10500.0, "afx1": 12000.0, "ahl": 13500.0, "ahv1": 15000.0}
+EST = {"CY": 0.83, "GA": 1.56, "PE": 0.42, "FIX": 20.0, "LAT": 140.0, "TT": 2.0, "DQ": 70.0, "DFIX": 1800.0, "ROW": 20.0, "RATE": 25.0,
+       "PF": 15.0, "PS": 8.0, "SX": 25.0, "SG": 15.0, "AS": 0.6, "A0": 3000.0, "A1": 2000.0, "GS": 400.0,
+       "RELU": (0, 1, 1, 0), "MS": (0, 0, 0, 1, 0, 1, 0, 1), "WIN0": "PD", "WIN": "PP", "PARTS": ((0, 2), (2, 4)), "LEAD": 0.0}
+PLAN = (
+    "000q02200a282k2a2c2u2o2K223u2e4e0m0G0I2M1m2G2m2O040K0x0o0u0s2C2q382i2Q082E323U060e3A0D2S2W0O1q1o0Q0U3Q1s3L3g0E2Z0S0k3Z40462U0B345a0M3k0i3O525i0c1y2w5e4U3e123J0z"
+    "102g3q1e3N4Q1u26143a3z423i16444a0W0Y181w0g3x1a5c1A3S5556301c5g4u4A4w2I3H1i3c4C1G4y4X5l4s594I4G4M4m4K4O364Y511E4E4T68626O1g1C1W1O6e1I1S3p6a648o666c6g6i5n6m1YhY6o"
+    "i0ia6ki46q6s6u6W7q4q1K5r5ti66wic6yie6Aig6Ci26E1M1k5G4k5Ii87Mii5u5p6G6I6L1Q5w4o6N8g5y5A5Dip7i7k8q8i6Q6Y6S8k7s707u7O5O5K5M5W5E6U727m8m74iw8s7U7W7Q767o7Y8u798w7w5Q"
+    "7S7y7A8y80ik5Sim1Ujoj4jgja4i5U7e7a7cit82847D7E7G5Y8B7I8C8E7gir87j68GiI888c7Ljc8Jj88f8aiy608L8PjiiKjq9ijQjejkjmiQjsjujx9njy3m8MjAjYiv8Q8SjCjE8UjG9k9o8W9qjIjKjP9s"
+    "iAkWiCjNkk8Y949790939uiU98jSk0jU9ckmiE9wiG9K9b9N9e9C9F9y9BkOkY9G9Jk2jWliiMiYkQiOlkl0lqiSkskSk49QiWkokqkU9Wlmloa2l2a4ls9Sl4j0l6k6k89Uku9Ya0aa2skbkcac3Da6l9lakelc"
+    "lua8kwkykAlwaekgkiaglylAkCajleakamaolDlI48kFkGaqaslhkKlLkIaukNawazlEj2aKbelGmllNaCccaA9hc4b6c6c8bgbiaMmmaOb8molQbamqmslOmumwlSlUbAaEaGcemylWlYm0mEmHmAmCmMmOmImL"
+    "m2m5mamcmemgm6m9bccgaIbkbmaQaSbCbEbImScaboaUcibraXckbK9PbMb2cmcpmYmUnEbGcqbObQcuaYn4csb4n0bSbVbscxbwc0bub0bzbWbYpen6ncnemWn2c3cyn8nad7d8ngninkdbdcdenmdgnodinqcD"
+    "dknsmRcAcEcGdydBnucImjcKoCnwnynDnBducMdwdqdscSd0d2cWcZcOcQdmdppgoEpioKoGogcUo8oMoOp6oaocp8paoIoinGoknMoQoedQdEoSnIpcdKdYomoUoXpkpmoonOnQnKpoproqot24oYnSp0nUp2ou"
+    "nWdGdMnYpwoyowo0o2o4pso6puoBpzp5dIeydOdUdSdWeUe2e0pEe4e6pBpCpGe8eaeceepIq9qaqdegeipKpMekqefSpOq2pYenpQpUepqgpTq12yq5eWqi4cqkqmpWqsquqoqqqAqwqDfUeYfWf2eqeAeCeseu"
+    "fog0f4fqfsfYfwewfuqyqGqIeEfyf0g2eGeIf6qMsUqOqSf8qKeKfaeQqQrW3Fg4qUqWfAg6qYr0g8fCr2fEfcr4d52AgaffeSfGfIr6fgr8gcrafksqdDfnqErcrergfirigefKfMgiglrkrmrqrpfOt2s4rsfR"
+    "t4t6sssueMsWrurAs6rCsyrYggsYt03s4grws8s0eOrEgvrygUgSt8tagYgmswsAsCgWrGrIh1q6gotcs2h8sEhahcrKsGtetgsaschkrNgxhesIsKtksetnsMrOsg3WsOsmsQsirSrQgqgsh2sTtiskgyrUsptV"
+    "tWtogCgAgItrh4gKu0uagMucgOtuuegQhghihSgEgGtztxtCtKtMugtOtsh6tYhUtAhWhnhqhMhOuitQtShQukuUuWhyupunu3tFtGu4tIu6u8hAhCusuAhEuquvuwuCuEhGuyhohKuKuGuIuMuOhshuhwhIuYuQ"
+    "uS")
+ARRIVE = (("acl0", 800.0), ("afx0", 2000.0), ("ahv0", 1500.0), ("ath", 2500.0), ("acl1", 800.0), ("afx1", 2000.0), ("ahl", 2500.0), ("ahv1", 1500.0))
 EXT = ("fx", "hv", "hl", "cl", "th", "yx", "yl")
 
 
@@ -101,7 +115,7 @@ def build(me):
         return (vc(out, in0), f)
 
     def actf(out, in_, fn, bias, scale):
-        return (vcost(width(in_), 1.0), lambda q, ap: q.activation(ap(out), ap(in_), fn, bias=bias, scale=val(ap, scale)))
+        return (vcost(width(in_), 1.0) + EST["SX"], lambda q, ap: q.activation(ap(out), ap(in_), fn, bias=bias, scale=val(ap, scale)))
 
     def ts(out, in0, s1, s2, op0, op1=None):
         add({"V": tsf(out, in0, s1, s2, op0, op1)}, [in0] + [s for s in (s1, s2) if isinstance(s, tuple)], [out])
@@ -119,6 +133,9 @@ def build(me):
     def act(out, in_, fn, bias=0.0, scale=1.0):
         add({"S": actf(out, in_, fn, bias, scale)}, [in_], [out])
 
+    def either(out, in_, s1, s2, op0, op1, fn, bias, scale):
+        add({"V": tsf(out, in_, s1, s2, op0, op1), "S": actf(out, in_, fn, bias, scale)}, [in_], [out])
+
     def move(out, in_):
         add({"V": (vc(out, in_), lambda q, ap: q.tensor_copy(ap(out), ap(in_))), "S": actf(out, in_, ACT.Identity, 0.0, 1.0)}, [in_], [out])
 
@@ -129,7 +146,7 @@ def build(me):
     def gather(out, win, off):
         d = FIX + width(out) * GA * CY
         add({"V": (d, lambda q, ap: q.tensor_copy(ap(out), ap(win).indirect(ap(off)))),
-             "S": (d, lambda q, ap: q.activation(ap(out), ap(win).indirect(ap(off)), ACT.Copy))}, [win, off], [out])
+             "S": (d + EST["SG"], lambda q, ap: q.activation(ap(out), ap(win).indirect(ap(off)), ACT.Copy))}, [win, off], [out])
 
     def gather_op(out, win, off, in1, op):
         d = FIX + width(out) * GA * CY
@@ -144,22 +161,23 @@ def build(me):
         R = []
         for (o, l, x, a, b) in lst:
             R += [t for t in (l, x) if t not in R]
-        add({"P": (30.0 + sum(max(64, width(x)) for (o, l, x, a, b) in lst) * PEC, f)}, R, [lst[0][0]])
+        d = EST["PF"] + sum(max(64, width(x)) * PEC + EST["PS"] * (l[0] in ("A", "A2", "D", "bt", "lt")) for (o, l, x, a, b) in lst)
+        add({"P": (d, f)}, R, [lst[0][0]])
 
-    def iota(out, pat, base, mult, behind=False):
+    def iota(out, pat, base, mult, behind=None):
         if SCRATCH[out[0]][2] == I32:
             f = lambda q, ap: q.iota(ap(out), pat, base, mult)
         else:
             f = lambda q, ap: q.iota(ap(out), pat, base, mult, allow_small_or_imprecise_dtypes=True)
         add({"G": (140.0 + 2 * width(out) * CY, f)}, [], [out])
         if behind:
-            ops[-1]["behind"] = "ahv1"
+            ops[-1]["behind"] = behind
 
-    def select(out, src, pat, base, behind=True):
+    def select(out, src, pat, base, behind=None):
         n = width(out)
         add({"G": (180.0 + 2 * n * CY, lambda q, ap: q.affine_select(ap(out), ap(c(src, 0, n)), pat, ALU.is_equal, 0.0, base, -1))}, [c(src, 0, n)], [out])
         if behind:
-            ops[-1]["behind"] = "ahv1"
+            ops[-1]["behind"] = behind
 
     def dma(pairs, rows, size, engs="YS", prio=0.0):
         f = lambda q, ap: [q.dma_start(ap(o), ap(i)) for (o, i) in pairs]
@@ -169,13 +187,14 @@ def build(me):
     sent = []
 
     def send(sem, pieces, in_line=True):
-        add({"G": (500.0, pieces)}, [s for d in pieces for (s, t) in pieces[d]], [], kind="r", sem=sem, prio=1e6)
+        add({"G": (EST["GS"], pieces)}, [s for d in pieces for (s, t) in pieces[d]], [], kind="r", sem=sem, prio=1e6)
         if sent and in_line:
             ops[-1]["behind"] = sent[-1]
         sent.append(sem)
 
     def arrive(sem, W):
-        add({}, [], W, kind="a", sem=sem, at=ARRIVE.get(sem, -1.0))
+        add({}, [], [], kind="a", sem=sem, at=EST["A0"] if sem == ARRIVE[0][0] else EST["A1"])
+        add({}, [], W, kind="b", sem=sem, at=dict(ARRIVE).get(sem, 500.0) * EST["AS"])
 
     others = [d for d in range(4) if d != me]
     S = slice
@@ -208,14 +227,14 @@ def build(me):
              for q in (2 * half, 2 * half + 1) for d in range(4)], 256, 512, engs="YS"[half], prio=8e6)
     lead[0] = 1e6
     fill(r("one"), 1.0)
-    fill(r("clw"), 0)
-    fill(r("big"), 32768.0)
-    fill(r("lv"), 0.0)
-    fill(r("bt"), 0.0)
+    times(r("big"), c("one", 0, 1024), 98304.0)
+    times(r("lt"), c("one", 0, 1056), 0.0)
+    times(r("bt"), c("one", 0, 1056), 0.0)
     for k in range(4):
-        move(c("thw", 1024 * k, 1024), r("one"))
+        move(c("thw", 1024 * k, 1024), c("one", 0, 1024))
     sends(0)
     sendhv(0)
+    iota(r("clw"), [[0, 1024]], 0, 0, "ahv0")
     cp(r("thh"), r("ths"))
     tt(r("thl"), r("ths"), r("thh"), ALU.subtract)
     send("ath", {d: [(r("thh"), r("dth", me)), (r("thl"), r("dth", 4 + me))] for d in others})
@@ -247,7 +266,6 @@ def build(me):
     iota(c("pi", 0, 1), [[0, 1]], 0, 1)
     iota(r("row"), [[1, 192]], 0, 0)
     iota(r("io3"), [[0, 8], [1, 16]], 0, 0)
-    iota(r("io2"), [[0, 16], [2, 8]], 0, 0)
     iota(r("CK"), [[1, 4], [0, 64]], 0, 0)
     pi = lambda k: c("pi", k, 1)
     pf = lambda k: c("pf", k, 1)
@@ -270,48 +288,43 @@ def build(me):
     ts(pf(8), pi(4), 16.0, pf(7), MUL, ADD)
     ts(pf(9), pi(1), 8.0, 7.0, MUL, ADD)
     ts(pf(10), pi(2), 64.0, None, MUL)
-    ts(pf(11), pi(2), -1.0, None, ADD)
     for f in range(2):
-        for k, wgt in enumerate((64.0, 1.0, 16.0)):
-            ts(pf(12 + 3 * f + k), pi(3), float(f), wgt, EQ, MUL)
+        ts(pf(12 + f), pi(3), float(f), None, EQ)
         ts(pf(18 + f), pi(7), float(f), 1024.0, EQ, MUL)
         ts(pf(20 + f), pi(8), float(f), None, EQ)
-    for k in range(6):
-        ts(c("RW", 192 * k, 192), r("row"), pf(8), pf(12 + k), EQ, MUL)
+    for f in range(2):
+        ts(c("RW", 576 * f + 192, 192), r("row"), pf(8), pf(12 + f), EQ, MUL)
+        times(c("RW", 576 * f, 192), c("RW", 576 * f + 192, 192), 64.0)
+        times(c("RW", 576 * f + 384, 192), c("RW", 576 * f + 192, 192), 16.0)
     ts(r("ONEW"), c("row", 0, 144), pf(1), None, EQ)
-    for k, wgt in enumerate((4.0, 8.0, -4.0)):
-        if k == 0 or any(EST["RELU"]):
-            ts(c("GW", 80 * k, 72), c("row", 0, 72), pf(9), wgt, EQ, MUL)
+    for k, wgt in enumerate((4.0, 8.0, -4.0, 1.0)):
+        ts(c("GW", 80 * k, 72), c("row", 0, 72), pf(9), wgt, EQ, MUL)
     for f in range(2):
         times(c("INVW", 144 * f, 144), r("ONEW"), pf(18 + f))
-        times(c("THW", 144 * f, 144), r("ONEW"), pf(20 + f))
+        times(c("THW", 80 * f, 72), c("GW", 240, 72), pf(20 + f))
     ts(r("SUMW"), c("row", 0, 144), pf(3), -0.125, EQ, MUL)
     ts(r("SELW"), c("row", 0, 144), pf(5), pf(6), EQ, MUL)
     ts(c("ID", 0, 128), c("row", 0, 128), pf(0), None, EQ)
-    wts = (1.0, -1.0, -float(1 << 20), 8192.0, 32768.0, 8.0, 1024.0, 2048.0, 3072.0, 128.0, -4096.0)
-    for k in range(1, 11):
+    wts = (1.0, -1.0, -float(1 << 20), 8192.0, 32768.0, 8.0, 1024.0, 2048.0, 3072.0, 256.0, -8192.0, 2.0)
+    for k in range(1, 12):
         times(c("ID", 128 * k, 128), c("ID", 0, 128), wts[k])
-    IDN, NEG, PEN, BST, LVI, ID8, K1, K2, K3, KD, KQ = [c("ID", 128 * k, 128) for k in range(11)]
+    IDN, NEG, PEN, BST, LVI, ID8, K1, K2, K3, KD, NBS, ID2 = [c("ID", 128 * k, 128) for k in range(12)]
     cp(r("XI"), c("row", 0, 64))
-    select(r("WX"), "one", [[1, 8], [0, 8], [8, 16]], 0, False)
+    select(r("WX"), "one", [[1, 8], [0, 8], [8, 16]], 0)
     ts(r("NW"), r("io3"), pf(2), None, EQ)
-    for w in range(2):
-        ts(c("XB", 128 * w, 128), r("io2"), pf((2, 11)[w]), -4096.0, EQ, MUL)
-        ts(c("XB", 256 + 128 * w, 128), r("io2"), pf((2, 11)[w]), 1024.0, EQ, MUL)
-    ts(pf(22), pi(0), 0.0, float(1 << 19), EQ, MUL)
-    ts(pf(23), pi(0), 1.0, -0.4375, EQ, MUL)
-    tt(pf(22), pf(22), pf(23), ADD)
+    times(r("CST"), c("one", 0, 384), 0.0)
+    fill(r("CST", S(0, 1)), float((1 << 19) + 4096))
+    fill(r("CST", S(32, 33)), -0.4375)
+    for k in range(RO):
+        fill(r("CST", S(64, 65), S(128 * k, 128 * k + 128)), -512.0 * (k + 1))
     for k in range(2):
-        ts(pf(23 + k), pi(0), 2.0, 1024.0 - 512.0 * k, EQ, MUL)
-        tt(pf(25 + k), pf(22), pf(23 + k), ADD)
-        times(c("CST", 128 * k, 128), c("one", 0, 128), pf(25 + k))
         ts(pf(27 + k), pi(0), 2.0, float(k), MUL, ADD)
         ts(c("XT", 128 * k, 128), r("io3"), pf(27 + k), 1.0 / 32.0, EQ, MUL)
     lead[0] = 0.0
     for k in range(2):
-        select(c("BC", 1024 * k, 1024), "big", [[1, 8], [16, 8], [0, 16]], 8 * k)
+        select(c("BC", 1024 * k, 1024), "big", [[1, 8], [16, 8], [0, 16]], 8 * k, "ahv1")
     for k in range(4):
-        iota(c("tio", 1024 * k, 1024), [[1, 1024]], 1024 * k, 0, True)
+        iota(c("tio", 1024 * k, 1024), [[1, 1024]], 1024 * k, 0, "ahv1")
     sl = lambda name, top, k, n=128: c(name, top - k, n)
 
     def window(f, a, b, how):
@@ -331,10 +344,9 @@ def build(me):
         F = 4096 * f
         X = 512 * f
         H = 256 * f
-        NE = EST["NE"]
-        lv = lambda cc: r("lv", ALL, 9 * f + 2 * cc + 1)
-        lvp = lambda cc, par: r("lv", ALL, S(9 * f + 2 * cc + 1 - par, 9 * f + 2 * cc + 3 - par))
-        btp = lambda cc, par: c("bt", 528 * f + 128 * cc + 1 - par, 128)
+        lv = lambda cc: c("lv", H + 64 * cc, 64)
+        odd = lambda t, cc: c(t, 528 * f + 128 * cc + 1, 128, 2)
+        pad = lambda t, cc, par: c(t, 528 * f + 128 * cc + 1 - par, 128)
         half = lambda m, par: c("ID", m[4] + 64 * par, 64)
         clu = lambda cc: c("clu", H + 64 * cc, 64)
 
@@ -355,14 +367,11 @@ def build(me):
         tt(cls(2), s2(0), s2(1), ALU.max)
         cp(c("clu", H + 64, 128), cls(1, 2))
         window(f, 0, 4, EST["WIN0"][f])
-        ts(c("U", X, 512), c("xc", X, 512), 1536.0, None, ADD)
-        keep = lead[0]
-        lead[0] = keep - EST["LATE"]
         for cc in range(4):
             gather(c("A2", F + 1024 * cc, 1024), r("thw"), clu(cc))
         b = bank()
         for cc in range(4):
-            mm([(p(b, 64 * cc, 64), sl("THW", 144 * f + 15, s), c("A2", F + 1024 * cc + 64 * s, 64), s == 0, s == 15) for s in range(16)])
+            mm([(p(b, 64 * cc, 64), c("A2", F + 1024 * cc + 128 * k, 128), sl("THW", 80 * f + 7, k, 64), k == 0, k == 7) for k in range(8)])
         move(c("tch", H, 256), p(b, 0, 256))
         tt(c("tcl", H, 256), p(b, 0, 256), c("tch", H, 256), ALU.subtract)
         b = bank()
@@ -373,14 +382,13 @@ def build(me):
             gather_op(c("vT", F + 1024 * rr, 1024), r("clw"), c("hbo", H + 64 * rr, 64), c("tio", 1024 * rr, 1024), ALU.is_lt)
             mm(base(b, rr, (1, 2), False) + [(p(b, 64 * rr, 64), sl("INVW", 144 * f + 15, s), c("vT", F + 1024 * rr + s, 1024 - s, 16), False, s == 15) for s in range(16)])
         cp(c("posT", H, 256), p(b, 0, 256))
-        lead[0] = keep
 
         for rnd in range(RO):
             last = rnd == RO - 1
             kb = bank()
             lst = [(p(kb, 0, 256), IDN, r("CK"), True, False)]
             if rnd:
-                lst += [(p(kb, 64 * cc, 64), lvp(cc, par), c("ID", PEN[4] + par, 128 - par, 2), False, False) for cc in range(4) for par in range(2)]
+                lst += [(p(kb, 64 * cc, 64), PEN, odd("lt", cc), False, False) for cc in range(4)]
             order = (0, 3, 1, 2)
             for cc in order:
                 a = F + 1024 * cc
@@ -400,42 +408,47 @@ def build(me):
             tt(c("M1", 128 * f, 128), p(kb, 0, 128), c("K", 128 * f, 128), MIN)
             km = c("Km", 64 * f, 64)
             tt(km, c("M1", 128 * f, 64), c("M1", 128 * f + 64, 64), MIN)
-            for cc in (1, 2, 3, 0):
-                tt(c("bt", 528 * f + 128 * cc + 1, 128, 2), p(kb, 64 * cc, 64), km, EQ)
-                if cc == 3:
-                    b = bank()
-                    mm([(p(b, 0, 64), IDN, r("XI"), True, False)]
-                       + [(p(b, 0, 64), btp(k, par), half((K1, K2, K3)[k - 1], par), False, (k, par) == (3, 1)) for k in (1, 2, 3) for par in range(2)])
-                    ts(c("ob", 64 * f, 64), p(b, 0, 64), pf(10), 4095.0, ADD, MIN)
+            for cc in (1, 2, 3):
+                tt(odd("bt", cc), p(kb, 64 * cc, 64), km, EQ)
+            b = bank()
+            mm([(p(b, 0, 64), IDN, r("XI"), True, False)]
+               + [(p(b, 0, 64), pad("bt", k, par), half((K1, K2, K3)[k - 1], par), False, (k, par) == (3, 1)) for k in (1, 2, 3) for par in range(2)])
+            ts(c("ob", 64 * f, 64), p(b, 0, 64), pf(10), 4095.0, ADD, MIN)
             for hf in range(2):
                 gather(c("Db", 1024 * f + 512 * hf, 512), c("D", F, 4096), c("ob", 64 * f + 32 * hf, 32))
-            for c0 in range(0, 4, NE):
-                eb = bank()
-                n = 64 * NE
-                lst = [(p(eb, 0, n), NEG, c(t, H + 64 * c0, n), t == "tch", False) for t in ("tch", "tcl")]
-                for k in range(NE):
-                    pc = p(eb, 64 * k, 64)
-                    lst += [(pc, btp(c0 + k, par), half(BST, par), False, False) for par in range(2)]
-                    if rnd:
-                        lst.append((pc, LVI, lv(c0 + k), False, False))
-                for k in range(NE):
-                    cc = c0 + k
-                    for hf in range(2):
-                        b = bank()
-                        a = F + 1024 * cc + 512 * hf
-                        mm([(p(b), IDN, c("D", a, 512), True, False)]
-                           + [(p(b, 64 * s, 64), NEG, c("Db", 1024 * f + 8 * hf + s, 1024 - 8 * hf - s, 16), False, s == 7) for s in range(8)])
-                        act(c("A2", a, 512), p(b), ACT.Abs)
-                        mm(lst + [(p(eb, 64 * k, 64), sl("ONEW", 15, 8 * hf + s), c("A2", a + 64 * s, 64), False, (k, hf, s) == (NE - 1, 1, 7)) for s in range(8)])
-                        lst = []
-                act(r("lv", ALL, S(9 * f + 2 * c0 + 1, 9 * f + 2 * (c0 + NE), 2)), p(eb, 0, n), ACT.Sign, bias=0.5 - (32768.0 if rnd else 0.0))
-                for cc in range(c0, c0 + NE):
-                    for hf in range(2):
-                        b = bank()
-                        a = F + 1024 * cc + 512 * hf
-                        mm([(p(b, 64 * s, 64), c("BC", 128 * (8 * hf + s), 128), lv(cc), True, True) for s in range(8)])
+            for cc in range(4):
+                pc = p(bank(), 0, 64)
+                lst = [(pc, NEG, c(t, H + 64 * cc, 64), t == "tch", False) for t in ("tch", "tcl")]
+                if cc:
+                    lst += [(pc, BST, odd("bt", cc), False, False)]
+                else:
+                    lst += [(pc, BST, c("one", 0, 64), False, False)]
+                    lst += [(pc, NBS, odd("bt", z), False, False) for z in (1, 2, 3)]
+                if rnd:
+                    lst.append((pc, LVI, odd("lt", cc), False, False))
+                for hf in range(2):
+                    b = bank()
+                    a = F + 1024 * cc + 512 * hf
+                    mm([(p(b), IDN, c("D", a, 512), True, False)])
+                    mm([(p(b, 64 * s, 64), NEG, c("Db", 1024 * f + 8 * hf + s, 1024 - 8 * hf - s, 16), False, s == 7) for s in range(8)])
+                    act(c("A2", a, 512), p(b), ACT.Abs)
+                    mm(lst + [(pc, c("A2", a + 128 * k, 128), sl("GW", 247, 4 * hf + k, 64), False, (hf, k) == (1, 3)) for k in range(4)])
+                    lst = []
+                act(odd("lt", cc), pc, ACT.Sign, bias=0.5 - (32768.0 if rnd else 0.0))
+                pc = p(bank(), 0, 64)
+                mm([(pc, pad("lt", cc, par), half(IDN, par), par == 0, par == 1) for par in range(2)])
+                move(lv(cc), pc)
+                for hf in range(2):
+                    b = bank()
+                    a = F + 1024 * cc + 512 * hf
+                    bc = [(p(b, 64 * s, 64), c("BC", 128 * (8 * hf + s), 128), lv(cc)) for s in range(8)]
+                    if EST["MS"][2 * cc + hf]:
+                        mm([(p(b), ID2, c("D", a, 512), True, False)] + [x + (False, s == 7) for s, x in enumerate(bc)])
+                        either(c("vw", a, 512), p(b), 0.5, -49152.0, MUL, ADD, ACT.Identity, -49152.0, 0.5)
+                    else:
+                        mm([x + (True, True) for x in bc])
                         tt(c("vw", a, 512), p(b), c("D", a, 512), MIN)
-                        ops[-1]["tag"] = ("M", f, rnd, 2 * cc + hf)
+                    ops[-1]["tag"] = ("M", f, rnd, 2 * cc + hf)
             parts = EST["PARTS"]
             if last:
                 pair = (1, 2, 0, 0)[me]
@@ -444,50 +457,40 @@ def build(me):
                 sm, se = bank(), (bank() if last else None)
                 n, hh, xx = 64 * (rb - ra), H + 64 * ra, X + 128 * ra
                 ps = p(sm, 0, 2 * n)
+                xa, da, u = c("xc", xx, 2 * n), c("dx", xx, 2 * n), c("U", xx, 2 * n)
                 for k, rr in enumerate(range(ra, rb)):
-                    for hf in range(2):
-                        gather(c("vT", F + 1024 * rr + 512 * hf, 512), c("vw", F, 4096), c("posT", H + 64 * rr + 32 * hf, 32))
+                    w = 512 if last else 1024
+                    for a in range(1024 * rr, 1024 * rr + 1024, w):
+                        gather(c("vT", F + a, w), c("vw", F, 4096), c("posT", H + a // 16, w // 16))
                     if last:
                         mm([(p(se, 64 * k, 64), sl("SELW", 15, a), c("vT", F + 1024 * rr + 64 * a, 64), a == 0, a == 15) for a in range(16)])
                     lst = []
                     if k == 0:
-                        lst = [(ps, IDN, c("xc", xx, 2 * n), True, False)]
-                        if not last:
-                            lst.append((ps, c("CST", 128 * rnd, 128), c("one", 0, 2 * n), False, False))
-                        if rnd == 1:
-                            lst.append((ps, KD, c("dx", xx, 2 * n), False, False))
-                    mm(lst + [(p(sm, 128 * k, 128), sl("SUMW", 7, u), c("vT", F + 1024 * rr + 128 * u, 128), False, not last and (rr, u) == (rb - 1, 7))
-                              for u in range(8)])
+                        lst = [(ps, IDN, xa, True, False), (ps, c("CST", 128 * rnd, 128), c("one", 0, 2 * n), False, False)]
+                        if rnd:
+                            lst.append((ps, KD, da, False, False))
+                    mm(lst + [(p(sm, 128 * k, 128), sl("SUMW", 7, u8), c("vT", F + 1024 * rr + 128 * u8, 128), False, (rr, u8) == (rb - 1, 7)) for u8 in range(8)])
                 ot = S(4 * f + ra, 4 * f + rb)
-                cols = [(128 * k + 64 * w, w, 64 * k) for k in range(rb - ra) for w in range(2)]
                 if last:
-                    Lt, dt = c("L", hh, n), c("d8", hh, n)
-                    add({"V": tsf(Lt, p(se, 0, n), -16384.0, None, ALU.is_lt, None), "S": actf(Lt, p(se, 0, n), ACT.Relu, -1.0, -1.0 / 16384.0)}, [p(se, 0, n)], [Lt])
-                    for again in (1, 0):
-                        b = bank()
-                        mm([(p(b, 0, n), r("NW"), Lt, True, False)] + ([(p(b, 0, n), ID8, Lt, False, False)] if again else [])
-                           + [(p(b, y, 64), c("XT", 128 * w, 128), c("dx", xx + x, 64), False, x == 2 * n - 64) for (x, w, y) in cols])
-                        if again:
-                            ts(r("OY", ALL, ot), p(b, 0, n), 4.5, None, ALU.is_lt)
-                            if part == 1:
-                                send("ay%d" % f, {d: [(r("OY", ALL, 4 * f + d), r("ll", 4 * f + me))] for d in others}, False)
-                        else:
-                            ts(dt, p(b, 0, n), 4.5, -7.0 / (1 << 17), ALU.is_gt, ADD)
-                    mm([(p(sm, x, 64), c("XB", 128 * w, 128), c("L", hh + y, 64), False, False) for (x, w, y) in cols])
-                    mm([(p(sm, x, 64), c("XB", 256 + 128 * w, 128), c("d8", hh + y, 64), False, x == 2 * n - 64) for (x, w, y) in cols])
-                else:
-                    ts(c("qn", xx, 2 * n), ps, float((1 << 19) + 18000), None, MIN)
-                    tt(ps, ps, c("qn", xx, 2 * n), ALU.subtract)
-                u = c("U", xx, 2 * n)
-                tt(u, ps, u, MIN)
+                    Lt = c("L", hh, n)
+                    either(Lt, p(se, 0, n), -16384.0, None, ALU.is_lt, None, ACT.Relu, -1.0, -1.0 / 49152.0)
+                    b = bank()
+                    mm([(p(b, 0, n), r("NW"), Lt, True, False), (p(b, 0, n), ID8, Lt, False, False)]
+                       + [(p(b, 64 * k, 64), c("XT", 128 * w, 128), c("dx", xx + 128 * k + 64 * w, 64), False, (k, w) == (rb - ra - 1, 1))
+                          for k in range(rb - ra) for w in range(2)])
+                    ts(r("OY", ALL, ot), p(b, 0, n), 4.5, None, ALU.is_lt)
+                    if part == 1:
+                        send("ay%d" % f, {d: [(r("OY", ALL, 4 * f + d), r("ll", 4 * f + me))] for d in others}, False)
+                ts(c("qn", xx, 2 * n), ps, float((1 << 19) + 4096 + 4 * 12288 + 700), None, MIN)
+                tt(ps, ps, c("qn", xx, 2 * n), ALU.subtract)
+                tt(u, ps, u if rnd else xa, MIN)
                 if last:
                     ts(c("yi", xx, 2 * n), u, 511, None, AND)
                     cp(r("OX", ALL, ot), c("yi", xx, 2 * n))
                 else:
-                    xa, da = c("xc", xx, 2 * n), c("dx", xx, 2 * n)
-                    ts(xa, u, -512.0 * (2 - rnd), None, ADD)
+                    ts(xa, u, 512.0 * (rnd + 1), None, ADD)
                     window(f, ra, rb, EST["WIN"][part])
-                    add({"V": tsf(da, xa, -256.0, 0.0, ADD, ALU.max), "S": actf(da, xa, ACT.Relu, -256.0, 1.0)}, [xa], [da])
+                    either(da, xa, -256.0, 0.0, ADD, ALU.max, ACT.Relu, -256.0, 1.0)
                 if last and part == 1:
                     send("ao%d" % f, {d: [(r("OX", ALL, 4 * f + d), r("lx", 4 * f + me))] for d in others}, False)
         yl = lambda d: r("yl", S(2 * d + f, 2 * d + f + 1))
@@ -508,6 +511,7 @@ def hazards(ops):
     seen = {}
     deps = []
     sends = {op["sem"]: i for i, op in enumerate(ops) if op["kind"] == "r"}
+    lands = {op["sem"]: i for i, op in enumerate(ops) if op["kind"] == "b"}
     for i, op in enumerate(ops):
         d = set()
         both = [(x, False) for x in op["R"] if x[0] not in EXT] + [(x, True) for x in op["W"] if x[0] not in EXT]
@@ -529,6 +533,9 @@ def hazards(ops):
             old.append((i, wr, x[2], x[3], x[4], x[5]))
         if op["kind"] == "a":
             d.add(sends[op["sem"]])
+        if op["kind"] == "b":
+            d.add(i - 1)
+            d.update(lands[a] for (a, x), (b, y) in zip(ARRIVE, ARRIVE[1:]) if b == op["sem"])
         if "behind" in op:
             d.add(sends[op["behind"]])
         deps.append(d)
@@ -553,7 +560,7 @@ def place(ops, deps, order, eng):
         op, e = ops[i], eng[i]
         t = max([done[j] + LAT for j in deps[i]] or [0.0])
         if e is None:
-            done[i] = t + 2500.0 if op["at"] < 0 else max(t + 2000.0, op["at"])
+            done[i] = t + op["at"]
             continue
         if i in opens:
             tb, bk = min((-LAT if h < 0 else done[h], b) for b, h in enumerate(holder) if h < 0 or done[h] >= 0.0)

from concourse.bass import DstId, RemoteDMATransfer
from concourse.mybir import AluOpType as ALU, ActivationFunctionType as ACT

RO = 3
BF, F32, I32, U16 = "bfloat16", "float32", "int32", "uint16"
SCRATCH = {}
for _where, _dt, _list in (
    ("dram", I32, (("ocl", 8, 128, 64), ("dcl", 8, 128, 64))),
    ("dram", BF, (("ofx", 8, 128, 128), ("ohv", 8, 128, 256), ("dhv", 8, 128, 256), ("dth", 8, 128, 64), ("xd0", 16, 4, 1024), ("xd1", 16, 4, 1024),
                  ("lx", 8, 128, 128), ("ll", 8, 128, 64))),
    ("sbuf", I32, (("hs", 512), ("hq", 512), ("hr", 512), ("ths", 64), ("clc", 8, 64), ("s1", 512), ("s2", 256), ("cls", 512), ("clw", 1024),
                   ("U", 1024), ("yi", 1024), ("pi", 16))),
    ("sbuf", U16, (("hbo", 512), ("posT", 512), ("clu", 512), ("ob", 128))),
    ("sbuf", F32, (("tio", 4096), ("K", 256), ("M1", 256), ("Km", 128), ("pf", 32), ("row", 192), ("io3", 128))),
    ("sbuf", BF, (("hu", 4, 256), ("hb", 1024), ("thh", 64), ("thl", 64), ("thw", 4096), ("one", 1152), ("big", 1024), ("xw", 8192), ("hh", 2048),
                  ("D", 8192), ("A", 8192), ("A2", 8192), ("Db", 2048), ("vw", 8192), ("vT", 8192), ("bt", 1056), ("lt", 1056), ("lv", 512),
                  ("tch", 512), ("tcl", 512), ("L", 512), ("qn", 1024), ("dx", 1024), ("CST", 384), ("XT", 256), ("xc", 1024),
                  ("OX", 8, 128), ("OY", 8, 64), ("GW", 320), ("ONEW", 144), ("INVW", 288), ("THW", 160), ("SUMW", 144), ("SELW", 144),
                  ("RW", 1152), ("ID", 1536), ("BC", 2048), ("NW", 128), ("WX", 1024), ("CK", 256), ("XI", 64))),
    ("psum", F32, tuple(("pb%d" % _b, 512) for _b in range(8))),
):
    for _x in _list:
        SCRATCH[_x[0]] = (_where, ([] if _where == "dram" else [128]) + list(_x[1:]), _dt)
SEMAPHORES = (["cV", "cS", "cP", "cG", "sent", "acl0", "afx0", "ahv0", "ath", "acl1", "afx1", "ahl", "ahv1", "ao0", "ao1", "ay0", "ay1"]
              + ["d%d" % _k for _k in range(60)])

EST = {"CY": 0.83, "GA": 1.56, "PE": 0.42, "FIX": 20.0, "LAT": 140.0, "TT": 2.0, "DQ": 70.0, "DFIX": 1800.0, "ROW": 20.0, "RATE": 25.0,
       "PF": 15.0, "PS": 8.0, "SX": 25.0, "SG": 15.0, "AS": 0.6, "A0": 3000.0, "A1": 2000.0, "GS": 400.0,
       "RELU": (0, 1, 1, 0), "MS": (0, 0, 0, 1, 0, 1, 0, 1), "WIN0": "PD", "WIN": "PP", "PARTS": ((0, 2), (2, 4)), "LEAD": 0.0}
PLAN = (
    "000q02200a282k2a2c2u2o2K223u2e4e0m0G0I2M1m2G2m2O040K0x0o0u0s2C2q382i2Q082E323U060e3A0D2S2W0O1q1o0Q0U3Q1s3L3g0E2Z0S0k3Z40462U0B345a0M3k0i3O525i0c1y2w5e4U3e123J0z"
    "102g3q1e3N4Q1u26143a3z423i16444a0W0Y181w0g3x1a5c1A3S5556301c5g4u4A4w2I3H1i3c4C1G4y4X5l4s594I4G4M4m4K4O364Y511E4E4T68626O1g1C1W1O6e1I1S3p6a648o666c6g6i5n6m1YhY6o"
    "i0ia6ki46q6s6u6W7q4q1K5r5ti66wic6yie6Aig6Ci26E1M1k5G4k5Ii87Mii5u5p6G6I6L1Q5w4o6N8g5y5A5Dip7i7k8q8i6Q6Y6S8k7s707u7O5O5K5M5W5E6U727m8m74iw8s7U7W7Q767o7Y8u798w7w5Q"
    "7S7y7A8y80ik5Sim1Ujoj4jgja4i5U7e7a7cit82847D7E7G5Y8B7I8C8E7gir87j68GiI888c7Ljc8Jj88f8aiy608L8PjiiKjq9ijQjejkjmiQjsjujx9njy3m8MjAjYiv8Q8SjCjE8UjG9k9o8W9qjIjKjP9s"
    "iAkWiCjNkk8Y949790939uiU98jSk0jU9ckmiE9wiG9K9b9N9e9C9F9y9BkOkY9G9Jk2jWliiMiYkQiOlkl0lqiSkskSk49QiWkokqkU9Wlmloa2l2a4ls9Sl4j0l6k6k89Uku9Ya0aa2skbkcac3Da6l9lakelc"
    "lua8kwkykAlwaekgkiaglylAkCajleakamaolDlI48kFkGaqaslhkKlLkIaukNawazlEj2aKbelGmllNaCccaA9hc4b6c6c8bgbiaMmmaOb8molQbamqmslOmumwlSlUbAaEaGcemylWlYm0mEmHmAmCmMmOmImL"
    "m2m5mamcmemgm6m9bccgaIbkbmaQaSbCbEbImScaboaUcibraXckbK9PbMb2cmcpmYmUnEbGcqbObQcuaYn4csb4n0bSbVbscxbwc0bub0bzbWbYpen6ncnemWn2c3cyn8nad7d8ngninkdbdcdenmdgnodinqcD"
    "dknsmRcAcEcGdydBnucImjcKoCnwnynDnBducMdwdqdscSd0d2cWcZcOcQdmdppgoEpioKoGogcUo8oMoOp6oaocp8paoIoinGoknMoQoedQdEoSnIpcdKdYomoUoXpkpmoonOnQnKpoproqot24oYnSp0nUp2ou"
    "nWdGdMnYpwoyowo0o2o4pso6puoBpzp5dIeydOdUdSdWeUe2e0pEe4e6pBpCpGe8eaeceepIq9qaqdegeipKpMekqefSpOq2pYenpQpUepqgpTq12yq5eWqi4cqkqmpWqsquqoqqqAqwqDfUeYfWf2eqeAeCeseu"
    "fog0f4fqfsfYfwewfuqyqGqIeEfyf0g2eGeIf6qMsUqOqSf8qKeKfaeQqQrW3Fg4qUqWfAg6qYr0g8fCr2fEfcr4d52AgaffeSfGfIr6fgr8gcrafksqdDfnqErcrergfirigefKfMgiglrkrmrqrpfOt2s4rsfR"
    "t4t6sssueMsWrurAs6rCsyrYggsYt03s4grws8s0eOrEgvrygUgSt8tagYgmswsAsCgWrGrIh1q6gotcs2h8sEhahcrKsGtetgsaschkrNgxhesIsKtksetnsMrOsg3WsOsmsQsirSrQgqgsh2sTtiskgyrUsptV"
    "tWtogCgAgItrh4gKu0uagMucgOtuuegQhghihSgEgGtztxtCtKtMugtOtsh6tYhUtAhWhnhqhMhOuitQtShQukuUuWhyupunu3tFtGu4tIu6u8hAhCusuAhEuquvuwuCuEhGuyhohKuKuGuIuMuOhshuhwhIuYuQ"
    "uS")
ARRIVE = (("acl0", 800.0), ("afx0", 2000.0), ("ahv0", 1500.0), ("ath", 2500.0), ("acl1", 800.0), ("afx1", 2000.0), ("ahl", 2500.0), ("ahv1", 1500.0))
EXT = ("fx", "hv", "hl", "cl", "th", "yx", "yl")


def r(name, *idx):
    if name in EXT:
        return (name, idx, 0, 0, 0, 0)
    shape = SCRATCH[name][1]
    full = list(idx) + [slice(None)] * (len(shape) - len(idx))
    lo, hi = [], []
    for s, n in zip(full, shape):
        if isinstance(s, slice):
            rg = range(*s.indices(n))
            lo.append(rg[0]); hi.append(rg[-1])
        else:
            lo.append(s); hi.append(s)
    a = b = 0
    for k in range(1, len(shape)):
        a = a * shape[k] + lo[k]; b = b * shape[k] + hi[k]
    return (name, idx, lo[0], hi[0], a, b)


def c(name, a, n, step=1):
    return r(name, slice(None), slice(a, a + n, step) if step != 1 else slice(a, a + n))


def p(vb, a=0, n=512):
    return ("@", vb, a, a + n)


def build(me):
    ops = []
    nvb = [0]
    lead = [0.0]
    CY, GA, PEC, FIX = EST["CY"], EST["GA"], EST["PE"], EST["FIX"]

    def bank():
        nvb[0] += 1
        return nvb[0]

    def add(alts, R, W, kind="c", lat=0.0, sem=None, at=0.0, prio=0.0, ring=0.0):
        ops.append(dict(alts=alts, R=R, W=W, kind=kind, lat=lat, sem=sem, at=at, prio=prio + lead[0], ring=ring))

    def width(x):
        if x[0] == "@":
            return x[3] - x[2]
        shape = SCRATCH[x[0]][1]
        full = list(x[1]) + [slice(None)] * (len(shape) - len(x[1]))
        n = 1
        for s, m in zip(full[1:], shape[1:]):
            if isinstance(s, slice):
                n *= len(range(*s.indices(m)))
        return n

    def narrow(x):
        return x[0] != "@" and SCRATCH[x[0]][2] in (BF, U16)

    def vcost(n, per):
        return FIX + max(64.0, n * per) * CY

    def vc(out, in_):
        return vcost(width(in_), 0.5 if narrow(out) and narrow(in_) else 1.0)

    def val(ap, s):
        return ap(s) if isinstance(s, tuple) else s

    def tsf(out, in0, s1, s2, op0, op1):
        def f(q, ap):
            if op1 is None:
                return q.tensor_scalar(ap(out), ap(in0), val(ap, s1), None, op0)
            return q.tensor_scalar(ap(out), ap(in0), val(ap, s1), val(ap, s2), op0, op1)
        return (vc(out, in0), f)

    def actf(out, in_, fn, bias, scale):
        return (vcost(width(in_), 1.0) + EST["SX"], lambda q, ap: q.activation(ap(out), ap(in_), fn, bias=bias, scale=val(ap, scale)))

    def ts(out, in0, s1, s2, op0, op1=None):
        add({"V": tsf(out, in0, s1, s2, op0, op1)}, [in0] + [s for s in (s1, s2) if isinstance(s, tuple)], [out])

    def tt(out, in0, in1, op):
        per = 1.0 if "@" in (in0[0], in1[0]) else EST["TT"]
        add({"V": (vcost(width(in0), per), lambda q, ap: q.tensor_tensor(ap(out), ap(in0), ap(in1), op))}, [in0, in1], [out])

    def cp(out, in_):
        add({"V": (vc(out, in_), lambda q, ap: q.tensor_copy(ap(out), ap(in_)))}, [in_], [out])

    def fill(out, v):
        add({"V": (vc(out, out), lambda q, ap: q.memset(ap(out), v))}, [], [out])

    def act(out, in_, fn, bias=0.0, scale=1.0):
        add({"S": actf(out, in_, fn, bias, scale)}, [in_], [out])

    def either(out, in_, s1, s2, op0, op1, fn, bias, scale):
        add({"V": tsf(out, in_, s1, s2, op0, op1), "S": actf(out, in_, fn, bias, scale)}, [in_], [out])

    def move(out, in_):
        add({"V": (vc(out, in_), lambda q, ap: q.tensor_copy(ap(out), ap(in_))), "S": actf(out, in_, ACT.Identity, 0.0, 1.0)}, [in_], [out])

    def times(out, in_, s):
        add({"V": tsf(out, in_, s, None, ALU.mult, None), "S": actf(out, in_, ACT.Identity, 0.0, s)},
            [in_] + ([s] if isinstance(s, tuple) else []), [out])

    def gather(out, win, off):
        d = FIX + width(out) * GA * CY
        add({"V": (d, lambda q, ap: q.tensor_copy(ap(out), ap(win).indirect(ap(off)))),
             "S": (d + EST["SG"], lambda q, ap: q.activation(ap(out), ap(win).indirect(ap(off)), ACT.Copy))}, [win, off], [out])

    def gather_op(out, win, off, in1, op):
        d = FIX + width(out) * GA * CY
        add({"V": (d, lambda q, ap: q.tensor_tensor(ap(out), ap(win).indirect(ap(off)), ap(in1), op))}, [win, off, in1], [out])

    def mm(lst):
        def f(q, ap):
            last = None
            for (o, l, x, a, b) in lst:
                last = q.matmul(ap(o), ap(l), ap(x), a, b)
            return last
        R = []
        for (o, l, x, a, b) in lst:
            R += [t for t in (l, x) if t not in R]
        d = EST["PF"] + sum(max(64, width(x)) * PEC + EST["PS"] * (l[0] in ("A", "A2", "D", "bt", "lt")) for (o, l, x, a, b) in lst)
        add({"P": (d, f)}, R, [lst[0][0]])

    def iota(out, pat, base, mult, behind=None):
        if SCRATCH[out[0]][2] == I32:
            f = lambda q, ap: q.iota(ap(out), pat, base, mult)
        else:
            f = lambda q, ap: q.iota(ap(out), pat, base, mult, allow_small_or_imprecise_dtypes=True)
        add({"G": (140.0 + 2 * width(out) * CY, f)}, [], [out])
        if behind:
            ops[-1]["behind"] = behind

    def select(out, src, pat, base, behind=None):
        n = width(out)
        add({"G": (180.0 + 2 * n * CY, lambda q, ap: q.affine_select(ap(out), ap(c(src, 0, n)), pat, ALU.is_equal, 0.0, base, -1))}, [c(src, 0, n)], [out])
        if behind:
            ops[-1]["behind"] = behind

    def dma(pairs, rows, size, engs="YS", prio=0.0):
        f = lambda q, ap: [q.dma_start(ap(o), ap(i)) for (o, i) in pairs]
        add({e: (EST["DQ"] * len(pairs), f) for e in engs}, [i for (o, i) in pairs], [o for (o, i) in pairs], kind="d", lat=EST["DFIX"], prio=prio,
            ring=rows / 16.0 * (EST["ROW"] + size / EST["RATE"]))

    sent = []

    def send(sem, pieces, in_line=True):
        add({"G": (EST["GS"], pieces)}, [s for d in pieces for (s, t) in pieces[d]], [], kind="r", sem=sem, prio=1e6)
        if sent and in_line:
            ops[-1]["behind"] = sent[-1]
        sent.append(sem)

    def arrive(sem, W):
        add({}, [], [], kind="a", sem=sem, at=EST["A0"] if sem == ARRIVE[0][0] else EST["A1"])
        add({}, [], W, kind="b", sem=sem, at=dict(ARRIVE).get(sem, 500.0) * EST["AS"])

    others = [d for d in range(4) if d != me]
    S = slice
    ALL = slice(None)
    SHR, AND, MUL, ADD, EQ, MIN = ALU.arith_shift_right, ALU.bitwise_and, ALU.mult, ALU.add, ALU.is_equal, ALU.min
    rows = lambda d, f: S(32 * d + 16 * f, 32 * d + 16 * f + 16)

    def loads(f, pr):
        box = lambda t, d: r("o" + t, 4 * f + d) if d != me else r("d" + t, 4 * f + d)
        dma([(box("cl", d), r("cl", rows(d, f))) for d in others], 48, 2048, engs="Y", prio=pr + 9e5)
        dma([(r("ofx", 4 * f + d), r("fx", rows(d, f))) for d in others], 48, 2048, engs="S", prio=pr + 9e5)
        hv = lambda d, m: (box("hv", d)[0], (4 * f + d, S(64 * m, 64 * m + 64))) + box("hv", d)[2:]
        dma([(hv(d, m), r("hv", rows(d, f), S(1024 * m, 1024 * m + 1024))) for d in others for m in range(2)], 96, 2048, engs="Y", prio=pr + 8e5)
        dma([(box("cl", me), r("cl", rows(me, f)))] + [(hv(me, m), r("hv", rows(me, f), S(1024 * m, 1024 * m + 1024))) for m in range(2)],
            48, 2048, engs="Y", prio=pr + 7e5)
        dma([(c("xc", 512 * f + 128 * me, 128), r("fx", rows(me, f)))], 128, 256, engs="S", prio=pr + 7e5)

    def sends(f):
        send("acl%d" % f, {d: [(r("ocl", 4 * f + d), r("dcl", 4 * f + me))] for d in others})
        send("afx%d" % f, {d: [(r("ofx", 4 * f + d), c("xc", 512 * f + 128 * me, 128))] for d in others})

    def sendhv(f):
        send("ahv%d" % f, {d: [(r("ohv", 4 * f + d), r("dhv", 4 * f + me))] for d in others})

    loads(0, 9e6)
    dma([(r("ths"), r("th"))], 128, 256, engs="S", prio=9.75e6)
    loads(1, 7e6)
    for half in range(2):
        dma([(r("hs", S(32 * q, 32 * q + 32), S(128 * d, 128 * d + 128)), r("hl", S(32 * d, 32 * d + 32), S(128 * q, 128 * q + 128)))
             for q in (2 * half, 2 * half + 1) for d in range(4)], 256, 512, engs="YS"[half], prio=8e6)
    lead[0] = 1e6
    fill(r("one"), 1.0)
    times(r("big"), c("one", 0, 1024), 98304.0)
    times(r("lt"), c("one", 0, 1056), 0.0)
    times(r("bt"), c("one", 0, 1056), 0.0)
    for k in range(4):
        move(c("thw", 1024 * k, 1024), c("one", 0, 1024))
    sends(0)
    sendhv(0)
    iota(r("clw"), [[0, 1024]], 0, 0, "ahv0")
    cp(r("thh"), r("ths"))
    tt(r("thl"), r("ths"), r("thh"), ALU.subtract)
    send("ath", {d: [(r("thh"), r("dth", me)), (r("thl"), r("dth", 4 + me))] for d in others})
    dma([(r("dth", me), r("thh")), (r("dth", 4 + me), r("thl"))], 256, 128, engs="Y")
    sends(1)
    ts(r("hq"), r("hs"), 15, None, AND)
    ts(r("hr"), r("hs"), 4, None, SHR)
    cp(r("hu", ALL, ALL, S(0, 128)), r("hq"))
    cp(r("hu", ALL, ALL, S(128, 256)), r("hr"))
    send("ahl", {d: [(r("hu", ALL, d), c("hb", 256 * me, 256))] for d in others})
    sendhv(1)
    cp(c("hb", 256 * me, 256), r("hu", ALL, me))
    lead[0] = 0.0
    arrive("ath", [r("dth", k + d) for d in others for k in (0, 4)])
    arrive("ahl", [c("hb", 256 * d, 256) for d in others])
    for f in range(2):
        arrive("acl%d" % f, [r("dcl", 4 * f + d) for d in others])
        arrive("afx%d" % f, [c("xc", 512 * f + 128 * d, 128) for d in others])
        arrive("ahv%d" % f, [r("dhv", 4 * f + d) for d in others])
        four = S(4 * f, 4 * f + 4)
        dma([(r("clc", S(64 * m, 64 * m + 64), four), r("dcl", four, S(m, 128, 2))) for m in range(2)], 512, 256, engs="S", prio=3e6 - 2e6 * f)
        dma([(r("hh", S(64 * m, 64 * m + 64), S(1024 * f, 1024 * f + 1024)), r("dhv", four, S(64 * m, 64 * m + 64))) for m in range(2)],
            128, 2048, engs="Y", prio=2.5e6 - 2e6 * f)
        dma([(r("thw", S(16 * gg + 2 * f, 16 * gg + 2 * f + 2)), r("dth", ALL, rows(me, f))) for gg in range(8)], 64, 2048, engs="Y", prio=2e6 - 1e6 * f)
        dma([(r("clw", S(64 * m + 4 * f + cc, 64 * m + 64, 16)), r("dcl", four, S(2 * cc + m, 128, 8))) for m in range(2) for cc in range(4)],
            512, 256, engs="Y", prio=1.5e6 - 1e6 * f)

    lead[0] = 1e6
    iota(c("pi", 0, 1), [[0, 1]], 0, 1)
    iota(r("row"), [[1, 192]], 0, 0)
    iota(r("io3"), [[0, 8], [1, 16]], 0, 0)
    iota(r("CK"), [[1, 4], [0, 64]], 0, 0)
    pi = lambda k: c("pi", k, 1)
    pf = lambda k: c("pf", k, 1)
    ts(pi(1), pi(0), 4, None, SHR)
    ts(pi(2), pi(0), 15, None, AND)
    ts(pi(3), pi(0), 4, 1, SHR, AND)
    ts(pi(4), pi(0), 5, None, SHR)
    ts(pi(5), pi(0), 4, 3, SHR, AND)
    ts(pi(6), pi(0), 6, None, SHR)
    ts(pi(7), pi(0), 2, 3, SHR, AND)
    ts(pi(8), pi(0), 1, 7, SHR, AND)
    cp(pf(0), pi(0))
    ts(pf(1), pi(1), 16.0, 15.0, MUL, ADD)
    cp(pf(2), pi(2))
    ts(pf(3), pi(2), 8.0, 7.0, MUL, ADD)
    ts(pf(4), pi(6), 16.0, 15.0, MUL, ADD)
    ts(pf(5), pi(5), 32.0, pf(4), MUL, ADD)
    ts(pf(6), pi(2), 0.0, None, EQ)
    ts(pf(7), pi(2), 64.0, None, ADD)
    ts(pf(8), pi(4), 16.0, pf(7), MUL, ADD)
    ts(pf(9), pi(1), 8.0, 7.0, MUL, ADD)
    ts(pf(10), pi(2), 64.0, None, MUL)
    for f in range(2):
        ts(pf(12 + f), pi(3), float(f), None, EQ)
        ts(pf(18 + f), pi(7), float(f), 1024.0, EQ, MUL)
        ts(pf(20 + f), pi(8), float(f), None, EQ)
    for f in range(2):
        ts(c("RW", 576 * f + 192, 192), r("row"), pf(8), pf(12 + f), EQ, MUL)
        times(c("RW", 576 * f, 192), c("RW", 576 * f + 192, 192), 64.0)
        times(c("RW", 576 * f + 384, 192), c("RW", 576 * f + 192, 192), 16.0)
    ts(r("ONEW"), c("row", 0, 144), pf(1), None, EQ)
    for k, wgt in enumerate((4.0, 8.0, -4.0, 1.0)):
        ts(c("GW", 80 * k, 72), c("row", 0, 72), pf(9), wgt, EQ, MUL)
    for f in range(2):
        times(c("INVW", 144 * f, 144), r("ONEW"), pf(18 + f))
        times(c("THW", 80 * f, 72), c("GW", 240, 72), pf(20 + f))
    ts(r("SUMW"), c("row", 0, 144), pf(3), -0.125, EQ, MUL)
    ts(r("SELW"), c("row", 0, 144), pf(5), pf(6), EQ, MUL)
    ts(c("ID", 0, 128), c("row", 0, 128), pf(0), None, EQ)
    wts = (1.0, -1.0, -float(1 << 20), 8192.0, 32768.0, 8.0, 1024.0, 2048.0, 3072.0, 256.0, -8192.0, 2.0)
    for k in range(1, 12):
        times(c("ID", 128 * k, 128), c("ID", 0, 128), wts[k])
    IDN, NEG, PEN, BST, LVI, ID8, K1, K2, K3, KD, NBS, ID2 = [c("ID", 128 * k, 128) for k in range(12)]
    cp(r("XI"), c("row", 0, 64))
    select(r("WX"), "one", [[1, 8], [0, 8], [8, 16]], 0)
    ts(r("NW"), r("io3"), pf(2), None, EQ)
    times(r("CST"), c("one", 0, 384), 0.0)
    fill(r("CST", S(0, 1)), float((1 << 19) + 4096))
    fill(r("CST", S(32, 33)), -0.4375)
    for k in range(RO):
        fill(r("CST", S(64, 65), S(128 * k, 128 * k + 128)), -512.0 * (k + 1))
    for k in range(2):
        ts(pf(27 + k), pi(0), 2.0, float(k), MUL, ADD)
        ts(c("XT", 128 * k, 128), r("io3"), pf(27 + k), 1.0 / 32.0, EQ, MUL)
    lead[0] = 0.0
    for k in range(2):
        select(c("BC", 1024 * k, 1024), "big", [[1, 8], [16, 8], [0, 16]], 8 * k, "ahv1")
    for k in range(4):
        iota(c("tio", 1024 * k, 1024), [[1, 1024]], 1024 * k, 0, "ahv1")
    sl = lambda name, top, k, n=128: c(name, top - k, n)

    def window(f, a, b, how):
        if how == "D":
            xd = "xd%d" % f
            dma([(r(xd, ALL, rr), c("xc", 512 * f + 128 * rr, 128)) for rr in range(a, b)], 128 * (b - a), 256, engs="Y")
            dma([(r("xw", S(16 * l, 16 * l + 16), S(4096 * f + 1024 * a, 4096 * f + 1024 * b)), r(xd, ALL, S(a, b))) for l in range(8)],
                128, 2048 * (b - a), engs="Y")
            return
        for rr in range(a, b):
            for up in range(2):
                bk = bank()
                mm([(p(bk, 128 * u, 128), c("WX", 128 * (4 * up + u), 128), c("xc", 512 * f + 128 * rr, 128), True, True) for u in range(4)])
                move(c("xw", 4096 * f + 1024 * rr + 512 * up, 512), p(bk))

    def stream(f):
        F = 4096 * f
        X = 512 * f
        H = 256 * f
        lv = lambda cc: c("lv", H + 64 * cc, 64)
        odd = lambda t, cc: c(t, 528 * f + 128 * cc + 1, 128, 2)
        pad = lambda t, cc, par: c(t, 528 * f + 128 * cc + 1 - par, 128)
        half = lambda m, par: c("ID", m[4] + 64 * par, 64)
        clu = lambda cc: c("clu", H + 64 * cc, 64)

        def base(b, rr, ks, closes):
            return [(p(b, 64 * rr, 64), c("RW", 192 * (3 * f + ks[t]) + 64 - 64 * m, 128), c("hb", 256 * rr + 128 * t + 64 * m, 64),
                     (t, m) == (0, 0), closes and (t, m) == (1, 1)) for t in range(2) for m in range(2)]
        s1, s2, cls = [lambda k, n=1, t=t, a=a: c(t, a + 64 * k, 64 * n) for (t, a) in (("s1", H), ("s2", 128 * f), ("cls", H))]
        lo, hi = r("clc", ALL, S(4 * f, 4 * f + 2)), r("clc", ALL, S(4 * f + 2, 4 * f + 4))
        tt(s1(0, 2), lo, hi, MIN)
        tt(cls(0), s1(0), s1(1), MIN)
        cp(clu(0), cls(0))
        tt(s1(2, 2), lo, hi, ALU.max)
        tt(cls(3), s1(2), s1(3), ALU.max)
        cp(clu(3), cls(3))
        tt(s2(0), s1(0), s1(1), ALU.max)
        tt(s2(1), s1(2), s1(3), MIN)
        tt(cls(1), s2(0), s2(1), MIN)
        tt(cls(2), s2(0), s2(1), ALU.max)
        cp(c("clu", H + 64, 128), cls(1, 2))
        window(f, 0, 4, EST["WIN0"][f])
        for cc in range(4):
            gather(c("A2", F + 1024 * cc, 1024), r("thw"), clu(cc))
        b = bank()
        for cc in range(4):
            mm([(p(b, 64 * cc, 64), c("A2", F + 1024 * cc + 128 * k, 128), sl("THW", 80 * f + 7, k, 64), k == 0, k == 7) for k in range(8)])
        move(c("tch", H, 256), p(b, 0, 256))
        tt(c("tcl", H, 256), p(b, 0, 256), c("tch", H, 256), ALU.subtract)
        b = bank()
        mm([x for rr in range(4) for x in base(b, rr, (0, 1), True)])
        cp(c("hbo", H, 256), p(b, 0, 256))
        b = bank()
        for rr in range(4):
            gather_op(c("vT", F + 1024 * rr, 1024), r("clw"), c("hbo", H + 64 * rr, 64), c("tio", 1024 * rr, 1024), ALU.is_lt)
            mm(base(b, rr, (1, 2), False) + [(p(b, 64 * rr, 64), sl("INVW", 144 * f + 15, s), c("vT", F + 1024 * rr + s, 1024 - s, 16), False, s == 15) for s in range(16)])
        cp(c("posT", H, 256), p(b, 0, 256))

        for rnd in range(RO):
            last = rnd == RO - 1
            kb = bank()
            lst = [(p(kb, 0, 256), IDN, r("CK"), True, False)]
            if rnd:
                lst += [(p(kb, 64 * cc, 64), PEN, odd("lt", cc), False, False) for cc in range(4)]
            order = (0, 3, 1, 2)
            for cc in order:
                a = F + 1024 * cc
                gather_op(c("D", a, 1024), c("xw", F, 4096), clu(cc), c("hh", 1024 * f, 1024), ALU.subtract)
                ops[-1]["tag"] = ("D", f, rnd, cc)
                pc = p(kb, 64 * cc, 64)
                if EST["RELU"][cc]:
                    ts(c("A", a, 1024), c("D", a, 1024), 0.0, None, ALU.max)
                    mm(lst + [(pc, c("D", a + 128 * k, 128), sl("GW", 167, k, 64), False, False) for k in range(8)])
                    lst = []
                else:
                    act(c("A", a, 1024), c("D", a, 1024), ACT.Abs)
                top = 87 if EST["RELU"][cc] else 7
                mm(lst + [(pc, c("A", a + 128 * k, 128), sl("GW", top, k, 64), False, cc == order[-1] and k == 7) for k in range(8)])
                lst = []
            move(c("K", 128 * f, 128), p(kb, 128, 128))
            tt(c("M1", 128 * f, 128), p(kb, 0, 128), c("K", 128 * f, 128), MIN)
            km = c("Km", 64 * f, 64)
            tt(km, c("M1", 128 * f, 64), c("M1", 128 * f + 64, 64), MIN)
            for cc in (1, 2, 3):
                tt(odd("bt", cc), p(kb, 64 * cc, 64), km, EQ)
            b = bank()
            mm([(p(b, 0, 64), IDN, r("XI"), True, False)]
               + [(p(b, 0, 64), pad("bt", k, par), half((K1, K2, K3)[k - 1], par), False, (k, par) == (3, 1)) for k in (1, 2, 3) for par in range(2)])
            ts(c("ob", 64 * f, 64), p(b, 0, 64), pf(10), 4095.0, ADD, MIN)
            for hf in range(2):
                gather(c("Db", 1024 * f + 512 * hf, 512), c("D", F, 4096), c("ob", 64 * f + 32 * hf, 32))
            for cc in range(4):
                pc = p(bank(), 0, 64)
                lst = [(pc, NEG, c(t, H + 64 * cc, 64), t == "tch", False) for t in ("tch", "tcl")]
                if cc:
                    lst += [(pc, BST, odd("bt", cc), False, False)]
                else:
                    lst += [(pc, BST, c("one", 0, 64), False, False)]
                    lst += [(pc, NBS, odd("bt", z), False, False) for z in (1, 2, 3)]
                if rnd:
                    lst.append((pc, LVI, odd("lt", cc), False, False))
                for hf in range(2):
                    b = bank()
                    a = F + 1024 * cc + 512 * hf
                    mm([(p(b), IDN, c("D", a, 512), True, False)])
                    mm([(p(b, 64 * s, 64), NEG, c("Db", 1024 * f + 8 * hf + s, 1024 - 8 * hf - s, 16), False, s == 7) for s in range(8)])
                    act(c("A2", a, 512), p(b), ACT.Abs)
                    mm(lst + [(pc, c("A2", a + 128 * k, 128), sl("GW", 247, 4 * hf + k, 64), False, (hf, k) == (1, 3)) for k in range(4)])
                    lst = []
                act(odd("lt", cc), pc, ACT.Sign, bias=0.5 - (32768.0 if rnd else 0.0))
                pc = p(bank(), 0, 64)
                mm([(pc, pad("lt", cc, par), half(IDN, par), par == 0, par == 1) for par in range(2)])
                move(lv(cc), pc)
                for hf in range(2):
                    b = bank()
                    a = F + 1024 * cc + 512 * hf
                    bc = [(p(b, 64 * s, 64), c("BC", 128 * (8 * hf + s), 128), lv(cc)) for s in range(8)]
                    if EST["MS"][2 * cc + hf]:
                        mm([(p(b), ID2, c("D", a, 512), True, False)] + [x + (False, s == 7) for s, x in enumerate(bc)])
                        either(c("vw", a, 512), p(b), 0.5, -49152.0, MUL, ADD, ACT.Identity, -49152.0, 0.5)
                    else:
                        mm([x + (True, True) for x in bc])
                        tt(c("vw", a, 512), p(b), c("D", a, 512), MIN)
                    ops[-1]["tag"] = ("M", f, rnd, 2 * cc + hf)
            parts = EST["PARTS"]
            if last:
                pair = (1, 2, 0, 0)[me]
                parts = [(pair, pair + 2)] + [(d, d + 1) for d in others if d not in (pair, pair + 1)] + [(me, me + 1)]
            for part, (ra, rb) in enumerate(parts):
                sm, se = bank(), (bank() if last else None)
                n, hh, xx = 64 * (rb - ra), H + 64 * ra, X + 128 * ra
                ps = p(sm, 0, 2 * n)
                xa, da, u = c("xc", xx, 2 * n), c("dx", xx, 2 * n), c("U", xx, 2 * n)
                for k, rr in enumerate(range(ra, rb)):
                    w = 512 if last else 1024
                    for a in range(1024 * rr, 1024 * rr + 1024, w):
                        gather(c("vT", F + a, w), c("vw", F, 4096), c("posT", H + a // 16, w // 16))
                    if last:
                        mm([(p(se, 64 * k, 64), sl("SELW", 15, a), c("vT", F + 1024 * rr + 64 * a, 64), a == 0, a == 15) for a in range(16)])
                    lst = []
                    if k == 0:
                        lst = [(ps, IDN, xa, True, False), (ps, c("CST", 128 * rnd, 128), c("one", 0, 2 * n), False, False)]
                        if rnd:
                            lst.append((ps, KD, da, False, False))
                    mm(lst + [(p(sm, 128 * k, 128), sl("SUMW", 7, u8), c("vT", F + 1024 * rr + 128 * u8, 128), False, (rr, u8) == (rb - 1, 7)) for u8 in range(8)])
                ot = S(4 * f + ra, 4 * f + rb)
                if last:
                    Lt = c("L", hh, n)
                    either(Lt, p(se, 0, n), -16384.0, None, ALU.is_lt, None, ACT.Relu, -1.0, -1.0 / 49152.0)
                    b = bank()
                    mm([(p(b, 0, n), r("NW"), Lt, True, False), (p(b, 0, n), ID8, Lt, False, False)]
                       + [(p(b, 64 * k, 64), c("XT", 128 * w, 128), c("dx", xx + 128 * k + 64 * w, 64), False, (k, w) == (rb - ra - 1, 1))
                          for k in range(rb - ra) for w in range(2)])
                    ts(r("OY", ALL, ot), p(b, 0, n), 4.5, None, ALU.is_lt)
                    if part == 1:
                        send("ay%d" % f, {d: [(r("OY", ALL, 4 * f + d), r("ll", 4 * f + me))] for d in others}, False)
                ts(c("qn", xx, 2 * n), ps, float((1 << 19) + 4096 + 4 * 12288 + 700), None, MIN)
                tt(ps, ps, c("qn", xx, 2 * n), ALU.subtract)
                tt(u, ps, u if rnd else xa, MIN)
                if last:
                    ts(c("yi", xx, 2 * n), u, 511, None, AND)
                    cp(r("OX", ALL, ot), c("yi", xx, 2 * n))
                else:
                    ts(xa, u, 512.0 * (rnd + 1), None, ADD)
                    window(f, ra, rb, EST["WIN"][part])
                    either(da, xa, -256.0, 0.0, ADD, ALU.max, ACT.Relu, -256.0, 1.0)
                if last and part == 1:
                    send("ao%d" % f, {d: [(r("OX", ALL, 4 * f + d), r("lx", 4 * f + me))] for d in others}, False)
        yl = lambda d: r("yl", S(2 * d + f, 2 * d + f + 1))
        dma([(yl(me), r("OY", ALL, 4 * f + me))], 128, 128, engs="Y")
        dma([(r("yx", rows(me, f)), r("OX", ALL, 4 * f + me))], 128, 256, engs="S")
        arrive("ay%d" % f, [r("ll", 4 * f + d) for d in others])
        dma([(yl(d), r("ll", 4 * f + d)) for d in others], 48, 1024, engs="Y")
        arrive("ao%d" % f, [r("lx", 4 * f + d) for d in others])
        dma([(r("yx", rows(d, f)), r("lx", 4 * f + d)) for d in others], 48, 2048, engs="Y")

    for f in range(2):
        lead[0] = EST["LEAD"] * (1 - f)
        stream(f)
    return ops


def hazards(ops):
    seen = {}
    deps = []
    sends = {op["sem"]: i for i, op in enumerate(ops) if op["kind"] == "r"}
    lands = {op["sem"]: i for i, op in enumerate(ops) if op["kind"] == "b"}
    for i, op in enumerate(ops):
        d = set()
        both = [(x, False) for x in op["R"] if x[0] not in EXT] + [(x, True) for x in op["W"] if x[0] not in EXT]
        for (x, wr) in both:
            if x[0] == "@":
                if seen.get(x[1], i) != i:
                    d.add(seen[x[1]])
                seen[x[1]] = i
                continue
            for (j, w2, a, b, e, f) in seen.get(x[0], ()):
                if (wr or w2) and a <= x[3] and x[2] <= b and e <= x[5] and x[4] <= f:
                    d.add(j)
        for (x, wr) in both:
            if x[0] == "@":
                continue
            old = seen.setdefault(x[0], [])
            if wr and len(SCRATCH[x[0]][1]) == 2 and all(isinstance(s, slice) and s.step in (None, 1) for s in x[1]):
                old[:] = [t for t in old if not (x[2] <= t[2] and t[3] <= x[3] and x[4] <= t[4] and t[5] <= x[5])]
            old.append((i, wr, x[2], x[3], x[4], x[5]))
        if op["kind"] == "a":
            d.add(sends[op["sem"]])
        if op["kind"] == "b":
            d.add(i - 1)
            d.update(lands[a] for (a, x), (b, y) in zip(ARRIVE, ARRIVE[1:]) if b == op["sem"])
        if "behind" in op:
            d.add(sends[op["behind"]])
        deps.append(d)
    return deps


def place(ops, deps, order, eng):
    LAT = EST["LAT"]
    first, lastuse = {}, {}
    for i, op in enumerate(ops):
        for x in op["R"] + op["W"]:
            if x[0] == "@":
                first.setdefault(x[1], i)
                lastuse[x[1]] = i
    opens = {i: vb for vb, i in first.items()}
    done = [-1.0] * len(ops)
    holder = [-1] * 8
    free = {e: 0.0 for e in "VSPGY"}
    rfree = 0.0
    bank_of, after = {}, {}
    for i in order:
        op, e = ops[i], eng[i]
        t = max([done[j] + LAT for j in deps[i]] or [0.0])
        if e is None:
            done[i] = t + op["at"]
            continue
        if i in opens:
            tb, bk = min((-LAT if h < 0 else done[h], b) for b, h in enumerate(holder) if h < 0 or done[h] >= 0.0)
            t = max(t, tb + LAT)
            if holder[bk] >= 0:
                after[i] = holder[bk]
            holder[bk] = lastuse[opens[i]]
            bank_of[opens[i]] = bk
        t = free[e] = max(t, free[e]) + op["alts"][e][0]
        if op["ring"]:
            rfree = max(rfree, t) + op["ring"]
            t = rfree + op["lat"]
        done[i] = t
    return done, bank_of, after


DIGITS = "0123456789abcdefghijklmnopqrstuvwxyzABCDEFGHIJKLMNOPQRSTUVWXYZ"
MADE = {}


def planned(plan):
    if not MADE:
        alls = [build(d) for d in range(4)]
        hz = [hazards(ops) for ops in alls]
        deps = [set().union(*[h[i] for h in hz]) for i in range(len(alls[0]))]
        v = [DIGITS.index(plan[k]) * 62 + DIGITS.index(plan[k + 1]) for k in range(0, len(plan), 2)]
        order = [x >> 1 for x in v]
        if sorted(order) != list(range(len(deps))):
            raise ValueError("the plan does not fit the calls")
        eng = [None] * len(deps)
        seen = set()
        for x in v:
            alts = sorted(alls[0][x >> 1]["alts"])
            eng[x >> 1] = None if not alts else alts[0] if x & 1 else alts[-1]
            if not deps[x >> 1] <= seen:
                raise ValueError("the plan breaks a hazard")
            seen.add(x >> 1)
        done, bank_of, after = place(alls[0], deps, order, eng)
        for i, h in after.items():
            for x in hz:
                x[i].add(h)
        MADE.update(ops=alls, deps=hz, order=order, eng=eng, done=done, bank=bank_of)
    return MADE


def split_engines(core, cores, topo):
    peers = [x for x in cores if x != core]
    for x in peers:
        if not topo.may_write(core, x):
            raise ValueError("no way to a rank")
    allowed = {x: topo.engines(core, x) for x in peers}
    few = min(len(v) for v in allowed.values())
    tight = [x for x in peers if len(allowed[x]) == few]
    k = 1
    while 2 * k <= few // len(tight):
        k *= 2
    out, used = {}, []
    for x in tight + [y for y in peers if y not in tight]:
        left = [e for e in allowed[x] if e not in used]
        out[x] = left[:k] if x in tight else left[::2][:k]
        used += out[x]
    return out


def rank_program(g, core, T, topo):
    me = T.rank_of(core)
    if me is None:
        return
    cores = list(T.cores)
    plan = planned(PLAN)
    ops, deps, order, eng, done, bank_of = plan["ops"][me], plan["deps"][me], plan["order"], plan["eng"], plan["done"], plan["bank"]
    queue = {"V": g.vector, "S": g.scalar, "P": g.tensor, "G": g, "Y": g.sync}
    mine = split_engines(core, cores, topo)
    inbound = sum(len(split_engines(x, cores, topo)[core]) for x in cores if x != core)

    def ap(x):
        if x[0] == "@":
            return T["pb%d" % bank_of[x[1]]][:, x[2]:x[3]]
        return T[x[0]][x[1]] if x[1] else T[x[0]][:]

    count = {}
    mark = {}
    clock = {}
    know = {e: {} for e in queue}
    ndma = [0]
    for i in order:
        op, e = ops[i], eng[i]
        if e is None:
            count[op["sem"]] = inbound
            mark[i] = (op["sem"], inbound)
            clock[i] = {op["sem"]: inbound}
            continue
        q, kn = queue[e], know[e]
        want = {}
        for j in deps[i]:
            if ops[j]["kind"] == "r":
                if "behind" in op:
                    continue
                raise ValueError("a source of a remote write is written again")
            if e == "P" and eng[j] == "P":
                continue
            s, v = mark[j]
            if want.get(s, (0, 0))[0] < v:
                want[s] = (v, j)
        for s in sorted(want, key=lambda s: (-done[want[s][1]], s)):
            v, j = want[s]
            if kn.get(s, 0) < v:
                q.wait_ge(T.sem[s], v)
                for s2, v2 in clock[j].items():
                    if kn.get(s2, 0) < v2:
                        kn[s2] = v2
        f = op["alts"][e][1]
        if op["kind"] == "c":
            s = "c" + e
            count[s] = count.get(s, 0) + 1
            f(q, ap).then_inc(T.sem[s], 1)
        elif op["kind"] == "d":
            s = "d%d" % ndma[0]
            ndma[0] += 1
            count[s] = 0
            for ins in f(q, ap):
                ins.then_inc(T.sem[s], 16)
                count[s] += 16
        else:
            s = "sent"
            trs = []
            for d in sorted(f):
                rid, pid = topo.addr(cores[d])[:2]
                es = mine[cores[d]]
                k = len(es) // len(f[d])
                for n, (src, dst) in enumerate(f[d]):
                    mask = sum(1 << x for x in es[n * k:n * k + k])
                    trs.append(RemoteDMATransfer(dst_ids=[DstId(rid=rid, pnc=pid)], dma_engine_mask=mask, remote_sem=T.sem[op["sem"]], src=ap(src), dst=ap(dst)))
                    count[s] = count.get(s, 0) + k
            q.remote_dma_fused(trs, local_sem=T.sem[s])
        mark[i] = (s, count[s])
        clock[i] = dict(kn)
        clock[i][s] = count[s]
    for s in sorted(count):
        g.wait_ge(T.sem[s], count[s])
